import numpy as np, ml_dtypes
CORES = [113,118,241,246]
N = 4
BF = ml_dtypes.bfloat16
V, M, S, CAP, P, RO, STEP, LN = 1024, 3584, 256, 64, 10, 3, 310, 2
W1 = 13 * np.arange(16) + 5; W2 = 255 - 14 * np.arange(16); A = N * CAP
def mix(d):
    u = np.add.reduce(W1[:, None] * d, axis=2) & 4095; w = np.add.reduce(W2[:, None] * d, axis=2) & 4095
    return u, (u * w) >> 5
def kid(d, c, hm, t):
    R, n = d.shape[0], d.shape[3]
    hv = np.take_along_axis(hm, d.reshape(R, 8, 1, 16 * n), 3).reshape(R, 8, 16, 16, n)
    e = np.add.reduce(np.minimum(hv, np.abs(c)[:, :, :, None]), axis=2)
    k = np.argmax(e, axis=2); u, h = mix(d); v = (h + 37 * np.max(e, axis=2) + t) & 4095
    void = np.any(d == v[:, :, None], axis=2) | (v >= M)
    new = np.where(np.arange(16)[:, None] == k[:, :, None], v[:, :, None], d)
    q = np.add.reduce((new < v[:, :, None]).astype(np.int64), axis=2)
    return ~void, np.sort(new, axis=2), np.where((((q - k) & 1) == 1)[:, :, None], -(c >> 2), c >> 2)
def spawn(D, C, hm, t):
    start = STEP * (t + 1); a = np.roll(np.any(C != 0, axis=2), -start, axis=2)
    o = np.argsort(~a, axis=2, kind="stable")[:, :, :S]; on = np.take_along_axis(a, o, 2); pl = (o + start) & (V - 1)
    good, ch, c = kid(np.take_along_axis(D, pl[:, :, None], 3), np.take_along_axis(C, pl[:, :, None], 3), hm, t)
    return pl, on, on & good, ch, c
def recs(rng, shape):
    return np.sort(rng.integers(0, M - 15, shape), axis=-2) + np.arange(16)[:, None]
def base(rng, share=None):
    lim = rng.choice(np.array([1, 3, 20, 127]), (N, 8, 1, V), p=[0.15, 0.15, 0.2, 0.5]); C = rng.integers(-lim, lim + 1, (N, 8, 16, V))
    if share is None: share = rng.choice(np.array([0.4, 0.55, 0.75, 0.92]), (N, 8, 1, 1))
    C = C * (rng.random((N, 8, 1, V)) < share)
    return recs(rng, (N, 8, 16, V)), C, rng.integers(0, 128, (N, 8, 16, M))
def plant(rng, D, C, hm, part, twin=False, t=0, own=False):
    live = np.any(C != 0, axis=2); pl, on, good, ch, c = spawn(D, C, hm, t); u, h = mix(ch)
    busy = np.zeros((N, 8, V), bool); np.put_along_axis(busy, pl, on, 2)
    q, g, s = np.nonzero(good & (rng.random(good.shape) < part)); r = h[q, g, s] & (N - 1)
    p = ((h[q, g, s] >> LN) + rng.integers(0, P, q.size) * (2 * u[q, g, s] + 1)) & (V - 1)
    one = np.unique((r * 8 + g) * V + p, return_index=True)[1]
    if not own: one = one[~busy[r[one], g[one], p[one]]]
    q, g, s, r, p = q[one], g[one], s[one], r[one], p[one]
    rec = ch[q, g, :, s]; w = c[q, g, :, s]; lv = live[r, g, p][:, None]; bs = busy[r, g, p][:, None]; n = one.size
    if twin:
        nxt = np.concatenate([rec[:, 1:], np.full((n, 1), M)], axis=1); way = rng.random(n)
        fit = (rec[:, :14] + 1 < rec[:, 1:15] - 2) & (rec[:, 2:] + 1 < nxt[:, 2:]); i = np.argmax(fit * (0.01 + rng.random(fit.shape)), axis=1)
        z = np.nonzero(np.any(fit, axis=1) & (way < 0.4))[0]
        rec[z, i[z]] += 1; rec[z, i[z] + 1] -= 2; rec[z, i[z] + 2] += 1
        i = np.where(rng.random(n) < 0.3, 15, rng.integers(0, 16, n))
        z = np.nonzero((way > 0.6) & (rec[np.arange(n), i] + 1 < nxt[np.arange(n), i]))[0]
        rec[z, i[z]] += 1
    D[r, g, :, p] = rec
    mode = rng.integers(0, 4, (n, 1)); old = C[r, g, :, p]; some = np.any(w != 0, axis=1)[:, None]
    new = np.where(lv & (mode == 0) & some, -w, np.where(lv & (mode == 1), np.where(w < 0, -127, 127), old))
    C[r, g, :, p] = np.where(bs & (mode == 3), rng.choice(np.array([-1, 1]), (n, 16)), new)
def pack(D, C, hm):
    return {"det": np.ascontiguousarray((256 * D + C + 128).reshape(N, 128, V)).astype(np.int32), "ham": np.ascontiguousarray(hm.reshape(N, 128, M)).astype(np.float32).astype(BF)}
def setup_inputs(rng):
    D, C, hm = base(rng)
    for t in range(RO - 1, -1, -1): plant(rng, D, C, hm, 0.35, False, t, True)
    return pack(D, C, hm)
def setup_inputs_slots(rng):
    D, C, hm = base(rng, 2.0); C[:, :, 0] = np.where(np.any(C != 0, axis=2), C[:, :, 0], 1)
    for q in range(N):
        good, ch, c = kid(D[q:q + 1], C[q:q + 1], hm[q:q + 1], 0); mine = good[0] & ((mix(ch)[1][0] & (N - 1)) == ((q + 1) & (N - 1)))
        for g in range(8):
            hit = rng.permutation(np.nonzero(mine[g])[0]); rest = rng.permutation(np.nonzero(~mine[g])[0])
            n = min((CAP, CAP + 1, CAP - 1, S, 0, 1, CAP, CAP + 1)[g], len(hit))
            seq = np.concatenate([rng.permutation(np.concatenate([hit[:n], rest[:S - n]])), rng.permutation(np.concatenate([hit[n:], rest[S - n:]]))])
            k = int(rng.integers(S, V - 63)); o = rng.permutation(V); at = (np.concatenate([np.sort(o[:k]), o[k:]]) + STEP) & (V - 1)
            d2 = np.zeros_like(D[q, g]); c2 = np.zeros_like(C[q, g])
            d2[:, at] = D[q, g][:, seq]; c2[:, at[:k]] = C[q, g][:, seq[:k]]; D[q, g] = d2; C[q, g] = c2
    return pack(D, C, hm)
def setup_inputs_ties(rng):
    D, C, hm = base(rng); ev = np.ascontiguousarray(D[:, ::2]); u, h = mix(ev)
    x = np.take_along_axis(ev, rng.integers(0, 16, (N, 4, 1, V)), 2); y = np.take_along_axis(ev, rng.integers(0, 16, (N, 4, 1, V)), 2)
    goal = rng.permuted(np.concatenate([x, x + 1, x - 1, y, y + 1, ev[:, :, :1], ev[:, :, 15:], 0 * x, 0 * x + M - 1, 0 * x + 4095], axis=2), axis=2)
    e = ((goal - h[:, :, None]) * pow(37, -1, 4096)) & 4095; ok = (e >= 1) & (e <= 2032)
    e = np.take_along_axis(e, np.argmax(ok, axis=2)[:, :, None], 2); ok = np.any(ok, axis=2)[:, :, None]
    z = (np.arange(16)[:, None] + rng.integers(0, 16, (N, 4, 1, V))) & 15
    new = ((e >> 4) + (z < (e & 15))) * rng.choice(np.array([-1, 1]), (N, 4, 16, V)); live = np.any(C[:, ::2] != 0, axis=2)[:, :, None]
    C[:, ::2] = np.where(ok & live, new, C[:, ::2])
    hm[:, ::2] = 127; hm[:, 1::2] = rng.choice(np.array([0, 9, 60]), (N, 4, 1, M))
    hm[np.arange(N), 2 * rng.integers(0, 4, N) + 1] = 0
    plant(rng, D, C, hm, 0.2)
    return pack(D, C, hm)
def setup_inputs_twins(rng):
    D, C, hm = base(rng); hm = np.repeat(hm[:1], N, axis=0); ix = rng.integers(0, 40, (N, 8, 1, V))
    pd = np.repeat(recs(rng, (1, 8, 16, 40)), N, axis=0)
    pc = np.repeat(np.where(np.arange(40) < 12, rng.integers(0, 4, (1, 8, 16, 40)), rng.integers(4, 128, (1, 8, 16, 40))), N, axis=0)
    use = rng.random((N, 8, 1, V)) < 0.6; live = np.any(C != 0, axis=2)[:, :, None]
    sign = np.where(rng.random((N, 8, 1, V)) < 0.4, 1, rng.choice(np.array([-1, 1]), (N, 8, 16, V)))
    D = np.where(use, np.take_along_axis(pd, ix, 3), D)
    C = np.where(use & live, np.take_along_axis(pc, ix, 3) * sign, C)
    plant(rng, D, C, hm, 0.5); plant(rng, D, C, hm, 0.4); plant(rng, D, C, hm, 0.4, True)
    return pack(D, C, hm)
def setup_inputs_thin(rng):
    D, C, hm = base(rng, 2.0); lone = np.arange(16)[:, None] == rng.integers(0, 16, (N, 8, 1, V))
    C[:, 1::2] = np.where(lone, np.where(C == 0, -1, C), 0)[:, 1::2]
    C[:, :, 0] = np.where(np.any(C != 0, axis=2), C[:, :, 0], 1); sizes = np.array([0, 1, 5, S - 1, S, S + 1, V - 1, V])
    for q in range(N):
        for g in range(8):
            n = int(sizes[g]) if q == 0 else int(rng.choice(sizes)); o = rng.permutation(V)
            if n == 5: o = np.array([0, V - 1, STEP - 1, STEP, STEP + 1])
            keep = np.zeros(V, np.int64); keep[o[:n]] = 1; C[q, g] = C[q, g] * keep
    plant(rng, D, C, hm, 0.3)
    return pack(D, C, hm)
def setup_inputs_spread(rng):
    D, C, hm = base(rng)
    D = np.sort(((M - 15) * rng.random((N, 8, 16, V)) ** rng.choice(np.array([1.0, 4.0]), (N, 8, 1, V))).astype(np.int64), axis=2) + np.arange(16)[:, None]
    size = np.exp2(7 * rng.random((N, 8, 1, V))); live = np.any(C != 0, axis=2)[:, :, None]
    C = np.minimum((size * rng.random((N, 8, 16, V))).astype(np.int64), 127) * rng.choice(np.array([-1, 1]), (N, 8, 16, V)) * live
    hm = np.minimum((np.exp2(7 * rng.random((N, 8, 1, M))) * rng.random((N, 8, 16, M))).astype(np.int64), 127)
    plant(rng, D, C, hm, 0.3)
    return pack(D, C, hm)
def check_inputs(d):
    bad = []
    x = d["det"].astype(np.int64).reshape(N, 8, 16, V); o = x >> 8
    if np.min(o) < 0 or np.max(o) > M - 1: bad.append("orbitals of det")
    if np.min(x & 255) < 1: bad.append("counts of det")
    if not np.all(o[:, :, 1:] > o[:, :, :-1]): bad.append("rising orbitals of det")
    h = d["ham"].astype(np.float32)
    if not np.all((h >= 0) & (h <= 127) & (h == np.floor(h))): bad.append("numbers of ham")
    return bad
def reference(det, ham):
    x = det.astype(np.int64).reshape(N, 8, 16, V); D = x >> 8; C = (x & 255) - 128
    hm = ham.astype(np.float32).astype(np.int64).reshape(N, 8, 16, M); num = np.arange(P)[:, None]
    for t in range(RO):
        pl, on, good, ch, c = spawn(D, C, hm, t)
        sel = np.zeros((N, 8, V), bool); np.put_along_axis(sel, pl, on, 2)
        C = C - np.sign(C) * sel[:, :, None]
        f = good[:, :, None] & ((mix(ch)[1] & (N - 1))[:, :, None] == np.arange(N)[:, None])
        before = np.add.accumulate(f.astype(np.int64), axis=3) - f.astype(np.int64)
        q, g, r, s = np.nonzero(f & (before < CAP)); a = q * CAP + before[q, g, r, s]
        ad = np.zeros((N, 8, 16, A), np.int64); ac = np.zeros((N, 8, 16, A), np.int64); there = np.zeros((N, 8, A), bool)
        ad[r, g, :, a] = ch[q, g, :, s]; ac[r, g, :, a] = c[q, g, :, s]; there[r, g, a] = True
        u, h = mix(ad)
        p = ((h >> LN)[:, :, None] + num * (2 * u + 1)[:, :, None]) & (V - 1)
        live = np.any(C != 0, axis=2); lp = np.take_along_axis(live, p.reshape(N, 8, P * A), 2).reshape(N, 8, P, A)
        dp = np.take_along_axis(D, p.reshape(N, 8, 1, P * A), 3).reshape(N, 8, 16, P, A)
        same = np.all(dp == ad[:, :, :, None], axis=2) & lp
        score = np.where(same, num, np.where(lp, 2 * P, P + num))
        ok = there & (np.min(score, axis=2) < 2 * P); place = np.take_along_axis(p, np.argmin(score, axis=2)[:, :, None], 2)[:, :, 0]
        r, g, a = np.nonzero(ok); low = np.full((N, 8, V), A); np.minimum.at(low, (r, g, place[r, g, a]), a)
        r, g, a = np.nonzero(ok & (np.take_along_axis(low, place, 2) == np.arange(A))); b = place[r, g, a]
        D[r, g, :, b] = ad[r, g, :, a]; C[r, g, :, b] = np.clip(C[r, g, :, b] + ac[r, g, :, a], -127, 127)
    return {"y": (256 * D + C + 128).reshape(N, 128, V).astype(np.float32)}

@@ -1,0 +1,746 @@
+from concourse.bass import DstId, RemoteDMATransfer
+from concourse.mybir import AluOpType as O, ActivationFunctionType as F
+import math
+
+WAKE, SLACK, BETA = 0.15, 0.03, 1.2
+F32, BF, I32, U16, F16 = "float32", "bfloat16", "int32", "uint16", "float16"
+BUFS = {
+    F32: dict(TD=1280, QT=1280, ONE=160, NEGI=128, ZG=24, WT=24, SHP=128, SHN=128, QW=128, QE=128, DM=136, SW=16, SC=2, TRS=16,
+              TRA=16, WX=8, XI=8, THR=1, XJ=1, RC=1, B1=1, B2=1, MC=160, MR=16, PA=24, TV=1024, TM=1024, DB=64, RF=64,
+              LM=136, LD=16, DF=256, EM=64, EU=64, ET=256, EB=256, EC=256, ED=256, DP=256, DN=256, CH=256, CF32=256, ON=16,
+              OK1=16, SN0=16, QQ=64, K1=64, K2=32, K5=64, K6=64, K7=64, K8=16, FS=16, XF=256, AT=256, AD=256, QA=256,
+              QS=256, QN=256, CV=256, ZF=64, ST=16, S1=160, S2=160, S3=160, S4=80, S5=32, S6=16, S7=16, SN=16, PT=16, M3=16,
+              M4=16, M5=16, NU=16, PW=16, LO=16, YT=1280, YN=256, PR5=1536, SB0=512, SB1=512, SB2=512, IN0=256,
+              IN1=256, IN2=256, PF=32),
+    BF: dict(TC=1280, ham=3584, ONEB=256, G8=8, G16=8, SEL8=8, SELB=8, RW=8, TRI=128, IDB=128, IDN=128, KC=128, KD=136, C128=128,
+             C64=128, BIGL=128, R8=128, WC=128, WBIG=8, ZW=1280, IM=160, SV0=128, SV1=128, SK0=128, SK1=128, SS0=128, SS1=128,
+             QB=1024, LV=64, OL=1024, BS=1088, AB=256, CN=256, hv=4096, MK=4096, F4B=48, R4=128, SG=256, SNB=16, R5=128, OM=64,
+             CFD=256, ABF=256, ABN=256, XB=1024, CMP=2560, FD=32, R6=128, CO=256, CNW=256, SVX0=128, SVX1=128),
+    I32: dict(DET=1024, CI=1024, PI=16, PJ=1, PK=24, PL=24, R32=64, LOW=64, MX=16, E3=16, VV=16, F4=48, H1=32,
+              H2=32, HP=16, HV=16, SGI=16, N1=16, N2=16, N3=16, N4=16, N5=16, N6=16, N7=16, KM2=16, KM1=16, FI=256, I1=32, I2=32,
+              PR=16, OW=16, J1=48, J2=32, JP=16, ZD=64, ZI=160, ZJ=160, HQ=16, ST0=16, PN=16, PM=16, PLC=16, DG=32, SL2=16),
+    F16: dict(OA=1024),
+    U16: dict(GU=16, DU=256, OFF=16, ZU=160, PU=256, PO=16, FO=16),
+}
+SCRATCH, WIDTH, WHERE = {}, {}, {}
+for _d in BUFS:
+    _p = 0
+    for _n, _w in BUFS[_d].items():
+        _n = "hamt" if _n == "ham" else _n
+        WIDTH[_n] = _w
+        if _w <= 160:
+            WHERE[_n] = ("small_" + _d, _p)
+            _p += (_w + 15) // 16 * 16
+        else:
+            SCRATCH[_n] = ("sbuf", [128, _w], _d)
+    if _p:
+        SCRATCH["small_" + _d] = ("sbuf", [128, _p], _d)
+TWO = list(BUFS[F16]) + list(BUFS[BF]) + list(BUFS[U16])
+PSUM = ["P%d" % _k for _k in range(7)] + ["TP"]
+for _n in PSUM:
+    WIDTH[_n] = 128 if _n == "TP" else 512
+    SCRATCH[_n] = ("psum", [128, WIDTH[_n]], BF if _n == "TP" else F32)
+SEMAPHORES = ["qv", "qs", "qt", "qg", "ld0", "ld1", "st0", "snd", "rx0", "rx1", "rx2"]
+
+
+def rank_program(g, core, T, topo):
+    me = T.rank_of(core)
+    if me is None:
+        return
+    V, S, PE = g.vector, g.scalar, g.tensor
+    ENG = {"v": V, "s": S, "t": PE, "g": g, "d": g.sync}
+    cnt, known, clk = {"v": 0, "s": 0, "t": 0, "g": 0}, {q: {} for q in ENG}, {}
+    wr, rd, last = {}, {}, {}
+    semof = {"v": ("qv", 1), "s": ("qs", 1), "t": ("qt", 1), "g": ("qg", 1)}
+
+    def w(name, a=0, b=None, st=1, p=128):
+        b = WIDTH[name] if b is None else b
+        n, o = WHERE.get(name, (name, 0))
+        ap = T[n][0:p, o + a:o + b] if st == 1 else T[n][0:p, o + a:o + b:st]
+        m = 0
+        if st == 1:
+            m = ((1 << (b - a)) - 1) << a
+        else:
+            for c in range(a, b, st):
+                m |= 1 << c
+        return (ap, [(name, m)], [])
+
+    def ind(win, off):
+        return (win[0].indirect(off[0]), win[1], off[1], 16 * off[1][0][1].bit_count())
+
+    def wait(q, q2, k):
+        if known[q].get(q2, 0) >= k:
+            return
+        sem, inc = semof[q2]
+        ENG[q].wait_ge(T.sem[sem], k * inc)
+        for a, n in list(clk.get((q2, k), {}).items()) + [(q2, k)]:
+            if known[q].get(a, 0) < n:
+                known[q][a] = n
+
+    def deps(q, reads, writes):
+        need = {}
+
+        def add(q2, k):
+            if need.get(q2, 0) < k:
+                need[q2] = k
+        for n, m in reads + writes:
+            if n in PSUM:
+                for q2, k in last.get(n, {}).items():
+                    if q2 != q:
+                        add(q2, k)
+        for n, m in reads:
+            for q2, k, m2 in wr.get(n, []):
+                if m & m2:
+                    add(q2, k)
+        for n, m in writes:
+            for q2, k, m2 in wr.get(n, []):
+                if m & m2 and not (q == "t" and q2 == "t"):
+                    add(q2, k)
+            for q2, k, m2 in rd.get(n, []):
+                if m & m2:
+                    add(q2, k)
+        for q2, k in sorted(need.items(), key=lambda x: x[0] == q):
+            wait(q, q2, k)
+
+    def note(q, k, reads, writes):
+        clk[(q, k)] = dict(known[q] if q in known else {})
+        for n, m in writes:
+            wr[n] = [x for x in wr.get(n, []) if x[2] & ~m] + [(q, k, m)]
+            rd[n] = [x for x in rd.get(n, []) if x[2] & ~m]
+        for n, m in reads:
+            rd[n] = [x for x in rd.get(n, []) if not (x[0] == q and not x[2] & ~m)] + [(q, k, m)]
+        for n, m in reads + writes:
+            if n in PSUM:
+                last.setdefault(n, {})[q] = k
+
+    calls = []
+
+    def wide(x):
+        return x[3] if len(x) > 3 else x[1][0][1].bit_count()
+
+    def E(q, f, ins, outs, cost):
+        def emit(reads, writes):
+            deps(q, reads, writes)
+            cnt[q] += 1
+            f().then_inc(T.sem[semof[q][0]], 1)
+            note(q, cnt[q], reads, writes)
+        reads = [r for x in ins for r in x[1] + x[2]] + [r for x in outs for r in x[2]]
+        calls.append((q, emit, reads, [r for x in outs for r in x[1]], cost, 0.0))
+
+    def dma(q, out, in_, sem, reads, writes):
+        def emit(reads, writes):
+            deps(q, reads, writes)
+            ENG[q].dma_start(out=out, in_=in_).then_inc(T.sem[sem], 16)
+            semof[sem] = (sem, 16)
+            clk[(sem, 1)] = dict(known[q])
+            note(sem, 1, reads, writes)
+        calls.append((q, emit, reads, writes, 0.1, 5.0))
+
+    def schedule():
+        n = len(calls)
+        succ, npred = [[] for _ in range(n)], [0] * n
+        W, R, B = {}, {}, {}
+        for j, (q, emit, reads, writes, cost, lat) in enumerate(calls):
+            pred = {}
+
+            def edge(i, wk):
+                pred[i] = max(pred.get(i, 0.0), wk)
+            for nm, m in reads + writes:
+                if nm in PSUM:
+                    for q2, i in B.get(nm, {}).items():
+                        edge(i, 0.0 if q2 == q else WAKE)
+            for nm, m in reads:
+                for i, m2 in W.get(nm, []):
+                    if m & m2:
+                        edge(i, WAKE)
+            for nm, m in writes:
+                for i, m2 in W.get(nm, []) + R.get(nm, []):
+                    if m & m2:
+                        edge(i, 0.0 if q == calls[i][0] == "t" else WAKE)
+            for i, wk in pred.items():
+                succ[i].append((j, wk))
+            npred[j] = len(pred)
+            for nm, m in writes:
+                W[nm] = [x for x in W.get(nm, []) if x[1] & ~m] + [(j, m)]
+                R[nm] = [x for x in R.get(nm, []) if x[1] & ~m]
+            for nm, m in reads:
+                R.setdefault(nm, []).append((j, m))
+            for nm, m in reads + writes:
+                if nm in PSUM:
+                    B.setdefault(nm, {})[q] = j
+        way = [0.0] * n
+        for j in range(n - 1, -1, -1):
+            way[j] = calls[j][4] + calls[j][5] + max([wk + way[k] for k, wk in succ[j]] + [0.0])
+        free, est, order, avail = {}, [0.0] * n, [], {}
+        for j in range(n):
+            if not npred[j]:
+                avail.setdefault(calls[j][0], []).append(j)
+        while len(order) < n:
+            best = None
+            for q, a in avail.items():
+                if a:
+                    t0 = free.get(q, 0.0)
+                    s = min(max(t0, est[j]) for j in a)
+                    if best is None or s < best[0]:
+                        best = (s, q)
+            s, q = best
+            t0 = free.get(q, 0.0)
+            j = max((j for j in avail[q] if max(t0, est[j]) <= s + SLACK), key=lambda j: (way[j], -j))
+            soon = [i for i in avail[q] if way[i] > way[j] and s + SLACK < est[i] < s + calls[j][4] - BETA * (est[i] - s)]
+            if soon:
+                i = max(soon, key=lambda i: way[i])
+                fit = [f for f in avail[q] if max(t0, est[f]) + calls[f][4] <= est[i] + SLACK]
+                j = max(fit, key=lambda f: (way[f], -f)) if fit else i
+            avail[q].remove(j)
+            free[q] = max(t0, est[j]) + calls[j][4]
+            order.append(j)
+            for k, wk in succ[j]:
+                est[k] = max(est[k], free[q] + calls[j][5] + wk)
+                npred[k] -= 1
+                if not npred[k]:
+                    avail.setdefault(calls[k][0], []).append(k)
+        for j in order:
+            calls[j][1](calls[j][2], calls[j][3])
+
+    def col(x):
+        return [x] if isinstance(x, tuple) else []
+
+    def ap(x):
+        return x[0] if isinstance(x, tuple) else x
+
+    def vcost(o, a, k=1.0):
+        if len(a) > 3:
+            return 0.06 + a[3] * 0.0016
+        if len(o) > 3:
+            return 0.06 + o[3] * 0.0035
+        return max(64, wide(a) * k) * 0.00104
+
+    def tt(o, a, b, op):
+        k = 1.0 if any(x[1][0][0] in PSUM for x in (a, b)) else 2.0
+        E("v", lambda: V.tensor_tensor(out=o[0], in0=a[0], in1=b[0], op=op), [a, b], [o], vcost(o, a, k))
+
+    def ts(o, a, s1, op0, s2=None, op1=None):
+        kw = dict(scalar2=None) if op1 is None else dict(scalar2=ap(s2), op1=op1)
+        k = 0.5 if a[1][0][0] in TWO and o[1][0][0] in TWO else 1.0
+        E("v", lambda: V.tensor_scalar(out=o[0], in0=a[0], scalar1=ap(s1), op0=op0, **kw), [a] + col(s1) + col(s2), [o], vcost(o, a, k))
+
+    def cp(o, a):
+        E("v", lambda: V.tensor_copy(out=o[0], in_=a[0]), [a], [o], vcost(o, a))
+
+    def fill(o, c):
+        E("v", lambda: V.memset(o[0], c), [], [o], vcost(o, o))
+
+    def act(o, a, f=F.Copy, bias=0.0, scale=1.0):
+        E("s", lambda: S.activation(out=o[0], in_=a[0], func=f, bias=ap(bias), scale=ap(scale)), [a] + col(bias) + col(scale), [o],
+          vcost(o, a))
+
+    def mm(o, l, r, start=True, stop=True):
+        k = 4 if l[1][0][0] in BUFS[F32] else 1
+        E("t", lambda: PE.matmul(out=o[0], lhsT=l[0], rhs=r[0], start=start, stop=stop), [l, r], [o], max(64, wide(r)) * k * 0.00104)
+
+    def tr(o, a):
+        E("t", lambda: PE.transpose(out=o[0], in_=a[0], identity=w("IDB")[0]), [a, w("IDB")], [o], 0.13)
+
+    def iota(o, pat, base, cm):
+        E("g", lambda: g.iota(o[0], pattern=pat, base=base, channel_multiplier=cm, allow_small_or_imprecise_dtypes=True), [], [o],
+          0.15 + 0.002 * wide(o))
+
+    def aff(o, a, pat, op, base, cm):
+        E("g", lambda: g.affine_select(out=o[0], in_=a[0], pattern=pat, compare_op=op, fill=0.0, base=base, channel_multiplier=cm),
+          [a], [o], 0.2 + 0.002 * wide(o))
+
+    ALL = (1 << 1024) - 1
+    dma("d", T["DET"][:, :], T.det[:, :], "ld0", [], [("DET", ALL)])
+    dma("d", T["hamt"][:, :], T.ham[:, :], "ld1", [("DET", ALL)], [("hamt", (1 << 3584) - 1)])
+
+    fill(w("ONEB"), 1.0)
+    fill(w("ONE"), 1.0)
+    fill(w("NEGI"), -1.0)
+    fill(w("QE"), 4096.0)
+    fill(w("C64"), 64.0)
+    iota(w("PI"), [[-1, 16]], 16, 1)
+    iota(w("PJ"), [[0, 1]], 0, 1)
+    aff(w("G8"), w("ONEB", 0, 8), [[-16, 8]], O.is_ge, 0, 1)
+    aff(w("G8"), w("G8"), [[16, 8]], O.is_ge, 15, -1)
+    for t in range(3):
+        iota(w("PK", 8 * t, 8 * t + 8), [[128, 8]], 310 * (t + 1), 1)
+    aff(w("TRI"), w("ONEB", 0, 128), [[1, 128]], O.is_ge, -1, -1)
+    iota(w("SW"), [[16, 16]], 1024, 0)
+    iota(w("KD"), [[0, 8], [-2048, 17]], 0, 0)
+    aff(w("DM"), w("ONE", 0, 136), [[-16, 8], [0, 17]], O.is_ge, 0, 1)
+    aff(w("DM"), w("DM"), [[16, 8], [0, 17]], O.is_ge, 15, -1)
+    aff(w("IDB"), w("ONEB", 0, 128), [[-1, 128]], O.is_equal, 0, 1)
+    aff(w("QE"), w("QE"), [[-16, 8], [-2, 16]], O.is_equal, 0, 1)
+    aff(w("QW"), w("ONE", 0, 128), [[-16, 8], [-2, 16]], O.is_equal, -1, 1)
+    tt(w("QW"), w("QW"), w("QE"), O.add)
+    aff(w("QW"), w("QW"), [[0, 8], [-1, 16]], O.is_ge, 7, 0)
+    aff(w("SHP"), w("ONE", 0, 128), [[1, 128]], O.is_equal, -1, -1)
+    aff(w("SHN"), w("ONE", 0, 128), [[1, 128]], O.is_equal, 1, -1)
+    iota(w("KC"), [[-1, 16], [0, 8]], 15, 0)
+    iota(w("SC"), [[128, 2]], 0, 1)
+    iota(w("WT", 0, 8), [[-208, 8]], 5, 13)
+    iota(w("WT", 8, 16), [[224, 8]], 255, -14)
+    aff(w("WT", 0, 16), w("WT", 0, 16), [[0, 2], [-16, 8]], O.is_ge, 0, 1)
+    aff(w("WT", 0, 16), w("WT", 0, 16), [[0, 2], [16, 8]], O.is_ge, 15, -1)
+    aff(w("WT", 16, 24), w("ONE", 0, 8), [[-16, 8]], O.is_equal, -15, 1)
+    ts(w("PL"), w("PK"), 1023, O.bitwise_and)
+    ts(w("PA"), w("PL"), -2048.0, O.add, 0.5, O.mult)
+    ts(w("PI"), w("PI"), 15, O.bitwise_and)
+    ts(w("MR"), w("PI"), 0.0, O.is_equal)
+    ts(w("PJ"), w("PJ"), 15, O.bitwise_and)
+    cp(w("RC"), w("PJ"))
+    ts(w("SW"), w("SW"), w("RC"), O.add)
+    aff(w("NEGI"), w("NEGI"), [[-1, 128]], O.is_equal, 0, 1)
+    for h in range(2):
+        aff(w("SV%d" % h), w("C64"), [[-2, 8], [0, 16]], O.is_equal, -h, 1)
+        aff(w("SK%d" % h), w("ONEB", 0, 128), [[-2, 8], [0, 16]], O.is_equal, -32 - h, 1)
+        aff(w("SS%d" % h), w("ONEB", 0, 128), [[-2, 8], [0, 16]], O.is_equal, -h, 1)
+
+    MAG = 12582912.0
+    START = [310 * (t + 1) & 1023 for t in range(3)]
+
+    def rot(t, a, b):
+        s, cut = START[t], 1024 - START[t]
+        out = []
+        if a < cut:
+            out.append((a, min(b, cut), a + s))
+        if b > cut:
+            out.append((max(a, cut), b, max(a, cut) - cut))
+        return out
+
+    for c in (0, 512):
+        ts(w("CI", c, c + 512), w("DET", c, c + 512), 255, O.bitwise_and)
+        ts(w("TC", c, c + 512), w("CI", c, c + 512), -128.0, O.add)
+    for a, b in ((0, 202), (202, 714), (714, 1024)):
+        for x, y, p in rot(0, a, b):
+            act(w("QB", x, y), w("TC", p, p + y - x), F.Abs)
+    for c in (0, 512):
+        ts(w("TV", c, c + 512), w("DET", c, c + 512), -128.0, O.add, 1 / 256, O.mult)
+        act(w("TM", c, c + 512), w("TV", c, c + 512), F.Identity, MAG)
+        act(w("TD", c, c + 512), w("TM", c, c + 512), F.Identity, -MAG)
+    fill(w("SHP", 0, 128, 16), 0.0)
+    fill(w("SHN", 15, 128, 16), 0.0)
+    fill(w("BIGL"), 0.0)
+    fill(w("BIGL", 15, 128, 16), 64.0)
+    fill(w("C128"), 1 / 128)
+    fill(w("TC", 1024, 1280), 0.0)
+    fill(w("TD", 1024, 1280), 0.0)
+    fill(w("ZG"), 0.0)
+    cp(w("ZG", 8, 16), w("G8"))
+    ts(w("G16"), w("G8"), 16.0 * 37, O.mult)
+    SEL = [w("ZG", 8, 24), w("ZG", 0, 16)]
+
+    for h in range(2):
+        aff(w("SVX%d" % h), w("ONEB", 0, 128), [[-2, 8], [0, 16]], O.is_equal, -16 - h, 1)
+    iota(w("TRS"), [[0, 8], [128, 2]], 256, 1)
+    iota(w("TRA"), [[0, 8], [128, 2]], 1024, 1)
+    iota(w("MC"), [[1, 10], [0, 16]], 2048, 0)
+    iota(w("IM"), [[1, 10], [0, 16]], 0, 0)
+    iota(w("XI"), [[16, 8]], 0, 0)
+    iota(w("XJ"), [[0, 1]], 0, 1)
+    aff(w("SEL8"), w("ONEB", 0, 8), [[-16, 8]], O.is_equal, -8, 1)
+    aff(w("RW"), w("G8"), [[16, 8]], O.is_ge, 7, -1)
+    for h in range(2):
+        z = w("ZW", 640 * h + 160, 640 * h + 320)
+        aff(z, w("ONEB", 0, 160), [[0, 10], [-16, 16]], O.is_ge, 128 * h, 1)
+        aff(z, z, [[0, 10], [16, 16]], O.is_ge, 15 - 128 * h, -1)
+
+    def late_constants():
+        for h in range(2):
+            tt(w("SV%d" % h), w("SV%d" % h), w("SVX%d" % h), O.add)
+        fill(w("R8"), 0.0)
+        cp(w("R8", 8, 128, 16), w("G8"))
+        ts(w("B1"), w("RC"), -8192.0, O.mult, 8192.0 * 15 + 4096, O.add)
+        ts(w("B2"), w("RC"), 8192.0, O.mult, 4096 - 8192.0 * 15, O.add)
+        for t in range(3):
+            fill(w("SB%d" % t, 0, 256), 0.0)
+
+    def last_constants():
+        ts(w("SELB"), w("SEL8"), 16.0, O.mult)
+        tt(w("RW"), w("RW"), w("SELB"), O.add)
+        for h in range(2):
+            z = [w("ZW", 640 * h + 160 * f, 640 * h + 160 * f + 160) for f in range(4)]
+            ts(z[0], z[1], 32.0, O.mult)
+            tt(z[3], z[1], w("IM"), O.mult)
+            ts(z[2], z[3], 32.0, O.mult)
+        ts(w("XI"), w("XI"), w("RC"), O.add)
+        L3 = math.log(3.0)
+        ts(w("XI"), w("XI"), -L3, O.mult, 55 * L3, O.add)
+        ts(w("XJ"), w("XJ"), -L3, O.mult, 55 * L3, O.add)
+        act(w("WX"), w("XI"), F.Exp)
+        act(w("THR"), w("XJ"), F.Exp)
+        ts(w("THR"), w("THR"), 2.2, O.mult)
+        for c in range(8):
+            ts(w("WC", 8 * c, 8 * c + 8), w("G8"), w("WX", c, c + 1), O.mult)
+        ts(w("WBIG"), w("G8"), 1e29, O.mult)
+        ts(w("IDN"), w("IDB"), -1 / 256, O.mult)
+
+    def t2w(src, n, X):
+        for r in range(16):
+            if r % 2:
+                act(w(X, r, 16 * n, 16), src, F.Copy, 0.0, w("MR", r, r + 1))
+            else:
+                ts(w(X, r, 16 * n, 16), src, w("MR", r, r + 1), O.mult)
+
+    peers = [q for q in range(4) if q != me]
+    near = [q for q in peers if T.cores[q] in topo.cores_of(core)]
+    far = [q for q in peers if q not in near]
+
+    def send(t):
+        sb, plan, used, share = "SB%d" % t, [], [], []
+        for i, q in enumerate(far):
+            e = topo.engines(core, T.cores[q])
+            k = len(e) // len(far)
+            share.append(k)
+            plan.append((q, e[i * k:(i + 1) * k]))
+            used += e[i * k:(i + 1) * k]
+        for i, q in enumerate(near):
+            e = [x for x in topo.engines(core, T.cores[q]) if x not in used]
+            k = min([len(e) // len(near)] + share)
+            plan.append((q, e[i * k:(i + 1) * k]))
+        got = sum(len(e) for q, e in plan)
+        rx = "rx%d" % t
+
+        def emit(reads, writes):
+            deps("g", reads, [])
+            tf = []
+            for q, e in plan:
+                rid, pid = topo.addr(T.cores[q], core)
+                tf.append(RemoteDMATransfer(dst_ids=[DstId(rid=rid, pnc=pid)], dma_engine_mask=sum(1 << x for x in e),
+                                            remote_sem=T.sem[rx], src=T[sb][:, 64 * q:64 * q + 64],
+                                            dst=T["IN%d" % t][:, 64 * me:64 * me + 64], alu_op=0))
+            g.remote_dma_fused(tf, local_sem=T.sem["snd"])
+            semof[rx] = (rx, got)
+            note(rx, 1, [], writes)
+        calls.append(("g", emit, w(sb, 0, 256)[1], [r for q in peers for r in w("IN%d" % t, 64 * q, 64 * q + 64)[1]], 0.5, 4.0))
+        act(w("IN%d" % t, 64 * me, 64 * me + 64), w(sb, 64 * me, 64 * me + 64))
+        return got
+
+    def first_qt(b):
+        mm(w("P6", 0, 512), w("QW"), w("TD", 512 * b, 512 * b + 512), True, False)
+        parts = [(0, 310, 714), (310, 512, 0)] if b == 0 else [(0, 512, 202)]
+        for i, (x, y, p) in enumerate(parts):
+            mm(w("P6", x, y), w("R8"), w("QB", p, p + y - x), False, i == len(parts) - 1)
+        act(w("QT", 512 * b, 512 * b + 512), w("P6", 0, 512))
+
+    sent = 0
+    for t in range(3):
+        IN, SB = "IN%d" % t, "SB%d" % t
+        if t:
+            for a in range(0, 1024, 256):
+                for x, y, p in rot(t, a, a + 256):
+                    act(w("QB", x, y), w("QT", p, p + y - x))
+        for k in range(8):
+            mm(w("P0", 8 * k, 8 * k + 8), w("QB", 128 * k, 128 * k + 128), w("SEL8") if t else w("G8"))
+        ts(w("LV"), w("P0", 0, 64), 0.0, O.is_gt)
+        ts(w("DB"), w("P0", 0, 64), 0.0, O.is_equal, 4096.0, O.mult)
+        mm(w("P1", 0, 64), w("TRI"), w("LV"), True, False)
+        for d in range(1, 8):
+            mm(w("P1", 8 * d, 64), w("ONEB", 0, 128), w("LV", 0, 64 - 8 * d), False, d == 7)
+        tt(w("RF"), w("P1", 0, 64), w("DB"), O.add)
+        tt(w("R32"), w("P1", 0, 64), w("DB"), O.add)
+        ts(w("LOW"), w("R32"), 15, O.bitwise_and)
+        for h in range(17):
+            act(w("BS", h, 1088, 17), w("RF"), F.Sign, 0.5 - 16 * h)
+        if t == 0:
+            late_constants()
+        for l in range(16):
+            ts(w("OL", l, 1024, 16), w("LOW"), float(l), O.is_equal)
+        for k in range(8):
+            c = (128 * k, 128 * k + 128)
+            ts(w("OA", *c), w("OL", *c), w("PA", 8 * t + k, 8 * t + k + 1), O.mult)
+        mm(w("P2", 0, 136), w("C128"), w("KD"), True, False)
+        for k in range(8):
+            mm(w("P2", 0, 136), w("OA", 128 * k, 128 * k + 128), w("BS", 136 * k, 136 * k + 136), False, k == 7)
+        for k in range(8):
+            mm(w("P0", 0, 8), w("ONEB", 0, 128), w("LV", 8 * k, 8 * k + 8), k == 0, k == 7)
+        if t:
+            cp(ind(w("TD"), w("FO")), w("AD"))
+        tt(w("LM"), w("P2", 0, 136), w("DM"), O.mult)
+        for n in (68, 34, 17):
+            tt(w("LM", 0, n), w("LM", 0, n), w("LM", n, 2 * n), O.add)
+        tt(w("LD"), w("LM", 0, 16), w("LM", 1, 17), O.subtract)
+        tt(w("GU"), w("LD"), w("SW"), O.min)
+        act(w("AB"), ind(w("TC"), w("GU")), F.Abs)
+        mm(w("P3", 0, 256), w("IDB"), w("AB"))
+        cp(w("DU"), ind(w("TD"), w("GU")))
+        CUT = [0, 64, 128, 192, 256]
+
+        def look(a, b):
+            return w("hv", 16 * a, 16 * b), ind(w("hamt"), w("DU", a, b))
+        for j in range(1, 4):
+            act(*look(CUT[j], CUT[j + 1]))
+        act(w("CN"), ind(w("TC"), w("GU")))
+        cp(w("DF"), w("DU"))
+        cp(*look(CUT[0], CUT[1]))
+        for h in range(2):
+            mm(w("P0", 64 + h, 96, 2), w("DF", 128 * h, 128 * h + 128), w("WT", 0, 16))
+
+        def mins(a, b):
+            for k in list(range(8, 16)) + list(range(8)):
+                tt(w("MK", 256 * k + a, 256 * k + b), w("hv", 16 * a + k, 16 * b, 16), w("P3", a, b), O.min)
+
+        UP = ["P1", "P6"]
+
+        def tree(h):
+            for p, ks in ((UP[h], range(8, 16)), ("P%d" % (1 + h), range(8))):
+                mm(w(p, 8 * ks[0], 8 * ks[0] + 64), w("C128"), w("KC", 8 * ks[0], 8 * ks[0] + 64), True, False)
+                for k in ks:
+                    mm(w(p, 8 * k, 8 * k + 8), w("MK", 256 * k + 128 * h, 256 * k + 128 * h + 128), w("G16"), False, k == ks[-1])
+            cp(w("EM" if h else "EU"), w(UP[h], 64, 128))
+
+        def top(h):
+            p, o = "P%d" % (1 + h), 128 * h
+            tt(w("ET", o, o + 64), w(p, 0, 64), w("EM" if h else "EU"), O.max)
+            for n in (32, 16):
+                tt(w("ET", o, o + n), w("ET", o, o + n), w("ET", o + n, o + 2 * n), O.max)
+            tt(w("MX", h, 16, 2), w("ET", o, o + 8), w("ET", o + 8, o + 16), O.max)
+        mm(w("P4", 0, 256), w("SHP"), w("DF"))
+        mm(w("P4", 256, 512), w("SHN"), w("DF"), True, False)
+        mm(w("P4", 256, 512), w("BIGL"), w("ONEB"), False, True)
+        mm(w("P5", 0, 256), w("NEGI"), w("DF"), True, False)
+        act(w("DP"), w("P4", 0, 256))
+        act(w("DN"), w("P4", 256, 512))
+        if t == 0:
+            first_qt(0)
+        mins(0, CUT[2])
+        tree(0)
+        mins(CUT[2], CUT[3])
+        for h in range(2):
+            ts(w("ON", h, 16, 2), w("P0", 0, 8), w("SC", h, h + 1), O.is_gt)
+        cp(w("H1"), w("P0", 64, 96))
+        ts(w("H2"), w("H1"), 4095, O.bitwise_and)
+        tt(w("HP"), w("H2", 0, 16), w("H2", 16, 32), O.mult)
+        ts(w("HP"), w("HP"), 5, O.arith_shift_right)
+        ts(w("HV"), w("HP"), 16.0, O.mult, 16.0 * t, O.add)
+        top(0)
+        mins(CUT[3], CUT[4])
+        tree(1)
+        top(1)
+        ts(w("F4", 32, 48), w("MX"), 15, O.bitwise_and)
+        tt(w("E3"), w("MX"), w("HV"), O.add)
+        ts(w("F4", 0, 16), w("E3"), 10, O.arith_shift_right, 63, O.bitwise_and)
+        ts(w("F4", 16, 32), w("E3"), 4, O.arith_shift_right, 63, O.bitwise_and)
+        cp(w("F4B"), w("F4"))
+        tr(w("TP", 0, 128, 1, 48), w("F4B"))
+        r4 = w("R4", 0, 128, 1, 48)
+        cp(r4, w("TP", 0, 128, 1, 48))
+        for h in range(2):
+            mm(w("P2", 128 * h, 128 * h + 128), w("SK%d" % h, 0, 128, 1, 48), r4)
+        for h in range(2):
+            mm(w("P6", 128 * h, 128 * h + 128), w("SV%d" % h, 0, 128, 1, 48), r4)
+        for h in range(2):
+            mm(w("P5", 128 * h, 128 * h + 128), w("SV%d" % h, 0, 128, 1, 48), r4, False, h == 1)
+        act(w("P0", 0, 256), w("P2", 0, 256), F.Relu, w("B2"), 8192.0)
+        act(w("P1", 0, 256), w("P2", 0, 256), F.Relu, w("B1"), -8192.0)
+        act(w("SG"), w("P5", 0, 256), F.Sign)
+        ts(w("FI"), w("CN"), 0.25, O.mult, -0.375, O.add)
+        ts(w("KM2"), w("F4", 32, 48), 2.0, O.mult)
+        ts(w("KM1"), w("F4", 32, 48), 1.0, O.add)
+        ts(w("VV"), w("E3"), 4, O.arith_shift_right, 4095, O.bitwise_and)
+        ts(w("OK1"), w("VV"), 3584.0, O.is_lt)
+        tt(w("OK1"), w("OK1"), w("ON"), O.mult)
+        tt(w("EB"), w("DN"), w("P6", 0, 256), O.min)
+        tt(w("P0", 0, 256), w("DF"), w("P0", 0, 256), O.add)
+        tt(w("P1", 0, 256), w("DF"), w("P1", 0, 256), O.subtract)
+        tt(w("EC"), w("EB"), w("P0", 0, 256), O.min)
+        tt(w("P1", 0, 256), w("DP"), w("P1", 0, 256), O.max)
+        tt(w("CH"), w("EC"), w("P1", 0, 256), O.max)
+        for h in range(2):
+            mm(w("P3", h, 16, 2), w("SG", 128 * h, 128 * h + 128), w("G8"))
+        for h in range(2):
+            mm(w("P2", h, 32, 2), w("CH", 128 * h, 128 * h + 128), w("WT", 0, 16))
+        act(w("P4", 0, 256), w("CH"), F.Copy, 0.0, 256.0)
+        cp(w("SGI"), w("P3", 0, 16))
+        tt(w("N1"), w("SGI"), w("KM2"), O.add)
+        ts(w("N2"), w("N1"), 14.0, O.is_gt)
+        ts(w("N4"), w("SGI"), 1, O.arith_shift_right)
+        tt(w("N5"), w("N4"), w("KM1"), O.add)
+        tt(w("N6"), w("N5"), w("N2"), O.add)
+        ts(w("N7"), w("N6"), 1, O.bitwise_and)
+        ts(w("SNB"), w("N7"), -2.0, O.mult, 1.0, O.add)
+        tr(w("TP", 0, 128, 1, 16), w("SNB"))
+        ts(w("N3"), w("SGI"), 1, O.bitwise_and)
+        ts(w("SN0"), w("N3"), 0.0, O.is_equal)
+        tt(w("OK1"), w("OK1"), w("SN0"), O.mult)
+        for q in range(4):
+            ts(w("QQ", 16 * q, 16 * q + 16), w("OK1"), -8.0, O.mult, 8.0 + q, O.add)
+        cp(w("R5", 0, 128, 1, 16), w("TP", 0, 128, 1, 16))
+        for h in range(2):
+            mm(w("P0", 128 * h, 128 * h + 128), w("SS%d" % h, 0, 128, 1, 16), w("R5", 0, 128, 1, 16))
+        cp(w("I1"), w("P2", 0, 32))
+        ts(w("I2"), w("I1"), 4095, O.bitwise_and)
+        tt(w("PR"), w("I2", 0, 16), w("I2", 16, 32), O.mult)
+        ts(w("OW"), w("PR"), 5, O.arith_shift_right, 3, O.bitwise_and)
+        for q in range(4):
+            tt(w("OM", 16 * q, 16 * q + 16), w("OW"), w("QQ", 16 * q, 16 * q + 16), O.is_equal)
+        mm(w("P5", 0, 64), w("TRI"), w("OM"), True, False)
+        for q in range(4):
+            mm(w("P5", 16 * q + 1, 16 * q + 16, 2), w("ONEB", 0, 128), w("OM", 16 * q, 16 * q + 16, 2), False, q == 3)
+        tt(w("CF32"), w("FI"), w("P0", 0, 256), O.mult)
+        for q in range(4):
+            ts(w("K1", 16 * q, 16 * q + 16), w("OM", 16 * q, 16 * q + 16), -4096.0, O.mult, 4096.0 + 64 * q, O.add)
+        ts(w("K5"), w("P5", 0, 64), 64.0, O.is_ge, 4096.0, O.mult)
+        tt(w("K6"), w("P5", 0, 64), w("K1"), O.add)
+        tt(w("K7"), w("K5"), w("K6"), O.add)
+        tt(w("K2"), w("K7", 0, 32), w("K7", 32, 64), O.min)
+        tt(w("K8"), w("K2", 0, 16), w("K2", 16, 32), O.min)
+        for h in range(2):
+            tt(w("FS", 8 * h, 8 * h + 8), w("K8", h, 16, 2), w("TRS", h, 16, 2), O.min)
+        t2w(w("FS"), 16, "XF")
+        for h in range(2):
+            mm(w("P6", 0, 16), w("XF", 128 * h, 128 * h + 128), SEL[h], h == 0, h == 1)
+        tt(w("ED"), w("CF32"), w("P4", 0, 256), O.add)
+        cp(w("OFF"), w("P6", 0, 16))
+        cp(ind(w(SB), w("OFF")), w("ED"))
+        sent += send(t)
+        act(w("P3", 256, 512), w("CN"), F.Sign)
+        if t == 0:
+            first_qt(1)
+        tt(w("CFD"), w("CN"), w("P3", 256, 512), O.subtract)
+        act(w("ABF"), w("CFD"), F.Abs)
+        mm(w("P0", 0, 256), w("QW"), w("DF"), True, False)
+        mm(w("P0", 0, 256), w("R8"), w("ABF"), False, True)
+        act(w("QS"), w("P0", 0, 256))
+        cp(ind(w("TC"), w("GU")), w("CFD"))
+        if t == 0:
+            last_constants()
+        cp(ind(w("QT"), w("GU")), w("QS"))
+        if t == 2:
+            for b in range(2):
+                mm(w("P5", 0, 512), w("NEGI"), w("TD", 512 * b, 512 * b + 512), True, False)
+                mm(w("P5", 0, 512), w("IDN"), w("TC", 512 * b, 512 * b + 512), False, True)
+                act(w("YT", 512 * b, 512 * b + 512), w("P5", 0, 512), F.Copy, 128.0, -256.0)
+        ts(w("AT", 0, 128), w(IN, 0, 128), 1 / 256, O.mult, MAG, O.add)
+        act(w("AT", 128, 256), w(IN, 128, 256), F.Identity, MAG, 1 / 256)
+        ts(w("AD", 0, 128), w("AT", 0, 128), -MAG, O.add)
+        act(w("AD", 128, 256), w("AT", 128, 256), F.Identity, -MAG)
+        for h in range(2):
+            mm(w("P1", h, 48, 2), w("AD", 128 * h, 128 * h + 128), w("WT"))
+        mm(w("P2", 0, 256), w("QW"), w("AD"))
+        act(w("P6", 0, 256), w("AD"), F.Copy, 0.0, -256.0)
+        cp(w("J1"), w("P1", 0, 48))
+        ts(w("J2"), w("J1", 0, 32), 4095, O.bitwise_and)
+        tt(w("JP"), w("J2", 0, 16), w("J2", 16, 32), O.mult)
+        ts(w("ZD", 32, 48), w("J2", 0, 16), 4, O.arith_shift_right, 31, O.bitwise_and)
+        ts(w("SL2"), w("J2", 0, 16), 15, O.bitwise_and)
+        ts(w("ZD", 0, 16), w("JP"), 12, O.arith_shift_right, 31, O.bitwise_and)
+        ts(w("ZD", 16, 32), w("JP"), 7, O.arith_shift_right, 31, O.bitwise_and)
+        ts(w("ZD", 48, 64), w("SL2"), 2.0, O.mult, 1.0, O.add)
+        for h in range(2):
+            cp(w("ZF", 32 * h, 32 * h + 32), w("ZD", h, 64, 2))
+        t2w(w("ZF"), 64, "XB")
+        act(w("QA"), w("P2", 0, 256))
+        ts(w("HQ"), w("JP"), 7, O.arith_shift_right, 1023, O.bitwise_and)
+        ts(w("ST0"), w("J2", 0, 16), 511, O.bitwise_and)
+        ts(w("ST"), w("ST0"), 2.0, O.mult, 1.0, O.add)
+        ts(w("NU"), w("J1", 32, 48), 1.0, O.is_lt, 4096.0, O.mult)
+        tt(w("P6", 0, 256), w(IN), w("P6", 0, 256), O.add)
+        for c in range(2):
+            for h in range(2):
+                for f in range(4):
+                    mm(w("P%d" % (3 + c), 0, 80), w("XB", (32 * h + 8 * f) * 16, (32 * h + 8 * f) * 16 + 128),
+                       w("ZW", 640 * h + 160 * f + 80 * c, 640 * h + 160 * f + 80 * c + 80), h + f == 0, h + f == 4)
+            z = (80 * c, 80 * c + 80)
+            cp(w("ZI", *z), w("P%d" % (3 + c), 0, 80))
+            ts(w("ZJ", *z), w("ZI", *z), 1023, O.bitwise_and)
+            cp(w("ZU", *z), w("ZJ", *z))
+        SCP = ["P5", "P0", "P1"]
+
+        def probe(m):
+            o = w("CMP", 256 * m, 256 * m + 256)
+            if m < 4:
+                tt(o, ind(w("QT", 0, 1024), w("ZU", 16 * m, 16 * m + 16)), w("QA"), O.is_equal)
+            else:
+                tt(o, w("PR5", 256 * (m - 4), 256 * (m - 3)), w("P2", 0, 256), O.is_equal)
+            for h in range(2):
+                mm(w(SCP[0 if m < 5 else 1 if m < 8 else 2], 16 * (m % 5) + h, 16 * (m % 5) + 16, 2),
+                   w("CMP", 256 * m + 128 * h, 256 * m + 128 * h + 128), w("RW"))
+
+        def score(c):
+            a, b = ((0, 5), (5, 8), (8, 10))[c]
+            p, z = w(SCP[c], 16 * (a % 5), 16 * (b - 1) % 80 + 16), (16 * a, 16 * b)
+            ts(w("S2", *z), p, 8.0, O.is_ge, -1024.0, O.mult)
+            ts(p, p, 8.0, O.is_equal, -1024.0, O.mult)
+            tt(w("S3", *z), w("S2", *z), w("MC", *z), O.add)
+            tt(w("S1", *z), p, w("S3", *z), O.add)
+        for m in range(6):
+            act(w("PR5", 256 * m, 256 * m + 256), ind(w("QT", 0, 1024), w("ZU", 16 * m + 64, 16 * m + 80)))
+        for m in range(6):
+            probe(m)
+        score(0)
+        tt(w("S4", 0, 32), w("S1", 0, 32), w("S1", 32, 64), O.min)
+        tt(w("S5", 0, 16), w("S4", 0, 16), w("S4", 16, 32), O.min)
+        tt(w("S6"), w("S5", 0, 16), w("S1", 64, 80), O.min)
+        for m in (6, 7):
+            probe(m)
+        score(1)
+        tt(w("S4", 32, 48), w("S1", 80, 96), w("S1", 96, 112), O.min)
+        tt(w("S5", 16, 32), w("S4", 32, 48), w("S1", 112, 128), O.min)
+        tt(w("S4", 48, 64), w("S5", 16, 32), w("S6"), O.min)
+        for m in (8, 9):
+            probe(m)
+        score(2)
+        tt(w("S4", 64, 80), w("S1", 128, 144), w("S1", 144, 160), O.min)
+        tt(w("S7"), w("S4", 64, 80), w("S4", 48, 64), O.min)
+        tt(w("M3"), w("S7"), w("ST"), O.mult)
+        tt(w("SN"), w("S7"), w("NU"), O.add)
+        ts(w("M4"), w("SN"), 2048.0, O.is_ge, 2048.0, O.mult)
+        ts(w("M5"), w("SN"), 2048.0, O.is_ge, 32.0, O.mult)
+        tt(w("PN"), w("M3"), w("HQ"), O.add)
+        ts(w("DG", 0, 16), w("PN"), 6, O.arith_shift_right, 15, O.bitwise_and)
+        ts(w("DG", 16, 32), w("PN"), 63, O.bitwise_and)
+        tt(w("FD", 0, 16), w("DG", 0, 16), w("M5"), O.add)
+        cp(w("FD", 16, 32), w("DG", 16, 32))
+        ts(w("PM"), w("PN"), 1023, O.bitwise_and)
+        tt(w("PLC"), w("PM"), w("M4"), O.add)
+        tt(w("PT"), w("PLC"), w("TRA"), O.min)
+        tr(w("TP", 0, 128, 1, 32), w("FD"))
+        for h in range(2):
+            cp(w("PF", 8 * h, 8 * h + 8), w("PLC", h, 16, 2))
+        cp(w("R6", 0, 128, 1, 32), w("TP", 0, 128, 1, 32))
+        for h in range(2):
+            mm(w("P0", 128 * h, 128 * h + 128), w("SV%d" % h, 0, 128, 1, 32), w("R6", 0, 128, 1, 32))
+        t2w(w("PF", 0, 16), 16, "XF")
+        for h in range(2):
+            mm(w("P1", 0, 16), w("XF", 128 * h, 128 * h + 128), SEL[h], h == 0, h == 1)
+        cp(w("PU"), w("P0", 0, 256))
+        cp(w("PW"), w("P1", 0, 16))
+        ts(w("PO"), w("PW"), 1279.0, O.min)
+        act(w("CO"), ind(w("TC"), w("PO")))
+        if t == 2:
+            act(w("P1", 0, 256), w("AD"), F.Copy, 128.0, 256.0)
+        tt(w("CV"), w("CO"), w("P6", 0, 256), O.add)
+        ts(w("CNW"), w("CV"), 127.0, O.min, -127.0, O.max)
+        if t < 2:
+            act(w("ABN"), w("CNW"), F.Abs)
+            mm(w("P2", 0, 256), w("R8"), w("ABN"))
+            tt(w("QN"), w("QA"), w("P2", 0, 256), O.add)
+        else:
+            tt(w("YN"), w("CNW"), w("P1", 0, 256), O.add)
+        for c in range(16):
+            a = 0 if c < 8 else 128
+            ts(w("MK", 256 * c + a, 256 * c + 256), w("PU", a, 256), w("PW", c, c + 1), O.is_equal)
+            wc = w("WC", 8 * (c % 8), 8 * (c % 8) + 8)
+            if c < 8:
+                mm(w("P3", 0, 16, 2), w("MK", 256 * c, 256 * c + 128), wc, c == 0, c == 7)
+            mm(w("P4", 1, 16, 2), w("MK", 256 * c + 128, 256 * c + 256), wc if c > 7 else w("WBIG"), c == 0, c == 15)
+        for h in range(2):
+            ts(w("LO", h, 16, 2), w("P%d" % (3 + h), h, 16, 2), w("THR"), O.is_ge, w("TRA", h, h + 1), O.mult)
+        for h in range(2):
+            tt(w("PF", 16 + 8 * h, 24 + 8 * h), w("LO", h, 16, 2), w("PT", h, 16, 2), O.max)
+        t2w(w("PF", 16, 32), 16, "XF")
+        for h in range(2):
+            mm(w("P5", 0, 16), w("XF", 128 * h, 128 * h + 128), SEL[h], h == 0, h == 1)
+        cp(w("FO"), w("P5", 0, 16))
+        if t < 2:
+            cp(ind(w("QT"), w("FO")), w("QN"))
+            cp(ind(w("TC"), w("FO")), w("CNW"))
+        else:
+            cp(ind(w("YT"), w("FO")), w("YN"))
+            dma("d", T.y[:, :], T["YT"][:, 0:1024], "st0", w("YT", 0, 1024)[1], [])
+    schedule()
+    wait("d", "st0", 1)
+    g.wait_ge(T.sem.snd, sent)
+    for q in ("v", "s", "t", "g"):
+        wait("g", q, cnt[q])

@@ -1,26 +1,23 @@
 from concourse.bass import DstId, RemoteDMATransfer
-from concourse.mybir import AluOpType as O, ActivationFunctionType as F
-import math
+from concourse.mybir import AluOpType as O, ActivationFunctionType as F, AxisListType as AX
 
 WAKE, SLACK, BETA = 0.15, 0.03, 1.2
 F32, BF, I32, U16, F16 = "float32", "bfloat16", "int32", "uint16", "float16"
 BUFS = {
-    F32: dict(TD=1280, QT=1280, ONE=160, NEGI=128, ZG=24, WT=24, SHP=128, SHN=128, QW=128, QE=128, DM=136, SW=16, SC=2, TRS=16,
-              TRA=16, WX=8, XI=8, THR=1, XJ=1, RC=1, B1=1, B2=1, MC=160, MR=16, PA=24, TV=1024, TM=1024, DB=64, RF=64,
-              LM=136, LD=16, DF=256, EM=64, EU=64, ET=256, EB=256, EC=256, ED=256, DP=256, DN=256, CH=256, CF32=256, ON=16,
-              OK1=16, SN0=16, QQ=64, K1=64, K2=32, K5=64, K6=64, K7=64, K8=16, FS=16, XF=256, AT=256, AD=256, QA=256,
-              QS=256, QN=256, CV=256, ZF=64, ST=16, S1=160, S2=160, S3=160, S4=80, S5=32, S6=16, S7=16, SN=16, PT=16, M3=16,
-              M4=16, M5=16, NU=16, PW=16, LO=16, YT=1280, YN=256, PR5=1536, SB0=512, SB1=512, SB2=512, IN0=256,
-              IN1=256, IN2=256, PF=32),
-    BF: dict(TC=1280, ham=3584, ONEB=256, G8=8, G16=8, SEL8=8, SELB=8, RW=8, TRI=128, IDB=128, IDN=128, KC=128, KD=136, C128=128,
-             C64=128, BIGL=128, R8=128, WC=128, WBIG=8, ZW=1280, IM=160, SV0=128, SV1=128, SK0=128, SK1=128, SS0=128, SS1=128,
-             QB=1024, LV=64, OL=1024, BS=1088, AB=256, CN=256, hv=4096, MK=4096, F4B=48, R4=128, SG=256, SNB=16, R5=128, OM=64,
-             CFD=256, ABF=256, ABN=256, XB=1024, CMP=2560, FD=32, R6=128, CO=256, CNW=256, SVX0=128, SVX1=128),
-    I32: dict(DET=1024, CI=1024, PI=16, PJ=1, PK=24, PL=24, R32=64, LOW=64, MX=16, E3=16, VV=16, F4=48, H1=32,
-              H2=32, HP=16, HV=16, SGI=16, N1=16, N2=16, N3=16, N4=16, N5=16, N6=16, N7=16, KM2=16, KM1=16, FI=256, I1=32, I2=32,
-              PR=16, OW=16, J1=48, J2=32, JP=16, ZD=64, ZI=160, ZJ=160, HQ=16, ST0=16, PN=16, PM=16, PLC=16, DG=32, SL2=16),
-    F16: dict(OA=1024),
-    U16: dict(GU=16, DU=256, OFF=16, ZU=160, PU=256, PO=16, FO=16),
+    F32: dict(TD=1536, QT=1536, TM=1024, TN=1024, YT=1280, ONE=160, I32=128, I256=128, QW32=128, SHU=16, KW=160, KX=160, SW=16, MR=16,
+              PA=24, RC=1, QB0=1, BN=1, BP=1, THR=1, WX=1, PW3=128, PWT=128, Z128=128, M64=256, MT=256, JC=2, RS8=136, RS16=256,
+              RS4=64, RSK=320, QC=64, HK=32, LM=136, LD=16, DP=256, DN=256, SCN=256, HI=256, CT=256, HV=16, MX=16, VX=16, VD=16, QQ=64,
+              SC2=64, REC=256, ED=256, QS=256, QN=256, AT=256, NA=256, KY=320, PL=16, PW=16, LO=16, YN=256, PR5=1792,
+              SA0=1280, SA1=1280, SA2=1280, SB0=1280, SB1=1280, SB2=1280, IA0=256, IA1=256, IA2=256, IB0=256, IB1=256, IB2=256),
+    BF: dict(TC=1536, ham=3584, ONEB=320, G8=8, G16=8, GM8=8, TRX=128, TRS=128, IDB=128, NEG=128, IBG=128, I2B=128, IQ=128, BLK=128,
+             KC=128, KD=136, DMB=136, C128=128, BL=128, R8=128, QW=128, SHP=128, SHN=128, WT=16, WC=128, WBIG=8, ZG=24, ZW=640,
+             IM=160, SS0=128, SS1=128, SH0=128, SH1=128, RW=16, KA=320, KB=320, KS=64, KZ=160, Z16=16, QB=1024, LV=64, OL=1024,
+             CN=256, hv=4096, MK=4096, XK=272, AE=256, SG=256, SGN=256, RN=256, FB=256, CA=256, OM=64, SGC=256, CFD=256, ABF=256,
+             ABN=256, CMP=2560, RZ=160, CO=256, CNW=256),
+    I32: dict(DET=1024, CI=1024, PI=16, PJ=1, PK=24, PLI=24, EI=4, EJ=4, EK=4, XI=16, R32=64, LOW=64, E3=16, VV=16, H1=32, H2=32,
+              HP=16, I1=32, I2=32, PR=16, OW=16, HS=32),
+    F16: dict(OA=1024, DF=256, VB=256, CH=256, XF=256, T16=32, R4=128, XB=512, RK=16, PL16=16, R6=128, PU=256),
+    U16: dict(GU=16, DU=256, OFF=16, ZU=160, PO=16, FO=16, OC=16, OL4=16, OQ=4, OW4=4),
 }
 SCRATCH, WIDTH, WHERE = {}, {}, {}
 for _d in BUFS:
@@ -35,12 +32,18 @@ for _d in BUFS:
             SCRATCH[_n] = ("sbuf", [128, _w], _d)
     if _p:
         SCRATCH["small_" + _d] = ("sbuf", [128, _p], _d)
+SCRATCH["BS"] = ("sbuf", [128, 8, 17, 8], BF)
 TWO = list(BUFS[F16]) + list(BUFS[BF]) + list(BUFS[U16])
-PSUM = ["P%d" % _k for _k in range(7)] + ["TP"]
+PSUM = ["P%d" % _k for _k in range(8)]
 for _n in PSUM:
-    WIDTH[_n] = 128 if _n == "TP" else 512
-    SCRATCH[_n] = ("psum", [128, WIDTH[_n]], BF if _n == "TP" else F32)
-SEMAPHORES = ["qv", "qs", "qt", "qg", "ld0", "ld1", "st0", "snd", "rx0", "rx1", "rx2"]
+    WIDTH[_n] = 512
+    SCRATCH[_n] = ("psum", [128, 512], F32)
+SEMAPHORES = ["qv", "qs", "qt", "qg", "ld0", "ld1", "ld2", "ld3", "ld4", "st0", "st1", "snd", "ra0", "ra1", "ra2", "rb0", "rb1", "rb2"]
+W1 = [13 * _i + 5 for _i in range(16)]
+W2 = [255 - 14 * _i for _i in range(16)]
+MID = 1792
+VOID = min(_c for _c in range(3584)
+           if all((((sum(W1) * _c) % 4096 * ((sum(W2) * _c) % 4096) >> 5) + _t) % 4096 >= 3584 for _t in range(3)))
 
 
 def rank_program(g, core, T, topo):
@@ -64,6 +67,11 @@ def rank_program(g, core, T, topo):
             for c in range(a, b, st):
                 m |= 1 << c
         return (ap, [(name, m)], [])
+
+    def bs(k=None, h=None):
+        if h is None:
+            return (T["BS"][:, k, :, :], [("BS", ((1 << 136) - 1) << (136 * k))], [])
+        return (T["BS"][:, :, h, :], [("BS", sum(255 << (136 * j + 8 * h) for j in range(8)))], [])
 
     def ind(win, off):
         return (win[0].indirect(off[0]), win[1], off[1], 16 * off[1][0][1].bit_count())
@@ -127,14 +135,14 @@ def rank_program(g, core, T, topo):
         reads = [r for x in ins for r in x[1] + x[2]] + [r for x in outs for r in x[2]]
         calls.append((q, emit, reads, [r for x in outs for r in x[1]], cost, 0.0))
 
-    def dma(q, out, in_, sem, reads, writes):
+    def dma(q, out, in_, sem, reads, writes, lat):
         def emit(reads, writes):
             deps(q, reads, writes)
             ENG[q].dma_start(out=out, in_=in_).then_inc(T.sem[sem], 16)
             semof[sem] = (sem, 16)
             clk[(sem, 1)] = dict(known[q])
             note(sem, 1, reads, writes)
-        calls.append((q, emit, reads, writes, 0.1, 5.0))
+        calls.append((q, emit, reads, writes, 0.1, lat))
 
     def schedule():
         n = len(calls)
@@ -171,6 +179,8 @@ def rank_program(g, core, T, topo):
         way = [0.0] * n
         for j in range(n - 1, -1, -1):
             way[j] = calls[j][4] + calls[j][5] + max([wk + way[k] for k, wk in succ[j]] + [0.0])
+        for j in range(5):
+            way[j] = 1e6 - j
         free, est, order, avail = {}, [0.0] * n, [], {}
         for j in range(n):
             if not npred[j]:
@@ -208,12 +218,14 @@ def rank_program(g, core, T, topo):
     def ap(x):
         return x[0] if isinstance(x, tuple) else x
 
+    CY = 0.0009
+
     def vcost(o, a, k=1.0):
         if len(a) > 3:
-            return 0.06 + a[3] * 0.0016
+            return 0.06 + a[3] * 1.56 * CY
         if len(o) > 3:
-            return 0.06 + o[3] * 0.0035
-        return max(64, wide(a) * k) * 0.00104
+            return 0.06 + o[3] * 3.8 * CY
+        return max(64, wide(a) * k) * CY
 
     def tt(o, a, b, op):
         k = 1.0 if any(x[1][0][0] in PSUM for x in (a, b)) else 2.0
@@ -225,7 +237,15 @@ def rank_program(g, core, T, topo):
         E("v", lambda: V.tensor_scalar(out=o[0], in0=a[0], scalar1=ap(s1), op0=op0, **kw), [a] + col(s1) + col(s2), [o], vcost(o, a, k))
 
     def cp(o, a):
-        E("v", lambda: V.tensor_copy(out=o[0], in_=a[0]), [a], [o], vcost(o, a))
+        k = 0.5 if a[1][0][0] in TWO and o[1][0][0] in TWO else 1.0
+        E("v", lambda: V.tensor_copy(out=o[0], in_=a[0]), [a], [o], vcost(o, a, k))
+
+    def scan(o, d0, d1, init, op0, op1):
+        E("v", lambda: V.tensor_tensor_scan(out=o[0], data0=d0[0], data1=d1[0], initial=init, op0=op0, op1=op1), [d0, d1], [o],
+          vcost(o, d1))
+
+    def total(o, a):
+        E("v", lambda: V.tensor_reduce(out=o[0], in_=a[0], axis=AX.X, op=O.add), [a], [o], vcost(o, a))
 
     def fill(o, c):
         E("v", lambda: V.memset(o[0], c), [], [o], vcost(o, o))
@@ -236,158 +256,204 @@ def rank_program(g, core, T, topo):
 
     def mm(o, l, r, start=True, stop=True):
         k = 4 if l[1][0][0] in BUFS[F32] else 1
-        E("t", lambda: PE.matmul(out=o[0], lhsT=l[0], rhs=r[0], start=start, stop=stop), [l, r], [o], max(64, wide(r)) * k * 0.00104)
+        E("t", lambda: PE.matmul(out=o[0], lhsT=l[0], rhs=r[0], start=start, stop=stop), [l, r], [o],
+          max(min(64, wide(l)), wide(r)) * k * CY)
 
-    def tr(o, a):
-        E("t", lambda: PE.transpose(out=o[0], in_=a[0], identity=w("IDB")[0]), [a, w("IDB")], [o], 0.13)
+    def group(parts):
+        for i, (o, l, r) in enumerate(parts):
+            mm(o, l, r, i == 0, i == len(parts) - 1)
 
     def iota(o, pat, base, cm):
         E("g", lambda: g.iota(o[0], pattern=pat, base=base, channel_multiplier=cm, allow_small_or_imprecise_dtypes=True), [], [o],
-          0.15 + 0.002 * wide(o))
+          0.13 + 2 * CY * wide(o))
 
-    def aff(o, a, pat, op, base, cm):
-        E("g", lambda: g.affine_select(out=o[0], in_=a[0], pattern=pat, compare_op=op, fill=0.0, base=base, channel_multiplier=cm),
-          [a], [o], 0.2 + 0.002 * wide(o))
+    def aff(o, a, pat, op, base, cm, other=0.0):
+        E("g", lambda: g.affine_select(out=o[0], in_=a[0], pattern=pat, compare_op=op, fill=other, base=base, channel_multiplier=cm),
+          [a], [o], 0.17 + 2 * CY * wide(o))
 
-    ALL = (1 << 1024) - 1
-    dma("d", T["DET"][:, :], T.det[:, :], "ld0", [], [("DET", ALL)])
-    dma("d", T["hamt"][:, :], T.ham[:, :], "ld1", [("DET", ALL)], [("hamt", (1 << 3584) - 1)])
+    def scatter(win, off, data, parts=1):
+        n = 16 // parts
+        for i in range(parts):
+            cp(ind(w(win), w(off, n * i, n * i + n)), w(data, 16 * n * i, 16 * n * (i + 1)))
 
+    for c in range(4):
+        x = w("DET", 256 * c, 256 * c + 256)
+        dma("d", x[0], T.det[:, 256 * c:256 * c + 256], "ld%d" % c, [], x[1], 2.5 + 0.6 * c)
+    dma("d", T["hamt"][:, :], T.ham[:, :], "ld4", w("DET", 768, 1024)[1], w("hamt")[1], 6.0)
+
+    BIG, KB, Y0, MAG = 8192.0, 16384.0, 16640.0, 12582912.0
+    YCAP = Y0 + 256 * 20
     fill(w("ONEB"), 1.0)
     fill(w("ONE"), 1.0)
-    fill(w("NEGI"), -1.0)
-    fill(w("QE"), 4096.0)
-    fill(w("C64"), 64.0)
-    iota(w("PI"), [[-1, 16]], 16, 1)
+    fill(w("C128"), 1 / 128)
+    fill(w("DMB"), 0.0)
     iota(w("PJ"), [[0, 1]], 0, 1)
     aff(w("G8"), w("ONEB", 0, 8), [[-16, 8]], O.is_ge, 0, 1)
     aff(w("G8"), w("G8"), [[16, 8]], O.is_ge, 15, -1)
+    aff(w("IDB"), w("ONEB", 0, 128), [[-1, 128]], O.is_equal, 0, 1)
+    aff(w("TRS"), w("ONEB", 0, 128), [[1, 128]], O.is_ge, -1, -1)
     for t in range(3):
         iota(w("PK", 8 * t, 8 * t + 8), [[128, 8]], 310 * (t + 1), 1)
-    aff(w("TRI"), w("ONEB", 0, 128), [[1, 128]], O.is_ge, -1, -1)
-    iota(w("SW"), [[16, 16]], 1024, 0)
-    iota(w("KD"), [[0, 8], [-2048, 17]], 0, 0)
-    aff(w("DM"), w("ONE", 0, 136), [[-16, 8], [0, 17]], O.is_ge, 0, 1)
-    aff(w("DM"), w("DM"), [[16, 8], [0, 17]], O.is_ge, 15, -1)
-    aff(w("IDB"), w("ONEB", 0, 128), [[-1, 128]], O.is_equal, 0, 1)
-    aff(w("QE"), w("QE"), [[-16, 8], [-2, 16]], O.is_equal, 0, 1)
-    aff(w("QW"), w("ONE", 0, 128), [[-16, 8], [-2, 16]], O.is_equal, -1, 1)
-    tt(w("QW"), w("QW"), w("QE"), O.add)
-    aff(w("QW"), w("QW"), [[0, 8], [-1, 16]], O.is_ge, 7, 0)
-    aff(w("SHP"), w("ONE", 0, 128), [[1, 128]], O.is_equal, -1, -1)
-    aff(w("SHN"), w("ONE", 0, 128), [[1, 128]], O.is_equal, 1, -1)
-    iota(w("KC"), [[-1, 16], [0, 8]], 15, 0)
-    iota(w("SC"), [[128, 2]], 0, 1)
-    iota(w("WT", 0, 8), [[-208, 8]], 5, 13)
-    iota(w("WT", 8, 16), [[224, 8]], 255, -14)
-    aff(w("WT", 0, 16), w("WT", 0, 16), [[0, 2], [-16, 8]], O.is_ge, 0, 1)
-    aff(w("WT", 0, 16), w("WT", 0, 16), [[0, 2], [16, 8]], O.is_ge, 15, -1)
-    aff(w("WT", 16, 24), w("ONE", 0, 8), [[-16, 8]], O.is_equal, -15, 1)
-    ts(w("PL"), w("PK"), 1023, O.bitwise_and)
-    ts(w("PA"), w("PL"), -2048.0, O.add, 0.5, O.mult)
+    iota(w("PI"), [[-1, 16]], 16, 1)
+    iota(w("KD"), [[-2048, 17], [0, 8]], 0, 0)
+    aff(w("DMB"), w("DMB"), [[0, 17], [-16, 8]], O.is_ge, 0, 1, 262144.0)
+    aff(w("DMB"), w("DMB"), [[0, 17], [16, 8]], O.is_ge, 15, -1, 262144.0)
+    iota(w("SW"), [[16, 16]], 1280, 0)
+    iota(w("XI"), [[1, 16]], 0, 0)
+    iota(w("JC"), [[128, 2]], 1024, 1)
+    ts(w("NEG"), w("IDB"), -4096.0, O.mult)
+    tt(w("TRX"), w("TRS"), w("NEG"), O.add)
+    cp(w("TRS"), w("TRX"))
+    ts(w("NEG"), w("IDB"), -1.0, O.mult)
+    ts(w("PLI"), w("PK"), 1023, O.bitwise_and)
+    ts(w("PA"), w("PLI"), -2048.0, O.add, 0.5, O.mult)
     ts(w("PI"), w("PI"), 15, O.bitwise_and)
     ts(w("MR"), w("PI"), 0.0, O.is_equal)
     ts(w("PJ"), w("PJ"), 15, O.bitwise_and)
     cp(w("RC"), w("PJ"))
     ts(w("SW"), w("SW"), w("RC"), O.add)
-    aff(w("NEGI"), w("NEGI"), [[-1, 128]], O.is_equal, 0, 1)
+    fill(w("RS8"), 0.0)
+    fill(w("RS8", 0, 136, 8), 1048576.0)
+    fill(w("TC", 1024, 1536), 0.0)
+    fill(w("TD", 1024, 1536), float(VOID))
+    aff(w("SHP"), w("ONEB", 0, 128), [[1, 128]], O.is_equal, -1, -1)
+    aff(w("SHN"), w("ONEB", 0, 128), [[1, 128]], O.is_equal, 1, -1)
+    iota(w("WT", 0, 8), [[-208, 8]], 5, 13)
+    iota(w("WT", 8, 16), [[224, 8]], 255, -14)
+    aff(w("WT"), w("WT"), [[0, 2], [-16, 8]], O.is_ge, 0, 1)
+    aff(w("WT"), w("WT"), [[0, 2], [16, 8]], O.is_ge, 15, -1)
+    iota(w("KC"), [[0, 8], [-1, 16]], 15, 0)
+    fill(w("QW32"), 4096.0)
+    aff(w("QW32"), w("QW32"), [[-16, 8], [-2, 16]], O.is_equal, 0, 1)
+    aff(w("I32"), w("ONE", 0, 128), [[-16, 8], [-2, 16]], O.is_equal, -1, 1)
+    tt(w("QW32"), w("QW32"), w("I32"), O.add)
+    aff(w("QW32"), w("QW32"), [[0, 8], [-1, 16]], O.is_ge, 7, 0)
+    cp(w("QW"), w("QW32"))
+    iota(w("QC"), [[0, 16], [1, 4]], 128, 0)
+    iota(w("KS"), [[0, 16], [256, 4]], 4096, 0)
+    iota(w("EI"), [[16, 4]], 0, 0)
     for h in range(2):
-        aff(w("SV%d" % h), w("C64"), [[-2, 8], [0, 16]], O.is_equal, -h, 1)
-        aff(w("SK%d" % h), w("ONEB", 0, 128), [[-2, 8], [0, 16]], O.is_equal, -32 - h, 1)
-        aff(w("SS%d" % h), w("ONEB", 0, 128), [[-2, 8], [0, 16]], O.is_equal, -h, 1)
+        aff(w("SH%d" % h), w("ONEB", 0, 128), [[-2, 8], [-16, 16]], O.is_equal, 144 - h, 1)
+    fill(w("SHP", 0, 128, 16), 0.0)
+    fill(w("SHN", 15, 128, 16), 0.0)
+    fill(w("BL"), -BIG / 128)
+    fill(w("BL", 0, 128, 16), -BIG / 64)
+    fill(w("RS16"), 1.0)
+    fill(w("RS16", 0, 256, 16), 0.0)
+    fill(w("RS4"), 0.0)
+    fill(w("RS4", 0, 64, 4), 1048576.0)
+    fill(w("XK", 0, 16), 1.0)
+    fill(w("HK", 0, 16), float(MID * sum(W1)))
+    fill(w("HK", 16, 32), float(MID * sum(W2)))
+    fill(w("ZG"), 0.0)
+    cp(w("ZG", 8, 16), w("G8"))
+    SEL = [w("ZG", 8, 24), w("ZG", 0, 16)]
+    ts(w("G16"), w("G8"), 16.0 * 37, O.mult)
+    ts(w("GM8"), w("G8"), -8.0, O.mult)
+    ts(w("IBG"), w("IDB"), BIG, O.mult)
+    ts(w("I2B"), w("IDB"), 256.0, O.mult)
+    ts(w("IQ"), w("IDB"), 1 / 256, O.mult)
+    cp(w("I32"), w("IDB"))
+    ts(w("I256"), w("IDB"), 256.0, O.mult)
+    ts(w("BN"), w("RC"), 15.0, O.is_equal, BIG, O.mult)
+    ts(w("BP"), w("RC"), 0.0, O.is_equal, -BIG, O.mult)
+    ts(w("QB0"), w("RC"), 8.0, O.is_lt, 4097.0 * MID, O.mult)
+    fill(w("R8"), 0.0)
+    cp(w("R8", 8, 128, 16), w("G8"))
+    for r in range(16):
+        ts(w("BLK", r, 128, 16), w("G8"), -256.0, O.mult)
+    cp(w("OC"), w("XI"))
+    ts(w("OL4"), w("XI"), 4.0, O.mult, 3.0, O.add)
+    ts(w("EI"), w("EI"), w("RC"), O.add)
+    ts(w("EI"), w("EI"), 2, O.arith_shift_right)
+    cp(w("OQ"), w("EI"))
+    ts(w("EJ"), w("EI"), 7, O.bitwise_and)
+    ts(w("EK"), w("EI"), 3, O.arith_shift_right)
+    ts(w("EJ"), w("EJ"), 2.0, O.mult)
+    tt(w("OW4"), w("EJ"), w("EK"), O.add)
+    ts(w("M64", 0, 16), w("MR"), 64.0, O.mult)
+    for n in (16, 32, 64, 128):
+        cp(w("M64", n, 2 * n), w("M64", 0, n))
+    for h in range(2):
+        ts(w("MT", 128 * h, 128 * h + 128), w("M64", 0, 128), w("JC", h, h + 1), O.mult, 1 / 64, O.mult)
+    for t in range(3):
+        for q in range(4):
+            fill(w("SA%d" % t, 256 * q, 256 * q + 64), -1.0)
+            fill(w("SB%d" % t, 256 * q, 256 * q + 64), 0.0)
+    aff(w("SHU"), w("ONE", 0, 16), [[-1, 2], [-16, 8]], O.is_equal, -9, 1)
+    iota(w("IM"), [[1, 10], [0, 16]], 0, 0)
+    for h in range(2):
+        z = w("ZW", 320 * h, 320 * h + 160)
+        aff(z, w("ONEB", 0, 160), [[0, 10], [-16, 16]], O.is_ge, 128 * h, 1)
+        aff(z, z, [[0, 10], [16, 16]], O.is_ge, 15 - 128 * h, -1)
+        tt(w("ZW", 320 * h + 160, 320 * h + 320), z, w("IM"), O.mult)
+        aff(w("SS%d" % h), w("ONEB", 0, 128), [[-1, 8], [0, 16]], O.is_equal, -8 * h, 1)
+        ts(w("SS%d" % h), w("SS%d" % h), 64.0, O.mult)
+    fill(w("KZ"), 196608.0)
+    fill(w("Z16"), 0.0)
+    iota(w("KX"), [[0, 16], [1, 10]], 0, 0)
+    aff(w("KX"), w("KX"), [[-16, 8], [0, 20]], O.is_equal, -10, 1)
+    aff(w("KW"), w("ONE"), [[-16, 8], [0, 20]], O.is_equal, -9, 1)
+    tt(w("KW"), w("KW"), w("KX"), O.add)
+    ts(w("KW"), w("KW"), 1 / 64, O.mult)
+    iota(w("KA"), [[0, 16], [256, 20]], int(Y0), 0)
+    iota(w("KB"), [[0, 16], [-7, 2], [0, 10]], 8, 0)
+    ts(w("KB"), w("KB"), KB, O.mult)
+    ts(w("RW", 1, 16, 2), w("R8", 8, 128, 16), w("MR", 8, 9), O.mult, -KB, O.mult)
+    ts(w("WX"), w("RC"), 8.0, O.is_lt, -KB, O.mult)
+    ts(w("RW", 0, 16, 2), w("G8"), w("WX"), O.mult)
+    tt(w("RW", 0, 16, 2), w("RW", 0, 16, 2), w("RW", 1, 16, 2), O.subtract)
+    fill(w("RSK"), 0.0)
+    for h in range(2):
+        ts(w("RSK", 160 * h, 160 * h + 160, 20), w("ONE", 0, 8), w("JC", h, h + 1), O.mult, 1 / 64, O.mult)
+    ts(w("RSK", 0, 320, 20), w("RSK", 0, 320, 20), YCAP, O.add)
+    fill(w("PWT"), 1 / 3)
+    fill(w("Z128"), 0.0)
+    scan(w("PW3"), w("PWT"), w("Z128"), 3.0 ** 56, O.mult, O.add)
+    tt(w("PWT"), w("PW3"), w("I32"), O.mult)
+    total(w("THR"), w("PWT"))
+    ts(w("THR"), w("THR"), 2.2, O.mult)
+    tt(w("PWT", 0, 16), w("PW3", 48, 64), w("MR"), O.mult)
+    total(w("WX"), w("PWT", 0, 16))
+    for c in range(8):
+        ts(w("WC", 8 * c, 8 * c + 8), w("G8"), w("WX"), O.mult, 3.0 ** (48 - 16 * c), O.mult)
+    ts(w("WBIG"), w("G8"), 1e29, O.mult)
 
-    MAG = 12582912.0
     START = [310 * (t + 1) & 1023 for t in range(3)]
 
     def rot(t, a, b):
-        s, cut = START[t], 1024 - START[t]
-        out = []
-        if a < cut:
-            out.append((a, min(b, cut), a + s))
-        if b > cut:
-            out.append((max(a, cut), b, max(a, cut) - cut))
+        s, out = START[t], []
+        if a < s:
+            out.append((a, min(b, s), a - s + 1024))
+        if b > s:
+            out.append((max(a, s), b, max(a, s) - s))
         return out
 
-    for c in (0, 512):
-        ts(w("CI", c, c + 512), w("DET", c, c + 512), 255, O.bitwise_and)
-        ts(w("TC", c, c + 512), w("CI", c, c + 512), -128.0, O.add)
-    for a, b in ((0, 202), (202, 714), (714, 1024)):
-        for x, y, p in rot(0, a, b):
-            act(w("QB", x, y), w("TC", p, p + y - x), F.Abs)
-    for c in (0, 512):
-        ts(w("TV", c, c + 512), w("DET", c, c + 512), -128.0, O.add, 1 / 256, O.mult)
-        act(w("TM", c, c + 512), w("TV", c, c + 512), F.Identity, MAG)
-        act(w("TD", c, c + 512), w("TM", c, c + 512), F.Identity, -MAG)
-    fill(w("SHP", 0, 128, 16), 0.0)
-    fill(w("SHN", 15, 128, 16), 0.0)
-    fill(w("BIGL"), 0.0)
-    fill(w("BIGL", 15, 128, 16), 64.0)
-    fill(w("C128"), 1 / 128)
-    fill(w("TC", 1024, 1280), 0.0)
-    fill(w("TD", 1024, 1280), 0.0)
-    fill(w("ZG"), 0.0)
-    cp(w("ZG", 8, 16), w("G8"))
-    ts(w("G16"), w("G8"), 16.0 * 37, O.mult)
-    SEL = [w("ZG", 8, 24), w("ZG", 0, 16)]
+    for c in range(0, 1024, 256):
+        ts(w("CI", c, c + 256), w("DET", c, c + 256), 255, O.bitwise_and)
+        ts(w("TC", c, c + 256), w("CI", c, c + 256), -128.0, O.add)
+        for x, y, p in rot(0, c, c + 256):
+            act(w("QB", p, p + y - x), w("TC", x, y), F.Abs)
+    for c in range(0, 1024, 256):
+        ts(w("TD", c, c + 256), w("DET", c, c + 256), -128.0, O.add, 1 / 256, O.mult)
 
-    for h in range(2):
-        aff(w("SVX%d" % h), w("ONEB", 0, 128), [[-2, 8], [0, 16]], O.is_equal, -16 - h, 1)
-    iota(w("TRS"), [[0, 8], [128, 2]], 256, 1)
-    iota(w("TRA"), [[0, 8], [128, 2]], 1024, 1)
-    iota(w("MC"), [[1, 10], [0, 16]], 2048, 0)
-    iota(w("IM"), [[1, 10], [0, 16]], 0, 0)
-    iota(w("XI"), [[16, 8]], 0, 0)
-    iota(w("XJ"), [[0, 1]], 0, 1)
-    aff(w("SEL8"), w("ONEB", 0, 8), [[-16, 8]], O.is_equal, -8, 1)
-    aff(w("RW"), w("G8"), [[16, 8]], O.is_ge, 7, -1)
-    for h in range(2):
-        z = w("ZW", 640 * h + 160, 640 * h + 320)
-        aff(z, w("ONEB", 0, 160), [[0, 10], [-16, 16]], O.is_ge, 128 * h, 1)
-        aff(z, z, [[0, 10], [16, 16]], O.is_ge, 15 - 128 * h, -1)
+    def whole(c, scale):
+        act(w("TM", c, c + 256), w("TD", c, c + 256), F.Identity, MAG)
+        act(w("TN", c, c + 256), w("TM", c, c + 256), F.Identity, -MAG * scale, scale)
 
-    def late_constants():
-        for h in range(2):
-            tt(w("SV%d" % h), w("SV%d" % h), w("SVX%d" % h), O.add)
-        fill(w("R8"), 0.0)
-        cp(w("R8", 8, 128, 16), w("G8"))
-        ts(w("B1"), w("RC"), -8192.0, O.mult, 8192.0 * 15 + 4096, O.add)
-        ts(w("B2"), w("RC"), 8192.0, O.mult, 4096 - 8192.0 * 15, O.add)
-        for t in range(3):
-            fill(w("SB%d" % t, 0, 256), 0.0)
-
-    def last_constants():
-        ts(w("SELB"), w("SEL8"), 16.0, O.mult)
-        tt(w("RW"), w("RW"), w("SELB"), O.add)
-        for h in range(2):
-            z = [w("ZW", 640 * h + 160 * f, 640 * h + 160 * f + 160) for f in range(4)]
-            ts(z[0], z[1], 32.0, O.mult)
-            tt(z[3], z[1], w("IM"), O.mult)
-            ts(z[2], z[3], 32.0, O.mult)
-        ts(w("XI"), w("XI"), w("RC"), O.add)
-        L3 = math.log(3.0)
-        ts(w("XI"), w("XI"), -L3, O.mult, 55 * L3, O.add)
-        ts(w("XJ"), w("XJ"), -L3, O.mult, 55 * L3, O.add)
-        act(w("WX"), w("XI"), F.Exp)
-        act(w("THR"), w("XJ"), F.Exp)
-        ts(w("THR"), w("THR"), 2.2, O.mult)
-        for c in range(8):
-            ts(w("WC", 8 * c, 8 * c + 8), w("G8"), w("WX", c, c + 1), O.mult)
-        ts(w("WBIG"), w("G8"), 1e29, O.mult)
-        ts(w("IDN"), w("IDB"), -1 / 256, O.mult)
-
-    def t2w(src, n, X):
-        for r in range(16):
-            if r % 2:
-                act(w(X, r, 16 * n, 16), src, F.Copy, 0.0, w("MR", r, r + 1))
-            else:
-                ts(w(X, r, 16 * n, 16), src, w("MR", r, r + 1), O.mult)
+    def first_qt(c):
+        whole(c, 1.0)
+        parts = [(w("P7", 0, 256), w("QW32"), w("TN", c, c + 256))]
+        parts += [(w("P7", x - c, y - c), w("R8"), w("QB", p, p + y - x)) for x, y, p in rot(0, c, c + 256)]
+        group(parts)
+        act(w("QT", c, c + 256), w("P7", 0, 256))
 
     peers = [q for q in range(4) if q != me]
     near = [q for q in peers if T.cores[q] in topo.cores_of(core)]
     far = [q for q in peers if q not in near]
 
-    def send(t):
-        sb, plan, used, share = "SB%d" % t, [], [], []
+    def send(sb, dst, rx):
+        plan, used, share = [], [], []
         for i, q in enumerate(far):
             e = topo.engines(core, T.cores[q])
             k = len(e) // len(far)
@@ -399,7 +465,6 @@ def rank_program(g, core, T, topo):
             k = min([len(e) // len(near)] + share)
             plan.append((q, e[i * k:(i + 1) * k]))
         got = sum(len(e) for q, e in plan)
-        rx = "rx%d" % t
 
         def emit(reads, writes):
             deps("g", reads, [])
@@ -407,338 +472,242 @@ def rank_program(g, core, T, topo):
             for q, e in plan:
                 rid, pid = topo.addr(T.cores[q], core)
                 tf.append(RemoteDMATransfer(dst_ids=[DstId(rid=rid, pnc=pid)], dma_engine_mask=sum(1 << x for x in e),
-                                            remote_sem=T.sem[rx], src=T[sb][:, 64 * q:64 * q + 64],
-                                            dst=T["IN%d" % t][:, 64 * me:64 * me + 64], alu_op=0))
+                                            remote_sem=T.sem[rx], src=T[sb][:, 256 * q:256 * q + 64],
+                                            dst=T[dst][:, 64 * me:64 * me + 64], alu_op=0))
             g.remote_dma_fused(tf, local_sem=T.sem["snd"])
             semof[rx] = (rx, got)
             note(rx, 1, [], writes)
-        calls.append(("g", emit, w(sb, 0, 256)[1], [r for q in peers for r in w("IN%d" % t, 64 * q, 64 * q + 64)[1]], 0.5, 4.0))
-        act(w("IN%d" % t, 64 * me, 64 * me + 64), w(sb, 64 * me, 64 * me + 64))
+        calls.append(("g", emit, w(sb)[1], [r for q in peers for r in w(dst, 64 * q, 64 * q + 64)[1]], 0.5, 3.5))
+        act(w(dst, 64 * me, 64 * me + 64), w(sb, 256 * me, 256 * me + 64))
         return got
 
-    def first_qt(b):
-        mm(w("P6", 0, 512), w("QW"), w("TD", 512 * b, 512 * b + 512), True, False)
-        parts = [(0, 310, 714), (310, 512, 0)] if b == 0 else [(0, 512, 202)]
-        for i, (x, y, p) in enumerate(parts):
-            mm(w("P6", x, y), w("R8"), w("QB", p, p + y - x), False, i == len(parts) - 1)
-        act(w("QT", 512 * b, 512 * b + 512), w("P6", 0, 512))
+    def wrap(p):
+        group([(w(p, 0, 16), w("XF", 128 * h, 128 * h + 128), SEL[h]) for h in range(2)])
 
+    def half(n, h, p=128):
+        return w(n, 128 * h, 128 * h + 128, 1, p)
+
+    A = lambda n: w(n, 0, 256)
     sent = 0
     for t in range(3):
-        IN, SB = "IN%d" % t, "SB%d" % t
+        IA, IB = "IA%d" % t, "IB%d" % t
         if t:
-            for a in range(0, 1024, 256):
-                for x, y, p in rot(t, a, a + 256):
-                    act(w("QB", x, y), w("QT", p, p + y - x))
+            for a, b, onv in ((0, 384, 0), (384, 704, 1), (704, 1024, 1)):
+                for x, y, p in rot(t, a, b):
+                    if onv:
+                        ts(w("QB", p, p + y - x), w("TC", x, y), 0.0, O.not_equal)
+                    else:
+                        act(w("QB", p, p + y - x), w("TC", x, y), F.Abs)
         for k in range(8):
-            mm(w("P0", 8 * k, 8 * k + 8), w("QB", 128 * k, 128 * k + 128), w("SEL8") if t else w("G8"))
+            mm(w("P0", 8 * k, 8 * k + 8), w("QB", 128 * k, 128 * k + 128), w("G8"))
         ts(w("LV"), w("P0", 0, 64), 0.0, O.is_gt)
-        ts(w("DB"), w("P0", 0, 64), 0.0, O.is_equal, 4096.0, O.mult)
-        mm(w("P1", 0, 64), w("TRI"), w("LV"), True, False)
-        for d in range(1, 8):
-            mm(w("P1", 8 * d, 64), w("ONEB", 0, 128), w("LV", 0, 64 - 8 * d), False, d == 7)
-        tt(w("RF"), w("P1", 0, 64), w("DB"), O.add)
-        tt(w("R32"), w("P1", 0, 64), w("DB"), O.add)
+        group([(w("P1", 0, 64), w("TRX"), w("LV"))] + [(w("P1", 8 * d, 64), w("ONEB", 0, 128), w("LV", 0, 64 - 8 * d)) for d in range(1, 8)])
+        cp(w("R32"), w("P1", 0, 64))
         ts(w("LOW"), w("R32"), 15, O.bitwise_and)
         for h in range(17):
-            act(w("BS", h, 1088, 17), w("RF"), F.Sign, 0.5 - 16 * h)
-        if t == 0:
-            late_constants()
+            act(bs(h=h), w("P1", 0, 64), F.Sign, 4096.5 - 16 * h)
         for l in range(16):
             ts(w("OL", l, 1024, 16), w("LOW"), float(l), O.is_equal)
         for k in range(8):
             c = (128 * k, 128 * k + 128)
             ts(w("OA", *c), w("OL", *c), w("PA", 8 * t + k, 8 * t + k + 1), O.mult)
-        mm(w("P2", 0, 136), w("C128"), w("KD"), True, False)
-        for k in range(8):
-            mm(w("P2", 0, 136), w("OA", 128 * k, 128 * k + 128), w("BS", 136 * k, 136 * k + 136), False, k == 7)
-        for k in range(8):
-            mm(w("P0", 0, 8), w("ONEB", 0, 128), w("LV", 8 * k, 8 * k + 8), k == 0, k == 7)
+        group([(w("P2", 0, 136), w("C128"), w("KD")), (w("P2", 0, 136), w("IDB"), w("DMB"))]
+              + [(w("P2", 0, 136), w("OA", 128 * k, 128 * k + 128), bs(k=k)) for k in range(8)])
         if t:
-            cp(ind(w("TD"), w("FO")), w("AD"))
-        tt(w("LM"), w("P2", 0, 136), w("DM"), O.mult)
-        for n in (68, 34, 17):
-            tt(w("LM", 0, n), w("LM", 0, n), w("LM", n, 2 * n), O.add)
-        tt(w("LD"), w("LM", 0, 16), w("LM", 1, 17), O.subtract)
+            scatter("TD", "FO", "IB%d" % (t - 1), 2)
+        scan(w("LM"), w("RS8"), w("P2", 0, 136), 0.0, O.add, O.min)
+        tt(w("LD"), w("LM", 7, 128, 8), w("LM", 15, 136, 8), O.subtract)
         tt(w("GU"), w("LD"), w("SW"), O.min)
-        act(w("AB"), ind(w("TC"), w("GU")), F.Abs)
-        mm(w("P3", 0, 256), w("IDB"), w("AB"))
         cp(w("DU"), ind(w("TD"), w("GU")))
-        CUT = [0, 64, 128, 192, 256]
+        act(w("CN"), ind(w("TC"), w("GU")))
+        act(A("P3"), w("CN"), F.Abs)
+        CUT = [0, 48, 128, 192, 256]
 
         def look(a, b):
             return w("hv", 16 * a, 16 * b), ind(w("hamt"), w("DU", a, b))
         for j in range(1, 4):
             act(*look(CUT[j], CUT[j + 1]))
-        act(w("CN"), ind(w("TC"), w("GU")))
-        cp(w("DF"), w("DU"))
         cp(*look(CUT[0], CUT[1]))
+        ts(w("DF"), w("DU"), -float(MID), O.add)
         for h in range(2):
-            mm(w("P0", 64 + h, 96, 2), w("DF", 128 * h, 128 * h + 128), w("WT", 0, 16))
-
-        def mins(a, b):
-            for k in list(range(8, 16)) + list(range(8)):
-                tt(w("MK", 256 * k + a, 256 * k + b), w("hv", 16 * a + k, 16 * b, 16), w("P3", a, b), O.min)
-
-        UP = ["P1", "P6"]
-
-        def tree(h):
-            for p, ks in ((UP[h], range(8, 16)), ("P%d" % (1 + h), range(8))):
-                mm(w(p, 8 * ks[0], 8 * ks[0] + 64), w("C128"), w("KC", 8 * ks[0], 8 * ks[0] + 64), True, False)
-                for k in ks:
-                    mm(w(p, 8 * k, 8 * k + 8), w("MK", 256 * k + 128 * h, 256 * k + 128 * h + 128), w("G16"), False, k == ks[-1])
-            cp(w("EM" if h else "EU"), w(UP[h], 64, 128))
-
-        def top(h):
-            p, o = "P%d" % (1 + h), 128 * h
-            tt(w("ET", o, o + 64), w(p, 0, 64), w("EM" if h else "EU"), O.max)
-            for n in (32, 16):
-                tt(w("ET", o, o + n), w("ET", o, o + n), w("ET", o + n, o + 2 * n), O.max)
-            tt(w("MX", h, 16, 2), w("ET", o, o + 8), w("ET", o + 8, o + 16), O.max)
+            mm(w("P0", h, 32, 2), half("DF", h), w("WT"))
         mm(w("P4", 0, 256), w("SHP"), w("DF"))
-        mm(w("P4", 256, 512), w("SHN"), w("DF"), True, False)
-        mm(w("P4", 256, 512), w("BIGL"), w("ONEB"), False, True)
-        mm(w("P5", 0, 256), w("NEGI"), w("DF"), True, False)
-        act(w("DP"), w("P4", 0, 256))
-        act(w("DN"), w("P4", 256, 512))
-        if t == 0:
-            first_qt(0)
-        mins(0, CUT[2])
-        tree(0)
-        mins(CUT[2], CUT[3])
-        for h in range(2):
-            ts(w("ON", h, 16, 2), w("P0", 0, 8), w("SC", h, h + 1), O.is_gt)
-        cp(w("H1"), w("P0", 64, 96))
+        mm(w("P4", 256, 512), w("SHN"), w("DF"))
+        mm(A("P5"), w("IDB"), w("DF"), True, False)
+        mm(A("P6"), w("IDB"), w("DF"), True, False)
+        mm(A("P6"), w("BL"), A("ONEB"), False, False)
+        act(w("DP"), w("P4", 0, 256), F.Identity, w("BP"))
+        act(w("DN"), w("P4", 256, 512), F.Identity, w("BN"))
+        tt(w("H1"), w("P0", 0, 32), w("HK"), O.add)
         ts(w("H2"), w("H1"), 4095, O.bitwise_and)
         tt(w("HP"), w("H2", 0, 16), w("H2", 16, 32), O.mult)
-        ts(w("HP"), w("HP"), 5, O.arith_shift_right)
-        ts(w("HV"), w("HP"), 16.0, O.mult, 16.0 * t, O.add)
-        top(0)
-        mins(CUT[3], CUT[4])
-        tree(1)
-        top(1)
-        ts(w("F4", 32, 48), w("MX"), 15, O.bitwise_and)
-        tt(w("E3"), w("MX"), w("HV"), O.add)
-        ts(w("F4", 0, 16), w("E3"), 10, O.arith_shift_right, 63, O.bitwise_and)
-        ts(w("F4", 16, 32), w("E3"), 4, O.arith_shift_right, 63, O.bitwise_and)
-        cp(w("F4B"), w("F4"))
-        tr(w("TP", 0, 128, 1, 48), w("F4B"))
-        r4 = w("R4", 0, 128, 1, 48)
-        cp(r4, w("TP", 0, 128, 1, 48))
+        ts(w("HP"), w("HP"), 5, O.arith_shift_right, 4095, O.bitwise_and)
         for h in range(2):
-            mm(w("P2", 128 * h, 128 * h + 128), w("SK%d" % h, 0, 128, 1, 48), r4)
-        for h in range(2):
-            mm(w("P6", 128 * h, 128 * h + 128), w("SV%d" % h, 0, 128, 1, 48), r4)
-        for h in range(2):
-            mm(w("P5", 128 * h, 128 * h + 128), w("SV%d" % h, 0, 128, 1, 48), r4, False, h == 1)
-        act(w("P0", 0, 256), w("P2", 0, 256), F.Relu, w("B2"), 8192.0)
-        act(w("P1", 0, 256), w("P2", 0, 256), F.Relu, w("B1"), -8192.0)
-        act(w("SG"), w("P5", 0, 256), F.Sign)
-        ts(w("FI"), w("CN"), 0.25, O.mult, -0.375, O.add)
-        ts(w("KM2"), w("F4", 32, 48), 2.0, O.mult)
-        ts(w("KM1"), w("F4", 32, 48), 1.0, O.add)
+            ts(w("HV", 8 * h, 8 * h + 8), w("HP", h, 16, 2), 16.0, O.mult, 16.0 * t, O.add)
+        if t == 0:
+            for c in range(0, 1024, 256):
+                first_qt(c)
+        if t == 2:
+            for c in range(0, 1024, 256):
+                whole(c, 256.0)
+        mm(A("P7"), w("NEG"), w("DF"), True, False)
+
+        def mins(a, b, h=None):
+            for k in range(16):
+                tt(w("MK", 256 * k + a, 256 * k + b), w("hv", 16 * a + k, 16 * b, 16), w("P3", a, b), O.min)
+            if h is not None:
+                p = "P%d" % (1 + h)
+                group([(w(p, 0, 128), w("C128"), w("KC"))]
+                      + [(w(p, k, 128, 16), w("MK", 256 * k + 128 * h, 256 * k + 128 * h + 128), w("G16")) for k in range(16)])
+                scan(half("SCN", h), w("RS16", 0, 128), w(p, 0, 128), 0.0, O.mult, O.max)
+        mins(0, CUT[2], 0)
+        mins(CUT[2], CUT[3])
+        mins(CUT[3], CUT[4], 1)
+        act(w("ABF"), A("P3"), F.Relu, -1.0)
+        act(w("FB"), w("CN"), F.Identity, 191.625, 0.25)
+        act(w("SGC"), w("CN"), F.Sign)
+        tt(w("E3"), w("SCN", 15, 256, 16), w("HV"), O.add)
+        cp(w("MX"), w("SCN", 15, 256, 16))
+        tt(w("XK", 16, 272), ind(w("MX"), w("OC")), w("SCN"), O.is_equal)
         ts(w("VV"), w("E3"), 4, O.arith_shift_right, 4095, O.bitwise_and)
-        ts(w("OK1"), w("VV"), 3584.0, O.is_lt)
-        tt(w("OK1"), w("OK1"), w("ON"), O.mult)
-        tt(w("EB"), w("DN"), w("P6", 0, 256), O.min)
-        tt(w("P0", 0, 256), w("DF"), w("P0", 0, 256), O.add)
-        tt(w("P1", 0, 256), w("DF"), w("P1", 0, 256), O.subtract)
-        tt(w("EC"), w("EB"), w("P0", 0, 256), O.min)
-        tt(w("P1", 0, 256), w("DP"), w("P1", 0, 256), O.max)
-        tt(w("CH"), w("EC"), w("P1", 0, 256), O.max)
+        ts(w("VB"), ind(w("VV"), w("OC")), -float(MID), O.add)
         for h in range(2):
-            mm(w("P3", h, 16, 2), w("SG", 128 * h, 128 * h + 128), w("G8"))
+            mm(half("P5", h), w("XK", 16 + 128 * h, 144 + 128 * h), w("IBG"), False, h == 1)
         for h in range(2):
-            mm(w("P2", h, 32, 2), w("CH", 128 * h, 128 * h + 128), w("WT", 0, 16))
-        act(w("P4", 0, 256), w("CH"), F.Copy, 0.0, 256.0)
-        cp(w("SGI"), w("P3", 0, 16))
-        tt(w("N1"), w("SGI"), w("KM2"), O.add)
-        ts(w("N2"), w("N1"), 14.0, O.is_gt)
-        ts(w("N4"), w("SGI"), 1, O.arith_shift_right)
-        tt(w("N5"), w("N4"), w("KM1"), O.add)
-        tt(w("N6"), w("N5"), w("N2"), O.add)
-        ts(w("N7"), w("N6"), 1, O.bitwise_and)
-        ts(w("SNB"), w("N7"), -2.0, O.mult, 1.0, O.add)
-        tr(w("TP", 0, 128, 1, 16), w("SNB"))
-        ts(w("N3"), w("SGI"), 1, O.bitwise_and)
-        ts(w("SN0"), w("N3"), 0.0, O.is_equal)
-        tt(w("OK1"), w("OK1"), w("SN0"), O.mult)
-        for q in range(4):
-            ts(w("QQ", 16 * q, 16 * q + 16), w("OK1"), -8.0, O.mult, 8.0 + q, O.add)
-        cp(w("R5", 0, 128, 1, 16), w("TP", 0, 128, 1, 16))
+            mm(half("P6", h), w("XK", 15 + 128 * h, 143 + 128 * h), w("IBG"), False, h == 1)
         for h in range(2):
-            mm(w("P0", 128 * h, 128 * h + 128), w("SS%d" % h, 0, 128, 1, 16), w("R5", 0, 128, 1, 16))
-        cp(w("I1"), w("P2", 0, 32))
+            mm(half("P4", h), half("VB", h), w("IDB"))
+        for h in range(2):
+            mm(half("P7", h), half("VB", h), w("IDB"), False, h == 1)
+        tt(w("HI"), A("P5"), w("DN"), O.min)
+        tt(A("P6"), A("P6"), w("DP"), O.max)
+        tt(w("CT"), A("P4"), w("HI"), O.min)
+        tt(w("CH"), w("CT"), A("P6"), O.max)
+        for h in range(2):
+            mm(w("P0", h, 32, 2), half("CH", h), w("WT"))
+        act(w("AE"), A("P7"), F.Abs)
+        act(w("SG"), w("AE"), F.Sign)
+        for h in range(2):
+            mm(w("P3", 8 * h, 8 * h + 8), half("SG", h), w("GM8"))
+        ts(w("VX"), w("VV"), 3584.0, O.is_ge, 8.0, O.mult)
+        tt(w("VD"), w("P3", 0, 16), w("VX"), O.add)
+        tt(w("QQ"), ind(w("VD"), w("OQ")), w("QC"), O.add)
+        tt(w("I1"), w("P0", 0, 32), w("HK"), O.add)
         ts(w("I2"), w("I1"), 4095, O.bitwise_and)
         tt(w("PR"), w("I2", 0, 16), w("I2", 16, 32), O.mult)
         ts(w("OW"), w("PR"), 5, O.arith_shift_right, 3, O.bitwise_and)
-        for q in range(4):
-            tt(w("OM", 16 * q, 16 * q + 16), w("OW"), w("QQ", 16 * q, 16 * q + 16), O.is_equal)
-        mm(w("P5", 0, 64), w("TRI"), w("OM"), True, False)
-        for q in range(4):
-            mm(w("P5", 16 * q + 1, 16 * q + 16, 2), w("ONEB", 0, 128), w("OM", 16 * q, 16 * q + 16, 2), False, q == 3)
-        tt(w("CF32"), w("FI"), w("P0", 0, 256), O.mult)
-        for q in range(4):
-            ts(w("K1", 16 * q, 16 * q + 16), w("OM", 16 * q, 16 * q + 16), -4096.0, O.mult, 4096.0 + 64 * q, O.add)
-        ts(w("K5"), w("P5", 0, 64), 64.0, O.is_ge, 4096.0, O.mult)
-        tt(w("K6"), w("P5", 0, 64), w("K1"), O.add)
-        tt(w("K7"), w("K5"), w("K6"), O.add)
-        tt(w("K2"), w("K7", 0, 32), w("K7", 32, 64), O.min)
-        tt(w("K8"), w("K2", 0, 16), w("K2", 16, 32), O.min)
+        tt(w("OM"), ind(w("OW"), w("OW4")), w("QQ"), O.is_equal)
+        group([(w("P3", 64, 128), w("C128"), w("KS")), (w("P3", 64, 128), w("TRS"), w("OM")),
+               (w("P3", 96, 128), w("ONEB", 0, 128), w("OM", 0, 32))])
+        scan(w("SC2"), w("RS4"), w("P3", 64, 128), 0.0, O.add, O.min)
+        tt(w("XF"), ind(w("SC2"), w("OL4")), w("MT"), O.min)
+        wrap("P4")
+        cp(w("OFF"), w("P4", 0, 16))
+        mm(A("P5"), w("QW"), w("CH"), True, False)
+        ts(w("HS", 0, 16), w("PR"), 7, O.arith_shift_right, 1023, O.bitwise_and)
+        ts(w("HS", 16, 32), w("I2", 0, 16), 511, O.bitwise_and)
+        cp(w("T16", 0, 16), w("HS", 0, 16))
+        ts(w("T16", 16, 32), w("HS", 16, 32), 2.0, O.mult, 1.0, O.add)
+        mm(w("P7", 0, 128, 1, 32), w("T16"), w("IDB"))
+        cp(w("R4", 0, 128, 1, 32), w("P7", 0, 128, 1, 32))
         for h in range(2):
-            tt(w("FS", 8 * h, 8 * h + 8), w("K8", h, 16, 2), w("TRS", h, 16, 2), O.min)
-        t2w(w("FS"), 16, "XF")
+            mm(half("P5", h), w("SH%d" % h, 0, 128, 1, 32), w("R4", 0, 128, 1, 32), False, h == 1)
+        act(w("REC"), A("P5"), F.Identity, w("QB0"))
+        scatter("SA%d" % t, "OFF", "REC")
+        sent += send("SA%d" % t, IA, "ra%d" % t)
+        group([(A("P1"), w("IDB"), w("CH")), (A("P1"), w("NEG"), w("DF"))])
+        act(w("SGN"), A("P1"), F.Sign)
+        mm(A("P2"), w("BLK"), w("SGN"))
+        act(w("RN"), A("P2"), F.Identity, 384.5, -1 / 256)
+        group([(A("P1"), w("BLK"), w("SGN")), (A("P1"), w("IDB"), w("FB")), (A("P1"), w("I2B"), w("RN"))])
+        act(w("CA"), A("P1"), F.Abs, -98304.0 - 128 - 192)
+        group([(A("P6"), w("IDB"), w("CH")), (A("P6"), w("IQ"), w("CA"))])
+        act(w("ED"), A("P6"), F.Identity, MID - 0.5)
+        scatter("SB%d" % t, "OFF", "ED")
+        sent += send("SB%d" % t, IB, "rb%d" % t)
+        group([(A("P2"), w("IDB"), w("CN")), (A("P2"), w("NEG"), w("SGC"))])
+        act(w("CFD"), A("P2"))
+        group([(A("P7"), w("QW"), w("DF")), (A("P7"), w("R8"), w("ABF"))])
+        act(w("QS"), A("P7"), F.Identity, w("QB0"))
+        if t:
+            scatter("QT", "FO", "QN", 2)
+        scatter("QT", "GU", "QS", 2)
+        scatter("TC", "GU", "CFD", 2)
         for h in range(2):
-            mm(w("P6", 0, 16), w("XF", 128 * h, 128 * h + 128), SEL[h], h == 0, h == 1)
-        tt(w("ED"), w("CF32"), w("P4", 0, 256), O.add)
-        cp(w("OFF"), w("P6", 0, 16))
-        cp(ind(w(SB), w("OFF")), w("ED"))
-        sent += send(t)
-        act(w("P3", 256, 512), w("CN"), F.Sign)
-        if t == 0:
-            first_qt(1)
-        tt(w("CFD"), w("CN"), w("P3", 256, 512), O.subtract)
-        act(w("ABF"), w("CFD"), F.Abs)
-        mm(w("P0", 0, 256), w("QW"), w("DF"), True, False)
-        mm(w("P0", 0, 256), w("R8"), w("ABF"), False, True)
-        act(w("QS"), w("P0", 0, 256))
-        cp(ind(w("TC"), w("GU")), w("CFD"))
-        if t == 0:
-            last_constants()
-        cp(ind(w("QT"), w("GU")), w("QS"))
-        if t == 2:
-            for b in range(2):
-                mm(w("P5", 0, 512), w("NEGI"), w("TD", 512 * b, 512 * b + 512), True, False)
-                mm(w("P5", 0, 512), w("IDN"), w("TC", 512 * b, 512 * b + 512), False, True)
-                act(w("YT", 512 * b, 512 * b + 512), w("P5", 0, 512), F.Copy, 128.0, -256.0)
-        ts(w("AT", 0, 128), w(IN, 0, 128), 1 / 256, O.mult, MAG, O.add)
-        act(w("AT", 128, 256), w(IN, 128, 256), F.Identity, MAG, 1 / 256)
-        ts(w("AD", 0, 128), w("AT", 0, 128), -MAG, O.add)
-        act(w("AD", 128, 256), w("AT", 128, 256), F.Identity, -MAG)
-        for h in range(2):
-            mm(w("P1", h, 48, 2), w("AD", 128 * h, 128 * h + 128), w("WT"))
-        mm(w("P2", 0, 256), w("QW"), w("AD"))
-        act(w("P6", 0, 256), w("AD"), F.Copy, 0.0, -256.0)
-        cp(w("J1"), w("P1", 0, 48))
-        ts(w("J2"), w("J1", 0, 32), 4095, O.bitwise_and)
-        tt(w("JP"), w("J2", 0, 16), w("J2", 16, 32), O.mult)
-        ts(w("ZD", 32, 48), w("J2", 0, 16), 4, O.arith_shift_right, 31, O.bitwise_and)
-        ts(w("SL2"), w("J2", 0, 16), 15, O.bitwise_and)
-        ts(w("ZD", 0, 16), w("JP"), 12, O.arith_shift_right, 31, O.bitwise_and)
-        ts(w("ZD", 16, 32), w("JP"), 7, O.arith_shift_right, 31, O.bitwise_and)
-        ts(w("ZD", 48, 64), w("SL2"), 2.0, O.mult, 1.0, O.add)
-        for h in range(2):
-            cp(w("ZF", 32 * h, 32 * h + 32), w("ZD", h, 64, 2))
-        t2w(w("ZF"), 64, "XB")
-        act(w("QA"), w("P2", 0, 256))
-        ts(w("HQ"), w("JP"), 7, O.arith_shift_right, 1023, O.bitwise_and)
-        ts(w("ST0"), w("J2", 0, 16), 511, O.bitwise_and)
-        ts(w("ST"), w("ST0"), 2.0, O.mult, 1.0, O.add)
-        ts(w("NU"), w("J1", 32, 48), 1.0, O.is_lt, 4096.0, O.mult)
-        tt(w("P6", 0, 256), w(IN), w("P6", 0, 256), O.add)
+            mm(w("P1", 16 * h, 16 * h + 16), half(IA, h), w("SHU"))
+        for r in range(16):
+            ts(w("XB", r, 512, 16), w("P1", 0, 32), w("MR", r, r + 1), O.mult)
         for c in range(2):
-            for h in range(2):
-                for f in range(4):
-                    mm(w("P%d" % (3 + c), 0, 80), w("XB", (32 * h + 8 * f) * 16, (32 * h + 8 * f) * 16 + 128),
-                       w("ZW", 640 * h + 160 * f + 80 * c, 640 * h + 160 * f + 80 * c + 80), h + f == 0, h + f == 4)
-            z = (80 * c, 80 * c + 80)
-            cp(w("ZI", *z), w("P%d" % (3 + c), 0, 80))
-            ts(w("ZJ", *z), w("ZI", *z), 1023, O.bitwise_and)
-            cp(w("ZU", *z), w("ZJ", *z))
-        SCP = ["P5", "P0", "P1"]
-
-        def probe(m):
-            o = w("CMP", 256 * m, 256 * m + 256)
-            if m < 4:
-                tt(o, ind(w("QT", 0, 1024), w("ZU", 16 * m, 16 * m + 16)), w("QA"), O.is_equal)
-            else:
-                tt(o, w("PR5", 256 * (m - 4), 256 * (m - 3)), w("P2", 0, 256), O.is_equal)
-            for h in range(2):
-                mm(w(SCP[0 if m < 5 else 1 if m < 8 else 2], 16 * (m % 5) + h, 16 * (m % 5) + 16, 2),
-                   w("CMP", 256 * m + 128 * h, 256 * m + 128 * h + 128), w("RW"))
-
-        def score(c):
-            a, b = ((0, 5), (5, 8), (8, 10))[c]
-            p, z = w(SCP[c], 16 * (a % 5), 16 * (b - 1) % 80 + 16), (16 * a, 16 * b)
-            ts(w("S2", *z), p, 8.0, O.is_ge, -1024.0, O.mult)
-            ts(p, p, 8.0, O.is_equal, -1024.0, O.mult)
-            tt(w("S3", *z), w("S2", *z), w("MC", *z), O.add)
-            tt(w("S1", *z), p, w("S3", *z), O.add)
-        for m in range(6):
-            act(w("PR5", 256 * m, 256 * m + 256), ind(w("QT", 0, 1024), w("ZU", 16 * m + 64, 16 * m + 80)))
-        for m in range(6):
-            probe(m)
-        score(0)
-        tt(w("S4", 0, 32), w("S1", 0, 32), w("S1", 32, 64), O.min)
-        tt(w("S5", 0, 16), w("S4", 0, 16), w("S4", 16, 32), O.min)
-        tt(w("S6"), w("S5", 0, 16), w("S1", 64, 80), O.min)
-        for m in (6, 7):
-            probe(m)
-        score(1)
-        tt(w("S4", 32, 48), w("S1", 80, 96), w("S1", 96, 112), O.min)
-        tt(w("S5", 16, 32), w("S4", 32, 48), w("S1", 112, 128), O.min)
-        tt(w("S4", 48, 64), w("S5", 16, 32), w("S6"), O.min)
-        for m in (8, 9):
-            probe(m)
-        score(2)
-        tt(w("S4", 64, 80), w("S1", 128, 144), w("S1", 144, 160), O.min)
-        tt(w("S7"), w("S4", 64, 80), w("S4", 48, 64), O.min)
-        tt(w("M3"), w("S7"), w("ST"), O.mult)
-        tt(w("SN"), w("S7"), w("NU"), O.add)
-        ts(w("M4"), w("SN"), 2048.0, O.is_ge, 2048.0, O.mult)
-        ts(w("M5"), w("SN"), 2048.0, O.is_ge, 32.0, O.mult)
-        tt(w("PN"), w("M3"), w("HQ"), O.add)
-        ts(w("DG", 0, 16), w("PN"), 6, O.arith_shift_right, 15, O.bitwise_and)
-        ts(w("DG", 16, 32), w("PN"), 63, O.bitwise_and)
-        tt(w("FD", 0, 16), w("DG", 0, 16), w("M5"), O.add)
-        cp(w("FD", 16, 32), w("DG", 16, 32))
-        ts(w("PM"), w("PN"), 1023, O.bitwise_and)
-        tt(w("PLC"), w("PM"), w("M4"), O.add)
-        tt(w("PT"), w("PLC"), w("TRA"), O.min)
-        tr(w("TP", 0, 128, 1, 32), w("FD"))
+            p, z = w("P%d" % (3 + c), 0, 80), (80 * c, 80 * c + 80)
+            group([(p, w("C128"), w("KZ", 0, 80))]
+                  + [(p, w("XB", 128 * j, 128 * j + 128), w("ZW", 160 * j + 80 * c, 160 * j + 80 * c + 80)) for j in range(4)])
+            ts(w("RZ", *z), p, -511.5, O.add)
+            tt(w("ZU", *z), p, w("RZ", *z), O.subtract)
+        mm(w("P5", 0, 320), w("C128"), w("KA"), True, False)
+        mm(w("P5", 0, 320), w("C128"), w("KB"), False, False)
         for h in range(2):
-            cp(w("PF", 8 * h, 8 * h + 8), w("PLC", h, 16, 2))
-        cp(w("R6", 0, 128, 1, 32), w("TP", 0, 128, 1, 32))
-        for h in range(2):
-            mm(w("P0", 128 * h, 128 * h + 128), w("SV%d" % h, 0, 128, 1, 32), w("R6", 0, 128, 1, 32))
-        t2w(w("PF", 0, 16), 16, "XF")
-        for h in range(2):
-            mm(w("P1", 0, 16), w("XF", 128 * h, 128 * h + 128), SEL[h], h == 0, h == 1)
-        cp(w("PU"), w("P0", 0, 256))
-        cp(w("PW"), w("P1", 0, 16))
-        ts(w("PO"), w("PW"), 1279.0, O.min)
-        act(w("CO"), ind(w("TC"), w("PO")))
+            mm(w("P5", 160 * h, 160 * h + 160), half(IA, h), w("KW"), False, False)
         if t == 2:
-            act(w("P1", 0, 256), w("AD"), F.Copy, 128.0, 256.0)
-        tt(w("CV"), w("CO"), w("P6", 0, 256), O.add)
-        ts(w("CNW"), w("CV"), 127.0, O.min, -127.0, O.max)
+            for c in range(0, 1024, 256):
+                group([(A("P2"), w("I32"), w("TN", c, c + 256)), (A("P2"), w("IDB"), w("TC", c, c + 256))])
+                act(w("YT", c, c + 256), A("P2"), F.Identity, 128.0)
+        NV = 3
+        for m in range(NV, 10):
+            act(w("PR5", 256 * (m - NV), 256 * (m - NV + 1)), ind(w("QT", 0, 1024), w("ZU", 16 * m, 16 * m + 16)))
+        act(A("P0"), w(IA))
+        for m in range(10):
+            o = w("CMP", 256 * m, 256 * m + 256)
+            if m < NV:
+                tt(o, ind(w("QT", 0, 1024), w("ZU", 16 * m, 16 * m + 16)), w(IA), O.is_equal)
+            else:
+                tt(o, w("PR5", 256 * (m - NV), 256 * (m - NV + 1)), A("P0"), O.is_equal)
+            for h in range(2):
+                mm(w("P5", 160 * h + m, 160 * h + 160, 10), w("CMP", 256 * m + 128 * h, 256 * m + 128 * h + 128), w("RW"),
+                   False, m == 9 and h == 1)
+        act(w("AT"), w(IB), F.Identity, MAG)
+        act(w("NA"), w("AT"), F.Identity, MAG, -1.0)
+        mm(A("P6"), w("I256"), w(IB), True, False)
+        mm(A("P6"), w("I256"), w("NA"), False, False)
+        scan(w("KY"), w("RSK"), w("P5", 0, 320), 0.0, O.max, O.min)
+        ts(w("RK"), w("KY", 19, 320, 20), -7.9921875, O.add, YCAP, O.min)
+        tt(w("PL16"), w("KY", 19, 320, 20), w("RK"), O.subtract)
+        tt(w("PL"), w("KY", 19, 320, 20), w("RK"), O.subtract)
+        mm(w("P7", 0, 128, 1, 16), w("PL16"), w("IDB"))
+        tt(w("XF"), ind(w("PL"), w("OC")), w("M64"), O.mult)
+        cp(w("R6", 0, 128, 1, 16), w("P7", 0, 128, 1, 16))
+        wrap("P1")
+        for h in range(2):
+            mm(half("P0", h), w("SS%d" % h, 0, 128, 1, 16), w("R6", 0, 128, 1, 16))
+        cp(w("PW"), w("P1", 0, 16))
+        cp(w("PU"), A("P0"))
+        cp(w("PO"), w("PW"))
+        act(w("CO"), ind(w("TC"), w("PO")))
+        mm(A("P6"), w("IDB"), w("CO"), False, True)
+        ts(w("CNW"), A("P6"), 127.0, O.min, -127.0, O.max)
         if t < 2:
             act(w("ABN"), w("CNW"), F.Abs)
-            mm(w("P2", 0, 256), w("R8"), w("ABN"))
-            tt(w("QN"), w("QA"), w("P2", 0, 256), O.add)
+            group([(A("P2"), w("I32"), w(IA)), (A("P2"), w("R8"), w("ABN"))])
+            act(w("QN"), A("P2"))
         else:
-            tt(w("YN"), w("CNW"), w("P1", 0, 256), O.add)
+            act(A("P2"), w("NA"), F.Identity, 128.0, -256.0)
+            tt(w("YN"), w("CNW"), A("P2"), O.add)
+        mm(w("P3", 0, 16), w("IDB"), w("Z16"), True, False)
         for c in range(16):
             a = 0 if c < 8 else 128
             ts(w("MK", 256 * c + a, 256 * c + 256), w("PU", a, 256), w("PW", c, c + 1), O.is_equal)
             wc = w("WC", 8 * (c % 8), 8 * (c % 8) + 8)
             if c < 8:
-                mm(w("P3", 0, 16, 2), w("MK", 256 * c, 256 * c + 128), wc, c == 0, c == 7)
-            mm(w("P4", 1, 16, 2), w("MK", 256 * c + 128, 256 * c + 256), wc if c > 7 else w("WBIG"), c == 0, c == 15)
-        for h in range(2):
-            ts(w("LO", h, 16, 2), w("P%d" % (3 + h), h, 16, 2), w("THR"), O.is_ge, w("TRA", h, h + 1), O.mult)
-        for h in range(2):
-            tt(w("PF", 16 + 8 * h, 24 + 8 * h), w("LO", h, 16, 2), w("PT", h, 16, 2), O.max)
-        t2w(w("PF", 16, 32), 16, "XF")
-        for h in range(2):
-            mm(w("P5", 0, 16), w("XF", 128 * h, 128 * h + 128), SEL[h], h == 0, h == 1)
-        cp(w("FO"), w("P5", 0, 16))
+                mm(w("P3", 0, 8), w("MK", 256 * c, 256 * c + 128), wc, False, False)
+            mm(w("P3", 8, 16), w("MK", 256 * c + 128, 256 * c + 256), wc if c > 7 else w("WBIG"), False, c == 15)
+        ts(w("LO"), w("P3", 0, 16), w("THR"), O.is_ge)
+        tt(w("XF"), ind(w("LO"), w("OC")), w("MT"), O.mult)
+        wrap("P4")
+        tt(w("FO"), w("P4", 0, 16), w("PW"), O.max)
         if t < 2:
-            cp(ind(w("QT"), w("FO")), w("QN"))
-            cp(ind(w("TC"), w("FO")), w("CNW"))
+            scatter("TC", "FO", "CNW")
         else:
-            cp(ind(w("YT"), w("FO")), w("YN"))
-            dma("d", T.y[:, :], T["YT"][:, 0:1024], "st0", w("YT", 0, 1024)[1], [])
+            scatter("YT", "FO", "YN")
+            dma("d", T.y[:, :], T["YT"][:, 0:1024], "st0", w("YT", 0, 1024)[1], [], 4.0)
     schedule()
     wait("d", "st0", 1)
     g.wait_ge(T.sem.snd, sent)

@@ -1,23 +1,27 @@
 from concourse.bass import DstId, RemoteDMATransfer
 from concourse.mybir import AluOpType as O, ActivationFunctionType as F, AxisListType as AX
 
-WAKE, SLACK, BETA = 0.15, 0.03, 1.2
+TURNS, JOLT, SPAN, HV0, DIG, FS, CQV, PQ = 600, 1.0, 5.0, 60, 1, 60, 1, 4
+SPLIT, FK, WR, PT, TB = 0, 8, 6, 2, 1
+ORDER = {}
+WAKE, NEAR, FAR = 0.15, 3.0, 3.0
 F32, BF, I32, U16, F16 = "float32", "bfloat16", "int32", "uint16", "float16"
 BUFS = {
-    F32: dict(TD=1536, QT=1536, TM=1024, TN=1024, YT=1280, ONE=160, I32=128, I256=128, QW32=128, SHU=16, KW=160, KX=160, SW=16, MR=16,
+    F32: dict(TD=1536, QT=1536, TM=1024, TN=1024, YT=1280, ONE=160, I32=128, I256=128, QW32=128, SW=16, MR=16,
               PA=24, RC=1, QB0=1, BN=1, BP=1, THR=1, WX=1, PW3=128, PWT=128, Z128=128, M64=256, MT=256, JC=2, RS8=136, RS16=256,
               RS4=64, RSK=320, QC=64, HK=32, LM=136, LD=16, DP=256, DN=256, SCN=256, HI=256, CT=256, HV=16, MX=16, VX=16, VD=16, QQ=64,
-              SC2=64, REC=256, ED=256, QS=256, QN=256, AT=256, NA=256, KY=320, PL=16, PW=16, LO=16, YN=256, PR5=1792,
+              SC2=64, REC=256, ED=256, QS=256, QN=256, AT=256, NA=256, KY=320, PL=16, PW=16, LO=16, YN=256, PR5=2560,
+              RC8=1, KI=128, NB=16, VAL=16, OLD=16, NL=16, D0=16, WIN=16, DW=16, AK=256,
               SA0=1280, SA1=1280, SA2=1280, SB0=1280, SB1=1280, SB2=1280, IA0=256, IA1=256, IA2=256, IB0=256, IB1=256, IB2=256),
     BF: dict(TC=1536, ham=3584, ONEB=320, G8=8, G16=8, GM8=8, TRX=128, TRS=128, IDB=128, NEG=128, IBG=128, I2B=128, IQ=128, BLK=128,
-             KC=128, KD=136, DMB=136, C128=128, BL=128, R8=128, QW=128, SHP=128, SHN=128, WT=16, WC=128, WBIG=8, ZG=24, ZW=640,
-             IM=160, SS0=128, SS1=128, SH0=128, SH1=128, RW=16, KA=320, KB=320, KS=64, KZ=160, Z16=16, QB=1024, LV=64, OL=1024,
+             KC=128, KD=136, DMB=136, C128=128, BL=128, R8=128, QW=128, SHP=128, SHN=128, WT=16, WC=128, WBIG=8, ZG=24, ZA=144,
+             ZB=144, ZX=128, KW=160, KX=160, AB=256, SS=128, SS1=128, SH0=128, SH1=128, RW=16, KA=160, KB=160, KS=64, KZ=80, Z16=16, QB=1024, LV=64, OL=1024,
              CN=256, hv=4096, MK=4096, XK=272, AE=256, SG=256, SGN=256, RN=256, FB=256, CA=256, OM=64, SGC=256, CFD=256, ABF=256,
-             ABN=256, CMP=2560, RZ=160, CO=256, CNW=256),
+             ABN=256, CMP=2560, RZ=160, CO=256, CQ=256, CNW=256, TR2=128, TWOS=128, MONE=128, IO=128, TH=2048, LW2=128, DK=256),
     I32: dict(DET=1024, CI=1024, PI=16, PJ=1, PK=24, PLI=24, EI=4, EJ=4, EK=4, XI=16, R32=64, LOW=64, E3=16, VV=16, H1=32, H2=32,
-              HP=16, I1=32, I2=32, PR=16, OW=16, HS=32),
-    F16: dict(OA=1024, DF=256, VB=256, CH=256, XF=256, T16=32, R4=128, XB=512, RK=16, PL16=16, R6=128, PU=256),
-    U16: dict(GU=16, DU=256, OFF=16, ZU=160, PO=16, FO=16, OC=16, OL4=16, OQ=4, OW4=4),
+              HP=16, I1=32, I2=32, PR=16, OW=16, HS=32, EL=16, EM=1, PN=16, PM=16, KJ=16),
+    F16: dict(OA=1024, DF=256, VB=256, CH=256, XF=256, T16=32, R4=128, IH=256, RK=16, PL16=16, R6=256, PU=256),
+    U16: dict(GU=16, DU=256, OFF=16, ZU=160, PO=16, FO=16, OC=16, OL4=16, OQ=4, OW4=4, OD=16),
 }
 SCRATCH, WIDTH, WHERE = {}, {}, {}
 for _d in BUFS:
@@ -33,12 +37,14 @@ for _d in BUFS:
     if _p:
         SCRATCH["small_" + _d] = ("sbuf", [128, _p], _d)
 SCRATCH["BS"] = ("sbuf", [128, 8, 17, 8], BF)
+SCRATCH["OL"] = ("sbuf", [128, 64, 16], BF)
 TWO = list(BUFS[F16]) + list(BUFS[BF]) + list(BUFS[U16])
 PSUM = ["P%d" % _k for _k in range(8)]
 for _n in PSUM:
     WIDTH[_n] = 512
     SCRATCH[_n] = ("psum", [128, 512], F32)
-SEMAPHORES = ["qv", "qs", "qt", "qg", "ld0", "ld1", "ld2", "ld3", "ld4", "st0", "st1", "snd", "ra0", "ra1", "ra2", "rb0", "rb1", "rb2"]
+SEMAPHORES = ["qv", "qs", "qt", "qg", "ld0", "ld1", "ld2", "ld3", "ld4", "st0", "snd"]
+SEMAPHORES += [_n + str(_t) for _n in ("ra", "rn", "rb") for _t in range(3)]
 W1 = [13 * _i + 5 for _i in range(16)]
 W2 = [255 - 14 * _i for _i in range(16)]
 MID = 1792
@@ -56,10 +62,10 @@ def rank_program(g, core, T, topo):
     wr, rd, last = {}, {}, {}
     semof = {"v": ("qv", 1), "s": ("qs", 1), "t": ("qt", 1), "g": ("qg", 1)}
 
-    def w(name, a=0, b=None, st=1, p=128):
+    def w(name, a=0, b=None, st=1, p=128, p0=0):
         b = WIDTH[name] if b is None else b
         n, o = WHERE.get(name, (name, 0))
-        ap = T[n][0:p, o + a:o + b] if st == 1 else T[n][0:p, o + a:o + b:st]
+        ap = T[n][p0:p, o + a:o + b] if st == 1 else T[n][p0:p, o + a:o + b:st]
         m = 0
         if st == 1:
             m = ((1 << (b - a)) - 1) << a
@@ -146,7 +152,7 @@ def rank_program(g, core, T, topo):
 
     def schedule():
         n = len(calls)
-        succ, npred = [[] for _ in range(n)], [0] * n
+        succ, npred, prev, done = [[] for _ in range(n)], [0] * n, [], [False] * n
         W, R, B = {}, {}, {}
         for j, (q, emit, reads, writes, cost, lat) in enumerate(calls):
             pred = {}
@@ -160,7 +166,7 @@ def rank_program(g, core, T, topo):
             for nm, m in reads:
                 for i, m2 in W.get(nm, []):
                     if m & m2:
-                        edge(i, WAKE)
+                        edge(i, 0.0 if nm[0] == "~" else WAKE)
             for nm, m in writes:
                 for i, m2 in W.get(nm, []) + R.get(nm, []):
                     if m & m2:
@@ -168,6 +174,7 @@ def rank_program(g, core, T, topo):
             for i, wk in pred.items():
                 succ[i].append((j, wk))
             npred[j] = len(pred)
+            prev.append(list(pred.items()))
             for nm, m in writes:
                 W[nm] = [x for x in W.get(nm, []) if x[1] & ~m] + [(j, m)]
                 R[nm] = [x for x in R.get(nm, []) if x[1] & ~m]
@@ -181,36 +188,76 @@ def rank_program(g, core, T, topo):
             way[j] = calls[j][4] + calls[j][5] + max([wk + way[k] for k, wk in succ[j]] + [0.0])
         for j in range(5):
             way[j] = 1e6 - j
-        free, est, order, avail = {}, [0.0] * n, [], {}
-        for j in range(n):
-            if not npred[j]:
-                avail.setdefault(calls[j][0], []).append(j)
-        while len(order) < n:
-            best = None
-            for q, a in avail.items():
-                if a:
-                    t0 = free.get(q, 0.0)
-                    s = min(max(t0, est[j]) for j in a)
-                    if best is None or s < best[0]:
-                        best = (s, q)
-            s, q = best
-            t0 = free.get(q, 0.0)
-            j = max((j for j in avail[q] if max(t0, est[j]) <= s + SLACK), key=lambda j: (way[j], -j))
-            soon = [i for i in avail[q] if way[i] > way[j] and s + SLACK < est[i] < s + calls[j][4] - BETA * (est[i] - s)]
-            if soon:
-                i = max(soon, key=lambda i: way[i])
-                fit = [f for f in avail[q] if max(t0, est[f]) + calls[f][4] <= est[i] + SLACK]
-                j = max(fit, key=lambda f: (way[f], -f)) if fit else i
-            avail[q].remove(j)
-            free[q] = max(t0, est[j]) + calls[j][4]
-            order.append(j)
-            for k, wk in succ[j]:
-                est[k] = max(est[k], free[q] + calls[j][5] + wk)
-                npred[k] -= 1
-                if not npred[k]:
-                    avail.setdefault(calls[k][0], []).append(k)
+
+        def lay(order, before, back):
+            start, busy = [0.0] * n, {}
+            for j in order:
+                q, c = calls[j][0], calls[j][4]
+                s = max([start[i] + calls[i][4] + calls[j if back else i][5] + wk for i, wk in before[j]]
+                        + [calls[j][5] if back else 0.0])
+                b = busy.setdefault(q, [])
+                lo, hi = 0, len(b)
+                while lo < hi:
+                    mid = (lo + hi) // 2
+                    lo, hi = (mid + 1, hi) if b[mid][1] <= s else (lo, mid)
+                while lo < len(b) and b[lo][0] < s + c - 1e-9:
+                    s = max(s, b[lo][1])
+                    lo += 1
+                b.insert(lo, (s, s + c))
+                start[j] = s
+            return start
+        def forth(key):
+            start = lay(sorted(range(n), key=lambda j: (j >= 5, key[j] if j >= 5 else 0.0, j)), prev, False)
+            return max(start[j] + calls[j][4] + calls[j][5] for j in range(n)), start
+
+        def back(start):
+            late = lay(sorted(range(n), key=lambda j: (-start[j] - calls[j][4], -j)), succ, True)
+            end = max(late[j] + calls[j][4] for j in range(n))
+            return [end - late[j] - calls[j][4] for j in range(n)]
+        kind = me // 2
+        if kind not in ORDER:
+            best = forth([-x for x in way])
+            base, seed = back(best[1]), 1
+            for turn in range(TURNS):
+                seed = seed * 48271 % 2147483647
+                t0, key = seed % 1000 / 1000 * best[0], list(base)
+                if turn % 3 == 0:
+                    for j in range(n):
+                        if turn and t0 - SPAN < base[j] < t0:
+                            key[j] += JOLT * ((j + seed) * 2654435761 % 1009) / 1009
+                else:
+                    j0 = seed // 1000 % n
+                    key[j0] += (JOLT * 2 * (seed // 7 % 101) / 100) * (1 if turn % 3 == 1 else -1)
+                    todo = [j0] if turn % 3 == 2 else []
+                    while todo:
+                        j = todo.pop()
+                        for i, wk in prev[j]:
+                            if key[i] > key[j]:
+                                key[i] = key[j]
+                                todo.append(i)
+                for j in range(n):
+                    kj = key[j]
+                    for k, wk in succ[j]:
+                        if key[k] < kj:
+                            key[k] = kj
+                new = forth(key)
+                if new[0] <= best[0]:
+                    best, base = new, key
+                if turn % 20 == 19:
+                    key = back(best[1])
+                    new = forth(key)
+                    if new[0] <= best[0]:
+                        best, base = new, key
+            ORDER[kind] = sorted(range(n), key=lambda j: (best[1][j], j))
+        order = ORDER[kind]
         for j in order:
-            calls[j][1](calls[j][2], calls[j][3])
+            calls[j][1](*[[x for x in calls[j][i] if x[0][0] != "~"] for i in (2, 3)])
+
+    def mark(name):
+        calls[-1][3].append(("~" + name, 1))
+
+    def behind(name):
+        calls[-1][2].append(("~" + name, 1))
 
     def col(x):
         return [x] if isinstance(x, tuple) else []
@@ -218,13 +265,13 @@ def rank_program(g, core, T, topo):
     def ap(x):
         return x[0] if isinstance(x, tuple) else x
 
-    CY = 0.0009
+    CY = 0.00083
 
     def vcost(o, a, k=1.0):
         if len(a) > 3:
-            return 0.06 + a[3] * 1.56 * CY
+            return 0.055 + a[3] * 1.56 * CY
         if len(o) > 3:
-            return 0.06 + o[3] * 3.8 * CY
+            return 0.055 + o[3] * 3.8 * CY
         return max(64, wide(a) * k) * CY
 
     def tt(o, a, b, op):
@@ -254,6 +301,15 @@ def rank_program(g, core, T, topo):
         E("s", lambda: S.activation(out=o[0], in_=a[0], func=f, bias=ap(bias), scale=ap(scale)), [a] + col(bias) + col(scale), [o],
           vcost(o, a))
 
+    def times(o, a, c):
+        act(o, a, F.Copy, 0.0, c)
+
+    def sfill(o, c):
+        times(o, w("ONEB", 0, wide(o)), c)
+
+    def half(n, h, p=128):
+        return w(n, 128 * h, 128 * h + 128, 1, p)
+
     def mm(o, l, r, start=True, stop=True):
         k = 4 if l[1][0][0] in BUFS[F32] else 1
         E("t", lambda: PE.matmul(out=o[0], lhsT=l[0], rhs=r[0], start=start, stop=stop), [l, r], [o],
@@ -279,7 +335,7 @@ def rank_program(g, core, T, topo):
     for c in range(4):
         x = w("DET", 256 * c, 256 * c + 256)
         dma("d", x[0], T.det[:, 256 * c:256 * c + 256], "ld%d" % c, [], x[1], 2.5 + 0.6 * c)
-    dma("d", T["hamt"][:, :], T.ham[:, :], "ld4", w("DET", 768, 1024)[1], w("hamt")[1], 6.0)
+    dma("d", T["hamt"][:, :], T.ham[:, :], "ld4", w("DET", 512, 768)[1], w("hamt")[1], 6.0)
 
     BIG, KB, Y0, MAG = 8192.0, 16384.0, 16640.0, 12582912.0
     YCAP = Y0 + 256 * 20
@@ -303,8 +359,10 @@ def rank_program(g, core, T, topo):
     iota(w("JC"), [[128, 2]], 1024, 1)
     ts(w("NEG"), w("IDB"), -4096.0, O.mult)
     tt(w("TRX"), w("TRS"), w("NEG"), O.add)
-    cp(w("TRS"), w("TRX"))
-    ts(w("NEG"), w("IDB"), -1.0, O.mult)
+    ts(w("TR2"), w("TRS"), 2.0, O.mult)
+    tt(w("TR2"), w("TR2"), w("IDB"), O.add)
+    fill(w("TWOS"), 2.0)
+    times(w("NEG"), w("IDB"), -1.0)
     ts(w("PLI"), w("PK"), 1023, O.bitwise_and)
     ts(w("PA"), w("PLI"), -2048.0, O.add, 0.5, O.mult)
     ts(w("PI"), w("PI"), 15, O.bitwise_and)
@@ -328,7 +386,7 @@ def rank_program(g, core, T, topo):
     aff(w("I32"), w("ONE", 0, 128), [[-16, 8], [-2, 16]], O.is_equal, -1, 1)
     tt(w("QW32"), w("QW32"), w("I32"), O.add)
     aff(w("QW32"), w("QW32"), [[0, 8], [-1, 16]], O.is_ge, 7, 0)
-    cp(w("QW"), w("QW32"))
+    act(w("QW"), w("QW32"))
     iota(w("QC"), [[0, 16], [1, 4]], 128, 0)
     iota(w("KS"), [[0, 16], [256, 4]], 4096, 0)
     iota(w("EI"), [[16, 4]], 0, 0)
@@ -338,7 +396,7 @@ def rank_program(g, core, T, topo):
     fill(w("SHN", 15, 128, 16), 0.0)
     fill(w("BL"), -BIG / 128)
     fill(w("BL", 0, 128, 16), -BIG / 64)
-    fill(w("RS16"), 1.0)
+    sfill(w("RS16"), 1.0)
     fill(w("RS16", 0, 256, 16), 0.0)
     fill(w("RS4"), 0.0)
     fill(w("RS4", 0, 64, 4), 1048576.0)
@@ -348,20 +406,17 @@ def rank_program(g, core, T, topo):
     fill(w("ZG"), 0.0)
     cp(w("ZG", 8, 16), w("G8"))
     SEL = [w("ZG", 8, 24), w("ZG", 0, 16)]
-    ts(w("G16"), w("G8"), 16.0 * 37, O.mult)
-    ts(w("GM8"), w("G8"), -8.0, O.mult)
-    ts(w("IBG"), w("IDB"), BIG, O.mult)
-    ts(w("I2B"), w("IDB"), 256.0, O.mult)
-    ts(w("IQ"), w("IDB"), 1 / 256, O.mult)
-    cp(w("I32"), w("IDB"))
-    ts(w("I256"), w("IDB"), 256.0, O.mult)
+    for n, c in (("G16", 16.0 * 37), ("GM8", -8.0), ("WBIG", 1e29)):
+        times(w(n), w("G8"), c)
+    for n, c in (("IBG", BIG), ("I2B", 256.0), ("IQ", 1 / 256), ("I32", 1.0), ("I256", 256.0)):
+        times(w(n), w("IDB"), c)
     ts(w("BN"), w("RC"), 15.0, O.is_equal, BIG, O.mult)
     ts(w("BP"), w("RC"), 0.0, O.is_equal, -BIG, O.mult)
     ts(w("QB0"), w("RC"), 8.0, O.is_lt, 4097.0 * MID, O.mult)
     fill(w("R8"), 0.0)
     cp(w("R8", 8, 128, 16), w("G8"))
     for r in range(16):
-        ts(w("BLK", r, 128, 16), w("G8"), -256.0, O.mult)
+        times(w("BLK", r, 128, 16), w("G8"), -256.0)
     cp(w("OC"), w("XI"))
     ts(w("OL4"), w("XI"), 4.0, O.mult, 3.0, O.add)
     ts(w("EI"), w("EI"), w("RC"), O.add)
@@ -371,39 +426,48 @@ def rank_program(g, core, T, topo):
     ts(w("EK"), w("EI"), 3, O.arith_shift_right)
     ts(w("EJ"), w("EJ"), 2.0, O.mult)
     tt(w("OW4"), w("EJ"), w("EK"), O.add)
+    iota(w("EL"), [[0, 2], [8, 2], [0, 4]], 0, 0)
+    ts(w("EM"), w("PJ"), 7, O.bitwise_and)
+    cp(w("RC8"), w("EM"))
+    ts(w("OD"), w("EL"), w("RC8"), O.add)
+    iota(w("KI"), [[0, 2], [1, 8], [0, 8]], 0, 0)
+    iota(w("IO"), [[1, 128]], 0, 0)
+    sfill(w("MONE"), -1.0)
     ts(w("M64", 0, 16), w("MR"), 64.0, O.mult)
     for n in (16, 32, 64, 128):
-        cp(w("M64", n, 2 * n), w("M64", 0, n))
+        act(w("M64", n, 2 * n), w("M64", 0, n))
     for h in range(2):
         ts(w("MT", 128 * h, 128 * h + 128), w("M64", 0, 128), w("JC", h, h + 1), O.mult, 1 / 64, O.mult)
     for t in range(3):
         for q in range(4):
-            fill(w("SA%d" % t, 256 * q, 256 * q + 64), -1.0)
-            fill(w("SB%d" % t, 256 * q, 256 * q + 64), 0.0)
-    aff(w("SHU"), w("ONE", 0, 16), [[-1, 2], [-16, 8]], O.is_equal, -9, 1)
-    iota(w("IM"), [[1, 10], [0, 16]], 0, 0)
-    for h in range(2):
-        z = w("ZW", 320 * h, 320 * h + 160)
-        aff(z, w("ONEB", 0, 160), [[0, 10], [-16, 16]], O.is_ge, 128 * h, 1)
-        aff(z, z, [[0, 10], [16, 16]], O.is_ge, 15 - 128 * h, -1)
-        tt(w("ZW", 320 * h + 160, 320 * h + 320), z, w("IM"), O.mult)
-        aff(w("SS%d" % h), w("ONEB", 0, 128), [[-1, 8], [0, 16]], O.is_equal, -8 * h, 1)
-        ts(w("SS%d" % h), w("SS%d" % h), 64.0, O.mult)
+            sfill(w("SA%d" % t, 256 * q, 256 * q + 64), -1.0)
+            sfill(w("SB%d" % t, 256 * q, 256 * q + 64), 0.0)
+    for z, m0, n in (("ZA", 0, 8), ("ZB", 8, 2)):
+        fill(w(z, 0, 16), 0.0)
+        iota(w("ZX"), [[0, 8], [1, 16]], m0, 0)
+        aff(w("ZX"), w("ZX"), [[-16, 8], [0, 16]], O.is_equal, -10, 1)
+        aff(w(z, 16, 144), w("ONEB", 0, 128), [[-16, 8], [0, 16]], O.is_equal, -9, 1)
+        tt(w(z, 16, 144), w(z, 16, 144), w("ZX"), O.add)
+        aff(w(z, 16, 144), w(z, 16, 144), [[0, 8], [-1, 16]], O.is_ge, n - 1, 0)
+    aff(w("SS"), w("ONEB", 0, 128), [[-1, 8], [0, 16]], O.is_equal, 0, 1)
+    times(w("SS"), w("SS"), 64.0)
+    aff(w("SS1"), w("ONEB", 0, 128), [[-1, 8], [0, 16]], O.is_equal, -8, 1)
+    times(w("SS1"), w("SS1"), 64.0)
     fill(w("KZ"), 196608.0)
     fill(w("Z16"), 0.0)
     iota(w("KX"), [[0, 16], [1, 10]], 0, 0)
     aff(w("KX"), w("KX"), [[-16, 8], [0, 20]], O.is_equal, -10, 1)
-    aff(w("KW"), w("ONE"), [[-16, 8], [0, 20]], O.is_equal, -9, 1)
+    aff(w("KW"), w("ONEB", 0, 160), [[-16, 8], [0, 20]], O.is_equal, -9, 1)
     tt(w("KW"), w("KW"), w("KX"), O.add)
-    ts(w("KW"), w("KW"), 1 / 64, O.mult)
-    iota(w("KA"), [[0, 16], [256, 20]], int(Y0), 0)
-    iota(w("KB"), [[0, 16], [-7, 2], [0, 10]], 8, 0)
-    ts(w("KB"), w("KB"), KB, O.mult)
+    times(w("KW"), w("KW"), 1 / 64)
+    iota(w("KA"), [[0, 8], [256, 20]], int(Y0), 0)
+    iota(w("KB"), [[0, 8], [-7, 2], [0, 10]], 8, 0)
+    times(w("KB"), w("KB"), KB)
     ts(w("RW", 1, 16, 2), w("R8", 8, 128, 16), w("MR", 8, 9), O.mult, -KB, O.mult)
     ts(w("WX"), w("RC"), 8.0, O.is_lt, -KB, O.mult)
     ts(w("RW", 0, 16, 2), w("G8"), w("WX"), O.mult)
     tt(w("RW", 0, 16, 2), w("RW", 0, 16, 2), w("RW", 1, 16, 2), O.subtract)
-    fill(w("RSK"), 0.0)
+    sfill(w("RSK"), 0.0)
     for h in range(2):
         ts(w("RSK", 160 * h, 160 * h + 160, 20), w("ONE", 0, 8), w("JC", h, h + 1), O.mult, 1 / 64, O.mult)
     ts(w("RSK", 0, 320, 20), w("RSK", 0, 320, 20), YCAP, O.add)
@@ -417,7 +481,6 @@ def rank_program(g, core, T, topo):
     total(w("WX"), w("PWT", 0, 16))
     for c in range(8):
         ts(w("WC", 8 * c, 8 * c + 8), w("G8"), w("WX"), O.mult, 3.0 ** (48 - 16 * c), O.mult)
-    ts(w("WBIG"), w("G8"), 1e29, O.mult)
 
     START = [310 * (t + 1) & 1023 for t in range(3)]
 
@@ -431,10 +494,10 @@ def rank_program(g, core, T, topo):
 
     for c in range(0, 1024, 256):
         ts(w("CI", c, c + 256), w("DET", c, c + 256), 255, O.bitwise_and)
-        ts(w("TC", c, c + 256), w("CI", c, c + 256), -128.0, O.add)
         for x, y, p in rot(0, c, c + 256):
-            act(w("QB", p, p + y - x), w("TC", x, y), F.Abs)
+            ts(w("QB", p, p + y - x), w("CI", x, y), 128.0, O.not_equal)
     for c in range(0, 1024, 256):
+        ts(w("TC", c, c + 256), w("CI", c, c + 256), -128.0, O.add)
         ts(w("TD", c, c + 256), w("DET", c, c + 256), -128.0, O.add, 1 / 256, O.mult)
 
     def whole(c, scale):
@@ -443,7 +506,7 @@ def rank_program(g, core, T, topo):
 
     def first_qt(c):
         whole(c, 1.0)
-        parts = [(w("P7", 0, 256), w("QW32"), w("TN", c, c + 256))]
+        parts = [(half("P7", h), w("QW32"), w("TN", c + 128 * h, c + 128 * h + 128)) for h in range(2)]
         parts += [(w("P7", x - c, y - c), w("R8"), w("QB", p, p + y - x)) for x, y, p in rot(0, c, c + 256)]
         group(parts)
         act(w("QT", c, c + 256), w("P7", 0, 256))
@@ -452,7 +515,7 @@ def rank_program(g, core, T, topo):
     near = [q for q in peers if T.cores[q] in topo.cores_of(core)]
     far = [q for q in peers if q not in near]
 
-    def send(sb, dst, rx):
+    def send(sb, dst, rx, rn):
         plan, used, share = [], [], []
         for i, q in enumerate(far):
             e = topo.engines(core, T.cores[q])
@@ -472,62 +535,68 @@ def rank_program(g, core, T, topo):
             for q, e in plan:
                 rid, pid = topo.addr(T.cores[q], core)
                 tf.append(RemoteDMATransfer(dst_ids=[DstId(rid=rid, pnc=pid)], dma_engine_mask=sum(1 << x for x in e),
-                                            remote_sem=T.sem[rx], src=T[sb][:, 256 * q:256 * q + 64],
+                                            remote_sem=T.sem[rn if q in near else rx], src=T[sb][:, 256 * q:256 * q + 64],
                                             dst=T[dst][:, 64 * me:64 * me + 64], alu_op=0))
             g.remote_dma_fused(tf, local_sem=T.sem["snd"])
-            semof[rx] = (rx, got)
-            note(rx, 1, [], writes)
-        calls.append(("g", emit, w(sb)[1], [r for q in peers for r in w(dst, 64 * q, 64 * q + 64)[1]], 0.5, 3.5))
+            for sem in sorted({rx, rn}):
+                mine = [(q, e) for q, e in plan if sem == (rn if q in near else rx)]
+                semof[sem] = (sem, sum(len(e) for q, e in mine))
+                note(sem, 1, [], [r for q, e in mine for r in w(dst, 64 * q, 64 * q + 64)[1]])
+        lands = lambda qs: [r for q in qs for r in w(dst, 64 * q, 64 * q + 64)[1]]
+        calls.append(("g", emit, w(sb)[1], lands(near) + [(rx, 1)], 0.5, NEAR))
+        calls.append(("x", lambda reads, writes: None, [(rx, 1)], lands(far), 0.0, FAR - NEAR))
         act(w(dst, 64 * me, 64 * me + 64), w(sb, 256 * me, 256 * me + 64))
         return got
 
     def wrap(p):
         group([(w(p, 0, 16), w("XF", 128 * h, 128 * h + 128), SEL[h]) for h in range(2)])
 
-    def half(n, h, p=128):
-        return w(n, 128 * h, 128 * h + 128, 1, p)
+    def ranks(end):
+        for k in range(8):
+            mm(w("P2", 8 * k, 8 * k + 8), w("QB", 128 * k, 128 * k + 128), w("G8"))
+        ts(w("LV"), w("P2", 0, 64), 0.0, O.is_gt)
+        mm(w("P5", 0, 64), w("TR2"), w("LV"), True, False)
+        for d in range(1, 8):
+            mm(w("P5", 8 * d, 64), w("TWOS"), w("LV", 0, 64 - 8 * d), False, end and d == 7)
 
     A = lambda n: w(n, 0, 256)
     sent = 0
     for t in range(3):
         IA, IB = "IA%d" % t, "IB%d" % t
-        if t:
-            for a, b, onv in ((0, 384, 0), (384, 704, 1), (704, 1024, 1)):
-                for x, y, p in rot(t, a, b):
-                    if onv:
-                        ts(w("QB", p, p + y - x), w("TC", x, y), 0.0, O.not_equal)
-                    else:
-                        act(w("QB", p, p + y - x), w("TC", x, y), F.Abs)
-        for k in range(8):
-            mm(w("P0", 8 * k, 8 * k + 8), w("QB", 128 * k, 128 * k + 128), w("G8"))
-        ts(w("LV"), w("P0", 0, 64), 0.0, O.is_gt)
-        group([(w("P1", 0, 64), w("TRX"), w("LV"))] + [(w("P1", 8 * d, 64), w("ONEB", 0, 128), w("LV", 0, 64 - 8 * d)) for d in range(1, 8)])
-        cp(w("R32"), w("P1", 0, 64))
-        ts(w("LOW"), w("R32"), 15, O.bitwise_and)
+        if t == 0:
+            ranks(True)
+        cp(w("R32"), w("P5", 0, 64))
+        ts(w("LOW"), w("R32"), 31, O.bitwise_and)
         for h in range(17):
-            act(bs(h=h), w("P1", 0, 64), F.Sign, 4096.5 - 16 * h)
-        for l in range(16):
-            ts(w("OL", l, 1024, 16), w("LOW"), float(l), O.is_equal)
+            act(bs(h=h), w("P5", 0, 64), F.Sign, 0.5 - 32 * h)
+        for d in range(2):
+            ts(w("LW2", d, 128, 2), w("LOW"), -2.0 * d, O.add)
+        for l in range(0, 16, 2):
+            x = (T["OL"][:, :, l:l + 2], [("OL", sum(3 << (16 * j + l) for j in range(64)))], [])
+            ts(x, w("LW2"), 2.0 * l + 1, O.is_equal)
         for k in range(8):
             c = (128 * k, 128 * k + 128)
-            ts(w("OA", *c), w("OL", *c), w("PA", 8 * t + k, 8 * t + k + 1), O.mult)
+            ts(w("OA", *c), (T["OL"][:, 8 * k:8 * k + 8, :], [("OL", ((1 << 128) - 1) << (128 * k))], []), w("PA", 8 * t + k, 8 * t + k + 1), O.mult)
         group([(w("P2", 0, 136), w("C128"), w("KD")), (w("P2", 0, 136), w("IDB"), w("DMB"))]
               + [(w("P2", 0, 136), w("OA", 128 * k, 128 * k + 128), bs(k=k)) for k in range(8)])
         if t:
-            scatter("TD", "FO", "IB%d" % (t - 1), 2)
+            scatter("TD", "FO", "IB%d" % (t - 1), PT)
         scan(w("LM"), w("RS8"), w("P2", 0, 136), 0.0, O.add, O.min)
+        if t and TB:
+            behind("tc%d" % (t - 1))
         tt(w("LD"), w("LM", 7, 128, 8), w("LM", 15, 136, 8), O.subtract)
         tt(w("GU"), w("LD"), w("SW"), O.min)
         cp(w("DU"), ind(w("TD"), w("GU")))
-        act(w("CN"), ind(w("TC"), w("GU")))
-        act(A("P3"), w("CN"), F.Abs)
-        CUT = [0, 48, 128, 192, 256]
+        act(w("AB"), ind(w("TC"), w("GU")), F.Abs)
+        mm(A("P3"), w("IDB"), w("AB"))
+        CUT = [0, HV0, 128, 192, 256]
 
         def look(a, b):
             return w("hv", 16 * a, 16 * b), ind(w("hamt"), w("DU", a, b))
         for j in range(1, 4):
             act(*look(CUT[j], CUT[j + 1]))
         cp(*look(CUT[0], CUT[1]))
+        act(w("CN"), ind(w("TC"), w("GU")))
         ts(w("DF"), w("DU"), -float(MID), O.add)
         for h in range(2):
             mm(w("P0", h, 32, 2), half("DF", h), w("WT"))
@@ -554,7 +623,10 @@ def rank_program(g, core, T, topo):
 
         def mins(a, b, h=None):
             for k in range(16):
-                tt(w("MK", 256 * k + a, 256 * k + b), w("hv", 16 * a + k, 16 * b, 16), w("P3", a, b), O.min)
+                x = w("hv", 16 * a + k, 16 * b, 16)
+                if a == CUT[3]:
+                    x = (x[0], x[1], w("HV")[1])
+                tt(w("MK", 256 * k + a, 256 * k + b), x, w("P3", a, b), O.min)
             if h is not None:
                 p = "P%d" % (1 + h)
                 group([(w(p, 0, 128), w("C128"), w("KC"))]
@@ -563,9 +635,13 @@ def rank_program(g, core, T, topo):
         mins(0, CUT[2], 0)
         mins(CUT[2], CUT[3])
         mins(CUT[3], CUT[4], 1)
-        act(w("ABF"), A("P3"), F.Relu, -1.0)
+        act(w("ABF"), w("AB"), F.Relu, -1.0)
         act(w("FB"), w("CN"), F.Identity, 191.625, 0.25)
         act(w("SGC"), w("CN"), F.Sign)
+        group([(A("P1"), w("QW"), w("DF")), (A("P1"), w("R8"), w("ABF"))])
+        act(w("QS"), A("P1"), F.Identity, w("QB0"))
+        group([(A("P2"), w("IDB"), w("CN")), (A("P2"), w("NEG"), w("SGC"))])
+        act(w("CFD"), A("P2"))
         tt(w("E3"), w("SCN", 15, 256, 16), w("HV"), O.add)
         cp(w("MX"), w("SCN", 15, 256, 16))
         tt(w("XK", 16, 272), ind(w("MX"), w("OC")), w("SCN"), O.is_equal)
@@ -597,7 +673,7 @@ def rank_program(g, core, T, topo):
         tt(w("PR"), w("I2", 0, 16), w("I2", 16, 32), O.mult)
         ts(w("OW"), w("PR"), 5, O.arith_shift_right, 3, O.bitwise_and)
         tt(w("OM"), ind(w("OW"), w("OW4")), w("QQ"), O.is_equal)
-        group([(w("P3", 64, 128), w("C128"), w("KS")), (w("P3", 64, 128), w("TRS"), w("OM")),
+        group([(w("P3", 64, 128), w("C128"), w("KS")), (w("P3", 64, 128), w("TRX"), w("OM")),
                (w("P3", 96, 128), w("ONEB", 0, 128), w("OM", 0, 32))])
         scan(w("SC2"), w("RS4"), w("P3", 64, 128), 0.0, O.add, O.min)
         tt(w("XF"), ind(w("SC2"), w("OL4")), w("MT"), O.min)
@@ -614,7 +690,7 @@ def rank_program(g, core, T, topo):
             mm(half("P5", h), w("SH%d" % h, 0, 128, 1, 32), w("R4", 0, 128, 1, 32), False, h == 1)
         act(w("REC"), A("P5"), F.Identity, w("QB0"))
         scatter("SA%d" % t, "OFF", "REC")
-        sent += send("SA%d" % t, IA, "ra%d" % t)
+        sent += send("SA%d" % t, IA, "ra%d" % t, "rn%d" % t)
         group([(A("P1"), w("IDB"), w("CH")), (A("P1"), w("NEG"), w("DF"))])
         act(w("SGN"), A("P1"), F.Sign)
         mm(A("P2"), w("BLK"), w("SGN"))
@@ -624,87 +700,191 @@ def rank_program(g, core, T, topo):
         group([(A("P6"), w("IDB"), w("CH")), (A("P6"), w("IQ"), w("CA"))])
         act(w("ED"), A("P6"), F.Identity, MID - 0.5)
         scatter("SB%d" % t, "OFF", "ED")
-        sent += send("SB%d" % t, IB, "rb%d" % t)
-        group([(A("P2"), w("IDB"), w("CN")), (A("P2"), w("NEG"), w("SGC"))])
-        act(w("CFD"), A("P2"))
-        group([(A("P7"), w("QW"), w("DF")), (A("P7"), w("R8"), w("ABF"))])
-        act(w("QS"), A("P7"), F.Identity, w("QB0"))
+        sent += send("SB%d" % t, IB, "rb%d" % t, "rb%d" % t)
         if t:
-            scatter("QT", "FO", "QN", 2)
-        scatter("QT", "GU", "QS", 2)
+            scatter("QT", "FO", "QN", PQ)
+        scatter("QT", "GU", "QS", PQ)
         scatter("TC", "GU", "CFD", 2)
-        for h in range(2):
-            mm(w("P1", 16 * h, 16 * h + 16), half(IA, h), w("SHU"))
-        for r in range(16):
-            ts(w("XB", r, 512, 16), w("P1", 0, 32), w("MR", r, r + 1), O.mult)
-        for c in range(2):
-            p, z = w("P%d" % (3 + c), 0, 80), (80 * c, 80 * c + 80)
-            group([(p, w("C128"), w("KZ", 0, 80))]
-                  + [(p, w("XB", 128 * j, 128 * j + 128), w("ZW", 160 * j + 80 * c, 160 * j + 80 * c + 80)) for j in range(4)])
-            ts(w("RZ", *z), p, -511.5, O.add)
-            tt(w("ZU", *z), p, w("RZ", *z), O.subtract)
-        mm(w("P5", 0, 320), w("C128"), w("KA"), True, False)
-        mm(w("P5", 0, 320), w("C128"), w("KB"), False, False)
-        for h in range(2):
-            mm(w("P5", 160 * h, 160 * h + 160), half(IA, h), w("KW"), False, False)
         if t == 2:
             for c in range(0, 1024, 256):
-                group([(A("P2"), w("I32"), w("TN", c, c + 256)), (A("P2"), w("IDB"), w("TC", c, c + 256))])
+                group([(A("P2"), w("IDB"), w("TC", c, c + 256))]
+                      + [(half("P2", h), w("I32"), w("TN", c + 128 * h, c + 128 * h + 128)) for h in range(2)])
                 act(w("YT", c, c + 256), A("P2"), F.Identity, 128.0)
-        NV = 3
-        for m in range(NV, 10):
-            act(w("PR5", 256 * (m - NV), 256 * (m - NV + 1)), ind(w("QT", 0, 1024), w("ZU", 16 * m, 16 * m + 16)))
-        act(A("P0"), w(IA))
-        for m in range(10):
-            o = w("CMP", 256 * m, 256 * m + 256)
-            if m < NV:
-                tt(o, ind(w("QT", 0, 1024), w("ZU", 16 * m, 16 * m + 16)), w(IA), O.is_equal)
-            else:
-                tt(o, w("PR5", 256 * (m - NV), 256 * (m - NV + 1)), A("P0"), O.is_equal)
+        hn, hf = me // 2, min(far) // 2
+        KEY, BRO = {hn: "P5", hf: "P7"}, {hn: "P0", hf: "P1"}
+        sets = [(64 * me, 64), (64 * near[0], 64), (128 * hf, 128)]
+        for a, n in sets:
+            k, o = n // 2, a * 10 // 16
+            ts(w("IH", a, a + n), w(IA, a, a + n), 2000.0, O.min)
+            pa, pb = ("P4", "P6") if n == 128 else ("P4", "P4") if a == 64 * me else ("P3", "P3")
+            one = [(w(pa, 0, k), w("ZA", 16 - 8 * u, 144 - 8 * u), w("IH", a + u, a + n, 2)) for u in range(2)]
+            two = [(w(pb, k, k + n // 8), w("ZB", 16 - 2 * u, 144 - 2 * u), w("IH", a + u, a + n, 8)) for u in range(8)]
+            for p, x, y, parts in ([(pa, 0, k + n // 8, one + two)] if pa == pb else [(pa, 0, k, one), (pb, k, k + n // 8, two)]):
+                group([(w(p, x, y), w("C128"), w("KZ", x, y))] + parts)
+                ts(w("RZ", o + x, o + y), w(p, x, y), -511.5, O.add)
+                tt(w("ZU", o + x, o + y), w(p, x, y), w("RZ", o + x, o + y), O.subtract)
+        for h in (hn, hf):
+            p = w(KEY[h], 0, 160)
+            mm(p, w("C128"), w("KA"), True, False)
+            mm(p, w("C128"), w("KB"), False, False)
+            mm(p, half("IH", h), w("KW"), False, False)
+
+        def probe(a, x, y):
+            o = a * 10 // 16
+            return w("PR5", 16 * (o + x), 16 * (o + y)), ind(w("QT", 0, 1024), w("ZU", o + x, o + y))
+
+        def same(a, n, m, x, y):
+            b, st = (10 * a + m, 8) if m < 8 else (10 * a + 8 * n + m - 8, 2)
+            tt(w("CMP", 256 * m + a + x, 256 * m + a + y), w("PR5", b + st * x, b + st * (y - 1) + 1, st),
+               w(BRO[a // 128], a % 128 + x, a % 128 + y), O.is_equal)
+
+        def key(h, m, end):
+            mm(w(KEY[h], m, 160, 10), w("CMP", 256 * m + 128 * h, 256 * m + 128 * h + 128), w("RW"), False, end)
+
+        def place(h):
+            c, ky = (8 * h, 8 * h + 8), w("KY", 160 * h + 19, 160 * h + 160, 20)
+            scan(w("KY", 160 * h, 160 * h + 160), w("RSK", 160 * h, 160 * h + 160), w(KEY[h], 0, 160), 0.0, O.max, O.min)
+            ts(w("RK", *c), ky, -7.9921875, O.add, YCAP, O.min)
+            tt(w("PL16", *c), ky, w("RK", *c), O.subtract)
+            tt(w("PL", *c), ky, w("RK", *c), O.subtract)
+            mm(w(KEY[h], 0, 128, 1, 8), w("PL16", *c), w("IDB"))
+            tt(half("XF", h), ind(w("PL", *c), w("OC", 0, 8)), w("M64", 0, 128), O.mult)
+            cp(half("R6", h, 8), w(KEY[h], 0, 128, 1, 8))
+            mm(w("P4", *c), half("XF", h), w("G8"))
+            mm(w(BRO[h], 0, 128), w("SS", 0, 128, 1, 8), half("R6", h, 8))
+            cp(w("PW", *c), w("P4", *c))
+            cp(half("PU", h), w(BRO[h], 0, 128))
+            cp(w("PO", *c), w("P4", *c))
+            act(half("CO", h), ind(w("TC"), w("PO", *c)))
+            if t < 2 and (DIG or h == hf):
+                c = c if DIG else (0, 16)
+                ts(w("PN", *c), w("PL", *c), 64.0, O.mult, 1024.0 - START[t + 1], O.add)
+                ts(w("PM", *c), w("PN", *c), 127, O.bitwise_and)
+                ts(w("KJ", *c), w("PN", *c), 7, O.arith_shift_right, 7, O.bitwise_and)
+                ts(w("NB", *c), w("PM", *c), -1.0, O.mult)
+                for j in range(*c):
+                    act(w("TH", 128 * j, 128 * j + 128), w("IO"), F.Sign, w("NB", j, j + 1))
+
+        def first(hc, hj, end=False):
+            for c in range(8 * hc, 8 * hc + 8):
+                x = w("MK", 256 * c + 128 * hj, 256 * c + 128 * hj + 128)
+                ts(x, half("PU", hj), w("PW", c, c + 1), O.is_equal)
+                mm(w("P3", 8 * hj, 8 * hj + 8), x, w("WC", 8 * (c % 8), 8 * (c % 8) + 8) if hc == hj else w("WBIG"), False,
+                   end and c % 8 == 7)
+        for a, n in sets[:2]:
+            act(w(BRO[hn], a % 128, a % 128 + n), w(IA, a, a + n))
+            act(*probe(a, 0, 40))
+            for m in range(10):
+                same(a, n, m, 0, n)
+                if a != 64 * me:
+                    key(hn, m, m == 9)
+        a, n = sets[2]
+        act(w(BRO[hf], 0, n), w(IA, a, a + n))
+        act(*probe(a, 0, 32))
+        act(*probe(a, 32, FS))
+        cp(*probe(a, FS, 80))
+        mm(w("P3", 0, 16), w("IDB"), w("Z16"), True, False)
+        if SPLIT:
+            place(hn)
+        for m in range(8):
+            same(a, n, m, 0, 64)
+        for m in (8, 9):
+            same(a, n, m, 0, 128)
+            key(hf, m, False)
+        for m in range(8):
+            same(a, n, m, 64, 128)
+            key(hf, m, m == 7)
+        if SPLIT:
+            first(hn, hn)
+            place(hf)
+            first(0, 1)
+            first(hf, hf, True)
+        else:
+            ky = w("KY", 19, 320, 20)
+            for h in (hn, hf):
+                scan(w("KY", 160 * h, 160 * h + 160), w("RSK", 160 * h, 160 * h + 160), w(KEY[h], 0, 160), 0.0, O.max, O.min)
+            ts(w("RK"), ky, -7.9921875, O.add, YCAP, O.min)
+            tt(w("PL16"), ky, w("RK"), O.subtract)
+            tt(w("PL"), ky, w("RK"), O.subtract)
+            mm(w("P7", 0, 128, 1, 16), w("PL16"), w("IDB"))
+            tt(w("XF"), ind(w("PL"), w("OC")), w("M64"), O.mult)
+            cp(half("R6", 0, 16), w("P7", 0, 128, 1, 16))
+            wrap("P4")
             for h in range(2):
-                mm(w("P5", 160 * h + m, 160 * h + 160, 10), w("CMP", 256 * m + 128 * h, 256 * m + 128 * h + 128), w("RW"),
-                   False, m == 9 and h == 1)
+                mm(half("P0", h), w("SS1" if h else "SS", 0, 128, 1, 16), half("R6", 0, 16))
+            cp(w("PO"), w("P4", 0, 16))
+            cp(w("PW"), w("P4", 0, 16))
+            cp(w("PU"), A("P0"))
+            act(w("CO"), ind(w("TC"), w("PO")))
+            if t < 2:
+                ts(w("PN"), w("PL"), 64.0, O.mult, 1024.0 - START[t + 1], O.add)
+                ts(w("PM"), w("PN"), 127, O.bitwise_and)
+                ts(w("KJ"), w("PN"), 7, O.arith_shift_right, 7, O.bitwise_and)
+                ts(w("NB"), w("PM"), -1.0, O.mult)
+                for j in range(16):
+                    act(w("TH", 128 * j, 128 * j + 128), w("IO"), F.Sign, w("NB", j, j + 1))
+            for c in range(16):
+                a = 32 * (c // 2) if c < 8 else 128
+                x = w("PU", a, 256)
+                if t < 2 and c >= FK:
+                    x = (x[0], x[1], w("NB")[1])
+                ts(w("MK", 256 * c + a, 256 * c + 256), x, w("PW", c, c + 1), O.is_equal)
+                wc = w("WC", 8 * (c % 8), 8 * (c % 8) + 8)
+                for x, y in ([(a, 128)] if a in (0, 64, 96) else [(32, 64), (64, 128)] if a == 32 else []):
+                    mm(w("P3", 0, 8, 1, y, x), w("MK", 256 * c + x, 256 * c + y), wc, False, False)
+                mm(w("P3", 8, 16), w("MK", 256 * c + 128, 256 * c + 256), wc if c > 7 else w("WBIG"), False, c == 15)
         act(w("AT"), w(IB), F.Identity, MAG)
-        act(w("NA"), w("AT"), F.Identity, MAG, -1.0)
-        mm(A("P6"), w("I256"), w(IB), True, False)
-        mm(A("P6"), w("I256"), w("NA"), False, False)
-        scan(w("KY"), w("RSK"), w("P5", 0, 320), 0.0, O.max, O.min)
-        ts(w("RK"), w("KY", 19, 320, 20), -7.9921875, O.add, YCAP, O.min)
-        tt(w("PL16"), w("KY", 19, 320, 20), w("RK"), O.subtract)
-        tt(w("PL"), w("KY", 19, 320, 20), w("RK"), O.subtract)
-        mm(w("P7", 0, 128, 1, 16), w("PL16"), w("IDB"))
-        tt(w("XF"), ind(w("PL"), w("OC")), w("M64"), O.mult)
-        cp(w("R6", 0, 128, 1, 16), w("P7", 0, 128, 1, 16))
-        wrap("P1")
-        for h in range(2):
-            mm(half("P0", h), w("SS%d" % h, 0, 128, 1, 16), w("R6", 0, 128, 1, 16))
-        cp(w("PW"), w("P1", 0, 16))
-        cp(w("PU"), A("P0"))
-        cp(w("PO"), w("PW"))
-        act(w("CO"), ind(w("TC"), w("PO")))
-        mm(A("P6"), w("IDB"), w("CO"), False, True)
+        if CQV:
+            act(A("P6"), w("AT"), F.Identity, MAG, -1.0)
+            tt(w("CQ"), w(IB), A("P6"), O.add)
+            group([(A("P6"), w("I2B"), w("CQ"))] + [(half("P6", h), w("IDB"), half("CO", h)) for h in (hn, hf)])
+        else:
+            act(w("NA"), w("AT"), F.Identity, MAG, -1.0)
+            group([(half("P6", h), w("I256"), half(x, h)) for h in range(2) for x in (IB, "NA")]
+                  + [(half("P6", h), w("IDB"), half("CO", h)) for h in (hn, hf)])
+        if t < 2:
+            act(w("ABN"), A("P6"), F.Abs)
         ts(w("CNW"), A("P6"), 127.0, O.min, -127.0, O.max)
         if t < 2:
-            act(w("ABN"), w("CNW"), F.Abs)
-            group([(A("P2"), w("I32"), w(IA)), (A("P2"), w("R8"), w("ABN"))])
-            act(w("QN"), A("P2"))
-        else:
-            act(A("P2"), w("NA"), F.Identity, 128.0, -256.0)
-            tt(w("YN"), w("CNW"), A("P2"), O.add)
-        mm(w("P3", 0, 16), w("IDB"), w("Z16"), True, False)
-        for c in range(16):
-            a = 0 if c < 8 else 128
-            ts(w("MK", 256 * c + a, 256 * c + 256), w("PU", a, 256), w("PW", c, c + 1), O.is_equal)
-            wc = w("WC", 8 * (c % 8), 8 * (c % 8) + 8)
-            if c < 8:
-                mm(w("P3", 0, 8), w("MK", 256 * c, 256 * c + 128), wc, False, False)
-            mm(w("P3", 8, 16), w("MK", 256 * c + 128, 256 * c + 256), wc if c > 7 else w("WBIG"), False, c == 15)
+            for a in range(0, 1024, 256):
+                for x, y, p in rot(t + 1, a, a + 256):
+                    act(w("QB", p, p + y - x), w("TC", x, y), F.Abs)
+            ranks(False)
+            ky = w("KY", 19, 320, 20)
+            ts(w("VAL"), ky, YCAP, O.is_lt)
+            ts(w("OLD"), ky, Y0 + 2560, O.is_lt)
+            tt(w("AK", 0, 128), ind(w("KJ"), w("OD", 0, 8)), w("KI"), O.is_equal)
+            tt(w("AK", 128, 256), ind(w("KJ"), w("OD", 0, 8)), w("KI"), O.is_le)
+            for h in range(2):
+                mm(w("P4", 16 + 8 * h, 24 + 8 * h), half("ABN", h), w("G8"))
+            tt(w("NL"), w("P4", 16, 32), w("VAL"), O.min)
+            tt(w("D0"), w("NL"), w("OLD"), O.subtract)
+            ts(w("WIN"), w("P3", 0, 16), w("THR"), O.is_lt)
+            tt(w("DW"), w("WIN"), w("D0"), O.mult)
+            tt(w("DK"), ind(w("DW"), w("OD")), w("AK"), O.mult)
         ts(w("LO"), w("P3", 0, 16), w("THR"), O.is_ge)
         tt(w("XF"), ind(w("LO"), w("OC")), w("MT"), O.mult)
         wrap("P4")
+        mark("wrap%d" % t)
         tt(w("FO"), w("P4", 0, 16), w("PW"), O.max)
         if t < 2:
-            scatter("TC", "FO", "CNW")
+            for h in range(2):
+                mm(w("P5", 0, 64), w("MONE"), w("DK", 64 * h, 64 * h + 64), False, False)
+                mm(w("P5", 0, 64), w("TWOS"), w("DK", 128 + 64 * h, 192 + 64 * h), False, False)
+            for j in range(16):
+                h, gg = j // 8, j % 8
+                mm(w("P5", gg, 64, 8), w("TH", 128 * j, 128 * j + 128), w("DK", 64 * h + gg, 64 * h + 64, 8), False, j == 15)
+                if j == WR:
+                    behind("wrap%d" % t)
+            group([(half("P2", h), w("I32"), half(IA, h)) for h in range(2)] + [(A("P2"), w("R8"), w("ABN"))])
+            act(w("QN"), A("P2"))
+        else:
+            act(w("NA"), w("AT"), F.Identity, MAG, -1.0)
+            act(A("P2"), w("NA"), F.Identity, 128.0, -256.0)
+            tt(w("YN"), w("CNW"), A("P2"), O.add)
+        if t < 2:
+            scatter("TC", "FO", "CNW", PT)
+            mark("tc%d" % t)
         else:
             scatter("YT", "FO", "YN")
             dma("d", T.y[:, :], T["YT"][:, 0:1024], "st0", w("YT", 0, 1024)[1], [], 4.0)

@@ -1,27 +1,30 @@
 from concourse.bass import DstId, RemoteDMATransfer
 from concourse.mybir import AluOpType as O, ActivationFunctionType as F, AxisListType as AX
 
-TURNS, JOLT, SPAN, HV0, DIG, FS, CQV, PQ = 600, 1.0, 5.0, 60, 1, 60, 1, 4
-SPLIT, FK, WR, PT, TB = 0, 8, 6, 2, 1
+TURNS, JOLT, SPAN, HV0, DIG, FS, CQV, PQ = 4000, 0.5, 0.1, 60, 1, 60, 1, 4
+NX, WR, PT, TB = 0, 99, 2, 1
+YV, TS, XD, FV = 1024, 0, 1, 0
+DUP, PF, PG, TE = ((0, 16),), 1, 2, 0
+PIECES = [0, 304, 608, 896, 1024]
 ORDER = {}
-WAKE, NEAR, FAR = 0.15, 3.0, 3.0
+WAKE, NEAR, FAR = 0.18, 2.1, 2.1
 F32, BF, I32, U16, F16 = "float32", "bfloat16", "int32", "uint16", "float16"
 BUFS = {
     F32: dict(TD=1536, QT=1536, TM=1024, TN=1024, YT=1280, ONE=160, I32=128, I256=128, QW32=128, SW=16, MR=16,
               PA=24, RC=1, QB0=1, BN=1, BP=1, THR=1, WX=1, PW3=128, PWT=128, Z128=128, M64=256, MT=256, JC=2, RS8=136, RS16=256,
-              RS4=64, RSK=320, QC=64, HK=32, LM=136, LD=16, DP=256, DN=256, SCN=256, HI=256, CT=256, HV=16, MX=16, VX=16, VD=16, QQ=64,
+              RS4=64, RSK=320, QC=64, HK=32, LM=136, LD=16, LE=16, DP=256, DN=256, SCN=256, HI=256, CT=256, HV=16, MX=16, VX=16, VD=16, QQ=64,
               SC2=64, REC=256, ED=256, QS=256, QN=256, AT=256, NA=256, KY=320, PL=16, PW=16, LO=16, YN=256, PR5=2560,
-              RC8=1, KI=128, NB=16, VAL=16, OLD=16, NL=16, D0=16, WIN=16, DW=16, AK=256,
-              SA0=1280, SA1=1280, SA2=1280, SB0=1280, SB1=1280, SB2=1280, IA0=256, IA1=256, IA2=256, IB0=256, IB1=256, IB2=256),
+              RC8=1, NB=16, VAL=16, OLD=16, NL=16, D0=16, WIN=16, DW=16, AK=256,
+              SA0=1280, SA1=1280, SA2=1280, SB0=1024, SB1=1024, SB2=1024, IA0=256, IA1=256, IA2=256, IB0=256, IB1=256, IB2=256),
     BF: dict(TC=1536, ham=3584, ONEB=320, G8=8, G16=8, GM8=8, TRX=128, TRS=128, IDB=128, NEG=128, IBG=128, I2B=128, IQ=128, BLK=128,
              KC=128, KD=136, DMB=136, C128=128, BL=128, R8=128, QW=128, SHP=128, SHN=128, WT=16, WC=128, WBIG=8, ZG=24, ZA=144,
              ZB=144, ZX=128, KW=160, KX=160, AB=256, SS=128, SS1=128, SH0=128, SH1=128, RW=16, KA=160, KB=160, KS=64, KZ=80, Z16=16, QB=1024, LV=64, OL=1024,
              CN=256, hv=4096, MK=4096, XK=272, AE=256, SG=256, SGN=256, RN=256, FB=256, CA=256, OM=64, SGC=256, CFD=256, ABF=256,
-             ABN=256, CMP=2560, RZ=160, CO=256, CQ=256, CNW=256, TR2=128, TWOS=128, MONE=128, IO=128, TH=2048, LW2=128, DK=256),
-    I32: dict(DET=1024, CI=1024, PI=16, PJ=1, PK=24, PLI=24, EI=4, EJ=4, EK=4, XI=16, R32=64, LOW=64, E3=16, VV=16, H1=32, H2=32,
+             ABN=256, CMP=2560, RZ=160, CO=256, CQ=256, CNW=256, TR2=128, TWOS=128, SD0=1024, SD1=1024, SD2=1024, KF=16, SQ=128, IO=256, R11=128, ZC=144, KQ=16, TH=2048, LW2=128, R32=64, DK=256),
+    I32: dict(DET=1024, CI=1024, PI=16, PJ=1, PK=24, PLI=24, EI=4, EJ=4, EK=4, XI=16, E3=16, VV=16, H1=32, H2=32,
               HP=16, I1=32, I2=32, PR=16, OW=16, HS=32, EL=16, EM=1, PN=16, PM=16, KJ=16),
-    F16: dict(OA=1024, DF=256, VB=256, CH=256, XF=256, T16=32, R4=128, IH=256, RK=16, PL16=16, R6=256, PU=256),
-    U16: dict(GU=16, DU=256, OFF=16, ZU=160, PO=16, FO=16, OC=16, OL4=16, OQ=4, OW4=4, OD=16),
+    F16: dict(OA=1024, DF=256, VB=256, CH=256, XF=256, T16=32, R4=128, IH=256, KU=64, RK=16, PL16=16, R6=256, PU=256),
+    U16: dict(GU=16, DU=256, OFF=16, ZU=160, PO=16, FO=16, OC=16, OL4=16, OQ=4, OW4=4, OD=16, OI=16, GS=16),
 }
 SCRATCH, WIDTH, WHERE = {}, {}, {}
 for _d in BUFS:
@@ -38,13 +41,14 @@ for _d in BUFS:
         SCRATCH["small_" + _d] = ("sbuf", [128, _p], _d)
 SCRATCH["BS"] = ("sbuf", [128, 8, 17, 8], BF)
 SCRATCH["OL"] = ("sbuf", [128, 64, 16], BF)
+SCRATCH["SK"] = ("sbuf", [128, 2, 8, 8], BF)
 TWO = list(BUFS[F16]) + list(BUFS[BF]) + list(BUFS[U16])
 PSUM = ["P%d" % _k for _k in range(8)]
 for _n in PSUM:
     WIDTH[_n] = 512
     SCRATCH[_n] = ("psum", [128, 512], F32)
 SEMAPHORES = ["qv", "qs", "qt", "qg", "ld0", "ld1", "ld2", "ld3", "ld4", "st0", "snd"]
-SEMAPHORES += [_n + str(_t) for _n in ("ra", "rn", "rb") for _t in range(3)]
+SEMAPHORES += [_n + str(_t) for _n in ("ra", "rn", "rb", "rc") for _t in range(3)]
 W1 = [13 * _i + 5 for _i in range(16)]
 W2 = [255 - 14 * _i for _i in range(16)]
 MID = 1792
@@ -78,6 +82,13 @@ def rank_program(g, core, T, topo):
         if h is None:
             return (T["BS"][:, k, :, :], [("BS", ((1 << 136) - 1) << (136 * k))], [])
         return (T["BS"][:, :, h, :], [("BS", sum(255 << (136 * j + 8 * h) for j in range(8)))], [])
+
+    def sk(k=None, h=None):
+        if h is not None:
+            return (T["SK"][:, h, :, :], [("SK", (1 << 64) - 1 << 64 * h)], [])
+        if k is None:
+            return (T["SK"][:, :, :, :], [("SK", (1 << 128) - 1)], [])
+        return (T["SK"][:, :, k, :], [("SK", (255 | 255 << 64) << 8 * k)], [])
 
     def ind(win, off):
         return (win[0].indirect(off[0]), win[1], off[1], 16 * off[1][0][1].bit_count())
@@ -190,64 +201,90 @@ def rank_program(g, core, T, topo):
             way[j] = 1e6 - j
 
         def lay(order, before, back):
-            start, busy = [0.0] * n, {}
+            start, busy = [0.0] * n, {q: ([], []) for q in set(queue)}
             for j in order:
-                q, c = calls[j][0], calls[j][4]
-                s = max([start[i] + calls[i][4] + calls[j if back else i][5] + wk for i, wk in before[j]]
-                        + [calls[j][5] if back else 0.0])
-                b = busy.setdefault(q, [])
-                lo, hi = 0, len(b)
-                while lo < hi:
-                    mid = (lo + hi) // 2
-                    lo, hi = (mid + 1, hi) if b[mid][1] <= s else (lo, mid)
-                while lo < len(b) and b[lo][0] < s + c - 1e-9:
-                    s = max(s, b[lo][1])
+                s, c = lat[j] if back else 0.0, cost[j]
+                for i, d in before[j]:
+                    if start[i] + d > s:
+                        s = start[i] + d
+                bs, be = busy[queue[j]]
+                m = lo = len(bs)
+                while lo and be[lo - 1] > s:
+                    lo -= 1
+                while lo < m and bs[lo] < s + c - 1e-9:
+                    if be[lo] > s:
+                        s = be[lo]
                     lo += 1
-                b.insert(lo, (s, s + c))
+                if lo and s - be[lo - 1] < 1e-9:
+                    be[lo - 1] = s + c
+                else:
+                    bs.insert(lo, s)
+                    be.insert(lo, s + c)
                 start[j] = s
             return start
+        queue, cost, lat = [[c[i] for c in calls] for i in (0, 4, 5)]
+        fore = [[(i, cost[i] + lat[i] + wk) for i, wk in prev[j]] for j in range(n)]
+        aft = [[(k, cost[k] + lat[j] + wk) for k, wk in succ[j]] for j in range(n)]
+        last_calls = [j for j in range(n) if not succ[j]]
+
         def forth(key):
-            start = lay(sorted(range(n), key=lambda j: (j >= 5, key[j] if j >= 5 else 0.0, j)), prev, False)
-            return max(start[j] + calls[j][4] + calls[j][5] for j in range(n)), start
+            key[:5] = [-1e6] * 5
+            start = lay([j for k, j in sorted(zip(key, range(n)))], fore, False)
+            return max(start[j] + cost[j] + lat[j] for j in last_calls), start
 
         def back(start):
-            late = lay(sorted(range(n), key=lambda j: (-start[j] - calls[j][4], -j)), succ, True)
+            late = lay(sorted(range(n), key=lambda j: (-start[j] - calls[j][4], -j)), aft, True)
             end = max(late[j] + calls[j][4] for j in range(n))
             return [end - late[j] - calls[j][4] for j in range(n)]
         kind = me // 2
+        if 0 in ORDER and kind not in ORDER:
+            at = {j: i for i, j in enumerate(ORDER[0])}
+            if all(at[i] < at[j] for j in range(n) for i, wk in prev[j]):
+                ORDER[kind] = ORDER[0]
         if kind not in ORDER:
             best = forth([-x for x in way])
-            base, seed = back(best[1]), 1
+            best = min(best, forth(back(best[1])))
+            now, seed, held = best, 1, None
             for turn in range(TURNS):
+                start = now[1]
+                if held is None:
+                    ends = {(calls[j][0], round(start[j] + calls[j][4], 6)): j for j in range(n)}
+                    held, j = [], max(range(n), key=lambda j: start[j] + calls[j][4] + calls[j][5])
+                    while start[j] > 0:
+                        ready, i = max([(start[i] + calls[i][4] + calls[i][5] + wk, i) for i, wk in prev[j]] + [(0.0, -1)])
+                        if ready < start[j] - 1e-6:
+                            held.append((j, ready))
+                            i = ends[(calls[j][0], round(start[j], 6))]
+                        j = i
                 seed = seed * 48271 % 2147483647
-                t0, key = seed % 1000 / 1000 * best[0], list(base)
-                if turn % 3 == 0:
-                    for j in range(n):
-                        if turn and t0 - SPAN < base[j] < t0:
-                            key[j] += JOLT * ((j + seed) * 2654435761 % 1009) / 1009
+                key = list(start)
+                if turn % 50 == 49 or not held:
+                    key = back(start)
                 else:
-                    j0 = seed // 1000 % n
-                    key[j0] += (JOLT * 2 * (seed // 7 % 101) / 100) * (1 if turn % 3 == 1 else -1)
-                    todo = [j0] if turn % 3 == 2 else []
-                    while todo:
-                        j = todo.pop()
-                        for i, wk in prev[j]:
-                            if key[i] > key[j]:
-                                key[i] = key[j]
-                                todo.append(i)
-                for j in range(n):
-                    kj = key[j]
-                    for k, wk in succ[j]:
-                        if key[k] < kj:
-                            key[k] = kj
+                    j0, ready = held[seed // 3 % len(held)]
+                    if seed % 3:
+                        key[j0] = ready - JOLT * (seed // 7 % 101) / 100
+                        todo = [j0]
+                        while todo:
+                            j = todo.pop()
+                            for i, wk in prev[j]:
+                                if key[i] > key[j]:
+                                    key[i] = key[j]
+                                    todo.append(i)
+                    else:
+                        ahead = [i for i in range(n) if calls[i][0] == calls[j0][0] and ready < start[i] + calls[i][4] and start[i] < start[j0]]
+                        todo = [ahead[seed // 7 % len(ahead)]]
+                        key[todo[0]] = start[j0] + JOLT * (seed // 11 % 101) / 100
+                        while todo:
+                            j = todo.pop()
+                            for k, wk in succ[j]:
+                                if key[k] < key[j]:
+                                    key[k] = key[j]
+                                    todo.append(k)
                 new = forth(key)
-                if new[0] <= best[0]:
-                    best, base = new, key
-                if turn % 20 == 19:
-                    key = back(best[1])
-                    new = forth(key)
-                    if new[0] <= best[0]:
-                        best, base = new, key
+                if new[0] <= now[0] + SPAN * (1 - turn / TURNS) * (seed // 13 % 97) / 97:
+                    now, held = new, None
+                    best = min(best, now)
             ORDER[kind] = sorted(range(n), key=lambda j: (best[1][j], j))
         order = ORDER[kind]
         for j in order:
@@ -327,15 +364,18 @@ def rank_program(g, core, T, topo):
         E("g", lambda: g.affine_select(out=o[0], in_=a[0], pattern=pat, compare_op=op, fill=other, base=base, channel_multiplier=cm),
           [a], [o], 0.17 + 2 * CY * wide(o))
 
-    def scatter(win, off, data, parts=1):
+    def scatter(win, off, data, parts=1, after=None):
         n = 16 // parts
         for i in range(parts):
             cp(ind(w(win), w(off, n * i, n * i + n)), w(data, 16 * n * i, 16 * n * (i + 1)))
+            if after:
+                behind(after)
 
     for c in range(4):
-        x = w("DET", 256 * c, 256 * c + 256)
-        dma("d", x[0], T.det[:, 256 * c:256 * c + 256], "ld%d" % c, [], x[1], 2.5 + 0.6 * c)
-    dma("d", T["hamt"][:, :], T.ham[:, :], "ld4", w("DET", 512, 768)[1], w("hamt")[1], 6.0)
+        a, b = PIECES[c:c + 2]
+        x = w("DET", a, b)
+        dma("d", x[0], T.det[:, a:b], "ld%d" % c, [], x[1], 2.0 + b / 400 - 0.1 * c)
+    dma("d", T["hamt"][:, :], T.ham[:, :], "ld4", [], w("hamt")[1], 9.0)
 
     BIG, KB, Y0, MAG = 8192.0, 16384.0, 16640.0, 12582912.0
     YCAP = Y0 + 256 * 20
@@ -351,7 +391,7 @@ def rank_program(g, core, T, topo):
     for t in range(3):
         iota(w("PK", 8 * t, 8 * t + 8), [[128, 8]], 310 * (t + 1), 1)
     iota(w("PI"), [[-1, 16]], 16, 1)
-    iota(w("KD"), [[-2048, 17], [0, 8]], 0, 0)
+    iota(w("KD"), [[-1280, 17], [0, 8]], 0, 0)
     aff(w("DMB"), w("DMB"), [[0, 17], [-16, 8]], O.is_ge, 0, 1, 262144.0)
     aff(w("DMB"), w("DMB"), [[0, 17], [16, 8]], O.is_ge, 15, -1, 262144.0)
     iota(w("SW"), [[16, 16]], 1280, 0)
@@ -362,9 +402,10 @@ def rank_program(g, core, T, topo):
     ts(w("TR2"), w("TRS"), 2.0, O.mult)
     tt(w("TR2"), w("TR2"), w("IDB"), O.add)
     fill(w("TWOS"), 2.0)
+    fill(w("KU"), 6128.0)
     times(w("NEG"), w("IDB"), -1.0)
     ts(w("PLI"), w("PK"), 1023, O.bitwise_and)
-    ts(w("PA"), w("PLI"), -2048.0, O.add, 0.5, O.mult)
+    ts(w("PA"), w("PLI"), -1280.0, O.add, 0.5, O.mult)
     ts(w("PI"), w("PI"), 15, O.bitwise_and)
     ts(w("MR"), w("PI"), 0.0, O.is_equal)
     ts(w("PJ"), w("PJ"), 15, O.bitwise_and)
@@ -426,13 +467,15 @@ def rank_program(g, core, T, topo):
     ts(w("EK"), w("EI"), 3, O.arith_shift_right)
     ts(w("EJ"), w("EJ"), 2.0, O.mult)
     tt(w("OW4"), w("EJ"), w("EK"), O.add)
-    iota(w("EL"), [[0, 2], [8, 2], [0, 4]], 0, 0)
     ts(w("EM"), w("PJ"), 7, O.bitwise_and)
     cp(w("RC8"), w("EM"))
-    ts(w("OD"), w("EL"), w("RC8"), O.add)
-    iota(w("KI"), [[0, 2], [1, 8], [0, 8]], 0, 0)
-    iota(w("IO"), [[1, 128]], 0, 0)
-    sfill(w("MONE"), -1.0)
+    ts(w("OD"), w("ONE", 0, 16), w("RC8"), O.mult)
+    iota(w("IO"), [[1, 256]], 0, 0)
+    fill(w("R11"), 0.0)
+    fill(w("R11", 11, 128, 16), 1 / 128)
+    fill(w("ZC", 0, 16), 0.0)
+    aff(w("ZC", 16, 144), w("ONEB", 0, 128), [[-16, 8], [128, 16]], O.is_equal, -11, 1)
+    iota(w("KQ"), [[256, 4], [0, 4]], 0, 0)
     ts(w("M64", 0, 16), w("MR"), 64.0, O.mult)
     for n in (16, 32, 64, 128):
         act(w("M64", n, 2 * n), w("M64", 0, n))
@@ -441,7 +484,6 @@ def rank_program(g, core, T, topo):
     for t in range(3):
         for q in range(4):
             sfill(w("SA%d" % t, 256 * q, 256 * q + 64), -1.0)
-            sfill(w("SB%d" % t, 256 * q, 256 * q + 64), 0.0)
     for z, m0, n in (("ZA", 0, 8), ("ZB", 8, 2)):
         fill(w(z, 0, 16), 0.0)
         iota(w("ZX"), [[0, 8], [1, 16]], m0, 0)
@@ -492,24 +534,31 @@ def rank_program(g, core, T, topo):
             out.append((max(a, s), b, max(a, s) - s))
         return out
 
-    for c in range(0, 1024, 256):
-        ts(w("CI", c, c + 256), w("DET", c, c + 256), 255, O.bitwise_and)
-        for x, y, p in rot(0, c, c + 256):
+    for c, d in zip(PIECES, PIECES[1:]):
+        ts(w("CI", c, d), w("DET", c, d), 255, O.bitwise_and)
+        for x, y, p in rot(0, c, d):
             ts(w("QB", p, p + y - x), w("CI", x, y), 128.0, O.not_equal)
     for c in range(0, 1024, 256):
         ts(w("TC", c, c + 256), w("CI", c, c + 256), -128.0, O.add)
         ts(w("TD", c, c + 256), w("DET", c, c + 256), -128.0, O.add, 1 / 256, O.mult)
 
-    def whole(c, scale):
+    def whole(c, scale, after=None):
         act(w("TM", c, c + 256), w("TD", c, c + 256), F.Identity, MAG)
+        if after:
+            behind(after)
         act(w("TN", c, c + 256), w("TM", c, c + 256), F.Identity, -MAG * scale, scale)
 
     def first_qt(c):
+        b = "P7" if c else "P6"
         whole(c, 1.0)
-        parts = [(half("P7", h), w("QW32"), w("TN", c + 128 * h, c + 128 * h + 128)) for h in range(2)]
-        parts += [(w("P7", x - c, y - c), w("R8"), w("QB", p, p + y - x)) for x, y, p in rot(0, c, c + 256)]
+        whole(c + 256, 1.0)
+        parts = [(half(b, h), w("QW32"), w("TN", c + 128 * h, c + 128 * h + 128)) for h in range(4)]
+        parts += [(w(b, x - c, y - c), w("R8"), w("QB", p, p + y - x)) for x, y, p in rot(0, c, c + 512)]
         group(parts)
-        act(w("QT", c, c + 256), w("P7", 0, 256))
+        mark("qt%d" % c)
+        for x in (0, 256):
+            act(w("QT", c + x, c + x + 256), w(b, x, x + 256))
+            behind("hv0")
 
     peers = [q for q in range(4) if q != me]
     near = [q for q in peers if T.cores[q] in topo.cores_of(core)]
@@ -535,17 +584,23 @@ def rank_program(g, core, T, topo):
             for q, e in plan:
                 rid, pid = topo.addr(T.cores[q], core)
                 tf.append(RemoteDMATransfer(dst_ids=[DstId(rid=rid, pnc=pid)], dma_engine_mask=sum(1 << x for x in e),
-                                            remote_sem=T.sem[rn if q in near else rx], src=T[sb][:, 256 * q:256 * q + 64],
-                                            dst=T[dst][:, 64 * me:64 * me + 64], alu_op=0))
+                                            remote_sem=T.sem[rn if q in near else rx], src=src(q)[0],
+                                            dst=T[dst][:, n * me:n * me + n], alu_op=0))
             g.remote_dma_fused(tf, local_sem=T.sem["snd"])
             for sem in sorted({rx, rn}):
                 mine = [(q, e) for q, e in plan if sem == (rn if q in near else rx)]
                 semof[sem] = (sem, sum(len(e) for q, e in mine))
-                note(sem, 1, [], [r for q, e in mine for r in w(dst, 64 * q, 64 * q + 64)[1]])
-        lands = lambda qs: [r for q in qs for r in w(dst, 64 * q, 64 * q + 64)[1]]
-        calls.append(("g", emit, w(sb)[1], lands(near) + [(rx, 1)], 0.5, NEAR))
+                note(sem, 1, [], lands([q for q, e in mine]))
+        n = 256 if sb == dst else 64
+        src = lambda q: w(sb, 256 * me, 256 * me + 256) if sb == dst else w(sb, 256 * q, 256 * q + 64)
+        lands = lambda qs: [r for q in qs for r in w(dst, n * q, n * q + n)[1]]
+        calls.append(("g", emit, [r for q in peers for r in src(q)[1]], lands(near) + [(rx, 1)], 0.5, NEAR + (n > 64) * 2.0))
+        if sb == dst:
+            behind("sent")
+        mark("sent")
         calls.append(("x", lambda reads, writes: None, [(rx, 1)], lands(far), 0.0, FAR - NEAR))
-        act(w(dst, 64 * me, 64 * me + 64), w(sb, 256 * me, 256 * me + 64))
+        if sb != dst:
+            act(w(dst, 64 * me, 64 * me + 64), w(sb, 256 * me, 256 * me + 64))
         return got
 
     def wrap(p):
@@ -555,7 +610,8 @@ def rank_program(g, core, T, topo):
         for k in range(8):
             mm(w("P2", 8 * k, 8 * k + 8), w("QB", 128 * k, 128 * k + 128), w("G8"))
         ts(w("LV"), w("P2", 0, 64), 0.0, O.is_gt)
-        mm(w("P5", 0, 64), w("TR2"), w("LV"), True, False)
+        mm(w("P5", 0, 64), w("C128"), w("KU"), True, False)
+        mm(w("P5", 0, 64), w("TR2"), w("LV"), False, False)
         for d in range(1, 8):
             mm(w("P5", 8 * d, 64), w("TWOS"), w("LV", 0, 64 - 8 * d), False, end and d == 7)
 
@@ -565,15 +621,14 @@ def rank_program(g, core, T, topo):
         IA, IB = "IA%d" % t, "IB%d" % t
         if t == 0:
             ranks(True)
-        cp(w("R32"), w("P5", 0, 64))
-        ts(w("LOW"), w("R32"), 31, O.bitwise_and)
+        ts(w("R32"), w("P5", 0, 64), 0.5, O.add)
+        tt(w("LW2", 0, 128, 2), w("R32"), w("P5", 0, 64), O.subtract)
+        tt(w("LW2", 1, 128, 2), w("P5", 0, 64), w("R32"), O.subtract)
         for h in range(17):
-            act(bs(h=h), w("P5", 0, 64), F.Sign, 0.5 - 32 * h)
-        for d in range(2):
-            ts(w("LW2", d, 128, 2), w("LOW"), -2.0 * d, O.add)
-        for l in range(0, 16, 2):
-            x = (T["OL"][:, :, l:l + 2], [("OL", sum(3 << (16 * j + l) for j in range(64)))], [])
-            ts(x, w("LW2"), 2.0 * l + 1, O.is_equal)
+            act(bs(h=h), w("R32"), F.Sign, 0.5 - 6144 - 32 * h)
+        for i in range(8):
+            x = (T["OL"][:, :, 7 - i:9 + i:2 * i + 1], [("OL", sum((1 << 7 - i | 1 << 8 + i) << 16 * j for j in range(64)))], [])
+            ts(x, w("LW2"), 2.0 * i + 1, O.is_equal)
         for k in range(8):
             c = (128 * k, 128 * k + 128)
             ts(w("OA", *c), (T["OL"][:, 8 * k:8 * k + 8, :], [("OL", ((1 << 128) - 1) << (128 * k))], []), w("PA", 8 * t + k, 8 * t + k + 1), O.mult)
@@ -584,10 +639,12 @@ def rank_program(g, core, T, topo):
         scan(w("LM"), w("RS8"), w("P2", 0, 136), 0.0, O.add, O.min)
         if t and TB:
             behind("tc%d" % (t - 1))
-        tt(w("LD"), w("LM", 7, 128, 8), w("LM", 15, 136, 8), O.subtract)
-        tt(w("GU"), w("LD"), w("SW"), O.min)
-        cp(w("DU"), ind(w("TD"), w("GU")))
+        tt(w("GU"), w("LM", 7, 128, 8), w("LM", 15, 136, 8), O.subtract)
+        for a, b in DUP:
+            cp(w("DU", 16 * a, 16 * b), ind(w("TD"), w("GU", a, b)))
+        mark("du%d" % t)
         act(w("AB"), ind(w("TC"), w("GU")), F.Abs)
+        mark("ab%d" % t)
         mm(A("P3"), w("IDB"), w("AB"))
         CUT = [0, HV0, 128, 192, 256]
 
@@ -595,16 +652,17 @@ def rank_program(g, core, T, topo):
             return w("hv", 16 * a, 16 * b), ind(w("hamt"), w("DU", a, b))
         for j in range(1, 4):
             act(*look(CUT[j], CUT[j + 1]))
+            if TB or j > 1:
+                behind("ab%d" % t)
+        mark("hv%d" % t)
         cp(*look(CUT[0], CUT[1]))
+        behind("du%d" % t)
         act(w("CN"), ind(w("TC"), w("GU")))
         ts(w("DF"), w("DU"), -float(MID), O.add)
         for h in range(2):
             mm(w("P0", h, 32, 2), half("DF", h), w("WT"))
         mm(w("P4", 0, 256), w("SHP"), w("DF"))
         mm(w("P4", 256, 512), w("SHN"), w("DF"))
-        mm(A("P5"), w("IDB"), w("DF"), True, False)
-        mm(A("P6"), w("IDB"), w("DF"), True, False)
-        mm(A("P6"), w("BL"), A("ONEB"), False, False)
         act(w("DP"), w("P4", 0, 256), F.Identity, w("BP"))
         act(w("DN"), w("P4", 256, 512), F.Identity, w("BN"))
         tt(w("H1"), w("P0", 0, 32), w("HK"), O.add)
@@ -614,11 +672,11 @@ def rank_program(g, core, T, topo):
         for h in range(2):
             ts(w("HV", 8 * h, 8 * h + 8), w("HP", h, 16, 2), 16.0, O.mult, 16.0 * t, O.add)
         if t == 0:
-            for c in range(0, 1024, 256):
+            for c in (0, 512):
                 first_qt(c)
         if t == 2:
             for c in range(0, 1024, 256):
-                whole(c, 256.0)
+                whole(c, 256.0, "hv2")
         mm(A("P7"), w("NEG"), w("DF"), True, False)
 
         def mins(a, b, h=None):
@@ -631,6 +689,7 @@ def rank_program(g, core, T, topo):
                 p = "P%d" % (1 + h)
                 group([(w(p, 0, 128), w("C128"), w("KC"))]
                       + [(w(p, k, 128, 16), w("MK", 256 * k + 128 * h, 256 * k + 128 * h + 128), w("G16")) for k in range(16)])
+                calls[-16][2].append(("~qt%d" % (512 * h), 1))
                 scan(half("SCN", h), w("RS16", 0, 128), w(p, 0, 128), 0.0, O.mult, O.max)
         mins(0, CUT[2], 0)
         mins(CUT[2], CUT[3])
@@ -642,25 +701,32 @@ def rank_program(g, core, T, topo):
         act(w("QS"), A("P1"), F.Identity, w("QB0"))
         group([(A("P2"), w("IDB"), w("CN")), (A("P2"), w("NEG"), w("SGC"))])
         act(w("CFD"), A("P2"))
-        tt(w("E3"), w("SCN", 15, 256, 16), w("HV"), O.add)
-        cp(w("MX"), w("SCN", 15, 256, 16))
-        tt(w("XK", 16, 272), ind(w("MX"), w("OC")), w("SCN"), O.is_equal)
-        ts(w("VV"), w("E3"), 4, O.arith_shift_right, 4095, O.bitwise_and)
-        ts(w("VB"), ind(w("VV"), w("OC")), -float(MID), O.add)
-        for h in range(2):
-            mm(half("P5", h), w("XK", 16 + 128 * h, 144 + 128 * h), w("IBG"), False, h == 1)
-        for h in range(2):
-            mm(half("P6", h), w("XK", 15 + 128 * h, 143 + 128 * h), w("IBG"), False, h == 1)
-        for h in range(2):
-            mm(half("P4", h), half("VB", h), w("IDB"))
-        for h in range(2):
-            mm(half("P7", h), half("VB", h), w("IDB"), False, h == 1)
-        tt(w("HI"), A("P5"), w("DN"), O.min)
-        tt(A("P6"), A("P6"), w("DP"), O.max)
-        tt(w("CT"), A("P4"), w("HI"), O.min)
-        tt(w("CH"), w("CT"), A("P6"), O.max)
-        for h in range(2):
-            mm(w("P0", h, 32, 2), half("CH", h), w("WT"))
+        for hs in ([(0,), (1,)] if TS else [(0, 1)]):
+            c, z = (8 * hs[0], 8 * hs[-1] + 8), (128 * hs[0], 128 * hs[-1] + 128)
+            top, oc = w("SCN", z[0] + 15, z[1], 16), w("OC", 0, c[1] - c[0])
+            mm(w("P5", *z), w("IDB"), w("DF", *z), True, False)
+            mm(w("P6", *z), w("IDB"), w("DF", *z), True, False)
+            mm(w("P6", *z), w("BL"), w("ONEB", *z), False, False)
+            tt(w("E3", *c), top, w("HV", *c), O.add)
+            cp(w("MX", *c), top)
+            tt(w("XK", 16 + z[0], 16 + z[1]), ind(w("MX", *c), oc), w("SCN", *z), O.is_equal)
+            ts(w("VV", *c), w("E3", *c), 4, O.arith_shift_right, 4095, O.bitwise_and)
+            ts(w("VB", *z), ind(w("VV", *c), oc), -float(MID), O.add)
+            mark("vb%d" % t)
+            for h in hs:
+                mm(half("P5", h), w("XK", 16 + 128 * h, 144 + 128 * h), w("IBG"), False, h == hs[-1])
+            for h in hs:
+                mm(half("P6", h), w("XK", 15 + 128 * h, 143 + 128 * h), w("IBG"), False, h == hs[-1])
+            for h in hs:
+                mm(half("P4", h), half("VB", h), w("IDB"))
+            for h in hs:
+                mm(half("P7", h), half("VB", h), w("IDB"), False, h == 1)
+            tt(w("HI", *z), w("P5", *z), w("DN", *z), O.min)
+            tt(w("P6", *z), w("P6", *z), w("DP", *z), O.max)
+            tt(w("CT", *z), w("P4", *z), w("HI", *z), O.min)
+            tt(w("CH", *z), w("CT", *z), w("P6", *z), O.max)
+            for h in hs:
+                mm(w("P0", h, 32, 2), half("CH", h), w("WT"))
         act(w("AE"), A("P7"), F.Abs)
         act(w("SG"), w("AE"), F.Sign)
         for h in range(2):
@@ -679,7 +745,17 @@ def rank_program(g, core, T, topo):
         tt(w("XF"), ind(w("SC2"), w("OL4")), w("MT"), O.min)
         wrap("P4")
         cp(w("OFF"), w("P4", 0, 16))
-        mm(A("P5"), w("QW"), w("CH"), True, False)
+        ts(w("LE"), w("GU"), -1279.0, O.add, 4096.0, O.mult)
+        behind("vb%d" % t)
+        cp(w("LD"), w("GU"))
+        behind("vb%d" % t)
+        tt(w("LE"), w("LE"), w("SW"), O.min)
+        tt(w("GS"), w("LD"), w("LE"), O.max)
+        if TE:
+            scatter("TC", "GS", "CFD", 4)
+            mark("tf%d" % t)
+        mm(A("P5"), w("R11"), w("IO"), True, False)
+        mm(A("P5"), w("QW"), w("CH"), False, False)
         ts(w("HS", 0, 16), w("PR"), 7, O.arith_shift_right, 1023, O.bitwise_and)
         ts(w("HS", 16, 32), w("I2", 0, 16), 511, O.bitwise_and)
         cp(w("T16", 0, 16), w("HS", 0, 16))
@@ -689,117 +765,104 @@ def rank_program(g, core, T, topo):
         for h in range(2):
             mm(half("P5", h), w("SH%d" % h, 0, 128, 1, 32), w("R4", 0, 128, 1, 32), False, h == 1)
         act(w("REC"), A("P5"), F.Identity, w("QB0"))
-        scatter("SA%d" % t, "OFF", "REC")
+        scatter("SA%d" % t, "OFF", "REC", 1, "tf%d" % t if TE > 1 and t != 1 else None)
         sent += send("SA%d" % t, IA, "ra%d" % t, "rn%d" % t)
         group([(A("P1"), w("IDB"), w("CH")), (A("P1"), w("NEG"), w("DF"))])
         act(w("SGN"), A("P1"), F.Sign)
         mm(A("P2"), w("BLK"), w("SGN"))
         act(w("RN"), A("P2"), F.Identity, 384.5, -1 / 256)
         group([(A("P1"), w("BLK"), w("SGN")), (A("P1"), w("IDB"), w("FB")), (A("P1"), w("I2B"), w("RN"))])
-        act(w("CA"), A("P1"), F.Abs, -98304.0 - 128 - 192)
-        group([(A("P6"), w("IDB"), w("CH")), (A("P6"), w("IQ"), w("CA"))])
-        act(w("ED"), A("P6"), F.Identity, MID - 0.5)
-        scatter("SB%d" % t, "OFF", "ED")
-        sent += send("SB%d" % t, IB, "rb%d" % t, "rb%d" % t)
+        act(w("SD%d" % t, 256 * me, 256 * me + 256), A("P1"), F.Abs, -98304.0 - 128 - 192)
+        sent += send("SD%d" % t, "SD%d" % t, "rc%d" % t, "rc%d" % t)
+        mm(A("P6"), w("IDB"), w("CH"))
+        act(w("SB%d" % t, 256 * me, 256 * me + 256), A("P6"), F.Identity, float(MID))
+        sent += send("SB%d" % t, "SB%d" % t, "rb%d" % t, "rb%d" % t)
         if t:
-            scatter("QT", "FO", "QN", PQ)
-        scatter("QT", "GU", "QS", PQ)
-        scatter("TC", "GU", "CFD", 2)
+            scatter("QT", "FO", "QN", PQ, "vb%d" % t)
+        scatter("QT", "GS", "QS", PF)
+        if not TE:
+            scatter("TC", "GS", "CFD", PG)
         if t == 2:
             for c in range(0, 1024, 256):
+                if c < YV:
+                    p = w("P2", 256, 512)
+                    act(p, w("TN", c, c + 256), F.Identity, 128.0)
+                    tt(w("YT", c, c + 256), w("TC", c, c + 256), p, O.add)
+                    continue
                 group([(A("P2"), w("IDB"), w("TC", c, c + 256))]
                       + [(half("P2", h), w("I32"), w("TN", c + 128 * h, c + 128 * h + 128)) for h in range(2)])
                 act(w("YT", c, c + 256), A("P2"), F.Identity, 128.0)
+        def probe(x, y):
+            return w("PR5", 16 * x, 16 * y), ind(w("QT", 0, 1024), w("ZU", x, y))
         hn, hf = me // 2, min(far) // 2
         KEY, BRO = {hn: "P5", hf: "P7"}, {hn: "P0", hf: "P1"}
         sets = [(64 * me, 64), (64 * near[0], 64), (128 * hf, 128)]
-        for a, n in sets:
-            k, o = n // 2, a * 10 // 16
+
+        def lists(p, z, o, a, n, u):
+            x, k = w(p, 0, n // u), (o + a // u, o + (a + n) // u)
+            group([(x, w("C128"), w("KZ", 0, n // u))]
+                  + [(x, w(z, 16 - 16 // u * i, 144 - 16 // u * i), w("IH", a + i, a + n, u)) for i in range(u)])
+            if n == 128:
+                mark("far%d" % t)
+            if n == 256:
+                for c in calls[-u:]:
+                    c[2].append(("~far%d" % t, 1))
+            ts(w("RZ", *k), x, -511.5, O.add)
+            tt(w("ZU", *k), x, w("RZ", *k), O.subtract)
+        for (a, n), p in zip(sets, ("P4", "P3", "P4")):
             ts(w("IH", a, a + n), w(IA, a, a + n), 2000.0, O.min)
-            pa, pb = ("P4", "P6") if n == 128 else ("P4", "P4") if a == 64 * me else ("P3", "P3")
-            one = [(w(pa, 0, k), w("ZA", 16 - 8 * u, 144 - 8 * u), w("IH", a + u, a + n, 2)) for u in range(2)]
-            two = [(w(pb, k, k + n // 8), w("ZB", 16 - 2 * u, 144 - 2 * u), w("IH", a + u, a + n, 8)) for u in range(8)]
-            for p, x, y, parts in ([(pa, 0, k + n // 8, one + two)] if pa == pb else [(pa, 0, k, one), (pb, k, k + n // 8, two)]):
-                group([(w(p, x, y), w("C128"), w("KZ", x, y))] + parts)
-                ts(w("RZ", o + x, o + y), w(p, x, y), -511.5, O.add)
-                tt(w("ZU", o + x, o + y), w(p, x, y), w("RZ", o + x, o + y), O.subtract)
+            lists(p, "ZA", 0, a, n, 2)
+            if a == 64 * me:
+                lists("P3", "ZB", 128, a, n, 8)
+                act(*probe(a // 2, (a + n) // 2))
+                act(*probe(128 + a // 8, 128 + (a + n) // 8))
+        lists("P6", "ZB", 128, 0, 256, 8)
         for h in (hn, hf):
             p = w(KEY[h], 0, 160)
             mm(p, w("C128"), w("KA"), True, False)
             mm(p, w("C128"), w("KB"), False, False)
             mm(p, half("IH", h), w("KW"), False, False)
 
-        def probe(a, x, y):
-            o = a * 10 // 16
-            return w("PR5", 16 * (o + x), 16 * (o + y)), ind(w("QT", 0, 1024), w("ZU", o + x, o + y))
+        group([(w("P2", 0, 16), w("C128"), w("KQ"))]
+              + [(w("P2", 0, 16), w("ZC", 16 - u, 144 - u), w("IH", u, 256, 16)) for u in range(16)])
+        for c in calls[-16:]:
+            c[2].append(("~far%d" % t, 1))
+        cp(w("OI"), w("P2", 0, 16))
+        mark("oi%d" % t)
 
-        def same(a, n, m, x, y):
-            b, st = (10 * a + m, 8) if m < 8 else (10 * a + 8 * n + m - 8, 2)
-            tt(w("CMP", 256 * m + a + x, 256 * m + a + y), w("PR5", b + st * x, b + st * (y - 1) + 1, st),
-               w(BRO[a // 128], a % 128 + x, a % 128 + y), O.is_equal)
+        def same(m, a, n):
+            b, st = (m, 8) if m < 8 else (2048 + m - 8, 2)
+            tt(w("CMP", 256 * m + a, 256 * m + a + n), w("PR5", b + st * a, b + st * (a + n - 1) + 1, st),
+               w(BRO[a // 128], a % 128, a % 128 + n), O.is_equal)
 
         def key(h, m, end):
             mm(w(KEY[h], m, 160, 10), w("CMP", 256 * m + 128 * h, 256 * m + 128 * h + 128), w("RW"), False, end)
 
-        def place(h):
-            c, ky = (8 * h, 8 * h + 8), w("KY", 160 * h + 19, 160 * h + 160, 20)
-            scan(w("KY", 160 * h, 160 * h + 160), w("RSK", 160 * h, 160 * h + 160), w(KEY[h], 0, 160), 0.0, O.max, O.min)
-            ts(w("RK", *c), ky, -7.9921875, O.add, YCAP, O.min)
-            tt(w("PL16", *c), ky, w("RK", *c), O.subtract)
-            tt(w("PL", *c), ky, w("RK", *c), O.subtract)
-            mm(w(KEY[h], 0, 128, 1, 8), w("PL16", *c), w("IDB"))
-            tt(half("XF", h), ind(w("PL", *c), w("OC", 0, 8)), w("M64", 0, 128), O.mult)
-            cp(half("R6", h, 8), w(KEY[h], 0, 128, 1, 8))
-            mm(w("P4", *c), half("XF", h), w("G8"))
-            mm(w(BRO[h], 0, 128), w("SS", 0, 128, 1, 8), half("R6", h, 8))
-            cp(w("PW", *c), w("P4", *c))
-            cp(half("PU", h), w(BRO[h], 0, 128))
-            cp(w("PO", *c), w("P4", *c))
-            act(half("CO", h), ind(w("TC"), w("PO", *c)))
-            if t < 2 and (DIG or h == hf):
-                c = c if DIG else (0, 16)
-                ts(w("PN", *c), w("PL", *c), 64.0, O.mult, 1024.0 - START[t + 1], O.add)
-                ts(w("PM", *c), w("PN", *c), 127, O.bitwise_and)
-                ts(w("KJ", *c), w("PN", *c), 7, O.arith_shift_right, 7, O.bitwise_and)
-                ts(w("NB", *c), w("PM", *c), -1.0, O.mult)
-                for j in range(*c):
-                    act(w("TH", 128 * j, 128 * j + 128), w("IO"), F.Sign, w("NB", j, j + 1))
-
-        def first(hc, hj, end=False):
-            for c in range(8 * hc, 8 * hc + 8):
-                x = w("MK", 256 * c + 128 * hj, 256 * c + 128 * hj + 128)
-                ts(x, half("PU", hj), w("PW", c, c + 1), O.is_equal)
-                mm(w("P3", 8 * hj, 8 * hj + 8), x, w("WC", 8 * (c % 8), 8 * (c % 8) + 8) if hc == hj else w("WBIG"), False,
-                   end and c % 8 == 7)
-        for a, n in sets[:2]:
-            act(w(BRO[hn], a % 128, a % 128 + n), w(IA, a, a + n))
-            act(*probe(a, 0, 40))
-            for m in range(10):
-                same(a, n, m, 0, n)
-                if a != 64 * me:
-                    key(hn, m, m == 9)
-        a, n = sets[2]
-        act(w(BRO[hf], 0, n), w(IA, a, a + n))
-        act(*probe(a, 0, 32))
-        act(*probe(a, 32, FS))
-        cp(*probe(a, FS, 80))
-        mm(w("P3", 0, 16), w("IDB"), w("Z16"), True, False)
-        if SPLIT:
-            place(hn)
-        for m in range(8):
-            same(a, n, m, 0, 64)
+        for a, n in sets:
+            act(w(BRO[a // 128], a % 128, a % 128 + n), w(IA, a, a + n))
+            if a == 64 * me:
+                for m in range(10):
+                    same(m, a, n)
+        (b, _), (a, n) = sets[1:]
+        for x, y in ((b, 32), (a, 32), (a + 64, 32 - FV)):
+            act(*probe(x // 2, x // 2 + y))
+        if FV:
+            cp(*probe(a // 2 + 64 - FV, a // 2 + 64))
+        for x, y in sets[1:]:
+            cp(*probe(128 + x // 8, 128 + (x + y) // 8))
+        for m in range(10):
+            same(m, b, 64)
+            key(hn, m, m == 9)
         for m in (8, 9):
-            same(a, n, m, 0, 128)
+            same(m, a, 128)
             key(hf, m, False)
         for m in range(8):
-            same(a, n, m, 64, 128)
+            same(m, a, 64)
+        for m in range(8):
+            same(m, a + 64, 64)
+            behind("oi%d" % t)
             key(hf, m, m == 7)
-        if SPLIT:
-            first(hn, hn)
-            place(hf)
-            first(0, 1)
-            first(hf, hf, True)
-        else:
+        if True:
             ky = w("KY", 19, 320, 20)
             for h in (hn, hf):
                 scan(w("KY", 160 * h, 160 * h + 160), w("RSK", 160 * h, 160 * h + 160), w(KEY[h], 0, 160), 0.0, O.max, O.min)
@@ -807,44 +870,52 @@ def rank_program(g, core, T, topo):
             tt(w("PL16"), ky, w("RK"), O.subtract)
             tt(w("PL"), ky, w("RK"), O.subtract)
             mm(w("P7", 0, 128, 1, 16), w("PL16"), w("IDB"))
-            tt(w("XF"), ind(w("PL"), w("OC")), w("M64"), O.mult)
-            cp(half("R6", 0, 16), w("P7", 0, 128, 1, 16))
-            wrap("P4")
-            for h in range(2):
-                mm(half("P0", h), w("SS1" if h else "SS", 0, 128, 1, 16), half("R6", 0, 16))
-            cp(w("PO"), w("P4", 0, 16))
-            cp(w("PW"), w("P4", 0, 16))
-            cp(w("PU"), A("P0"))
-            act(w("CO"), ind(w("TC"), w("PO")))
             if t < 2:
                 ts(w("PN"), w("PL"), 64.0, O.mult, 1024.0 - START[t + 1], O.add)
                 ts(w("PM"), w("PN"), 127, O.bitwise_and)
                 ts(w("KJ"), w("PN"), 7, O.arith_shift_right, 7, O.bitwise_and)
                 ts(w("NB"), w("PM"), -1.0, O.mult)
+                mark("nb%d" % t)
+            for h in range(2):
+                tt(half("XF", h), ind(w("PL", 8 * h, 8 * h + 8), w("OC", 0, 8)), half("M64", 0), O.mult)
+                if h and NX:
+                    behind("nb%d" % t)
+            cp(half("R6", 0, 16), w("P7", 0, 128, 1, 16))
+            for h in range(2):
+                c = (8 * h, 8 * h + 8)
+                mm(w("P4", *c), half("XF", h), w("G8"))
+                cp(w("PO", *c), w("P4", *c))
+                act(half("CO", h), ind(w("TC"), w("PO", *c)))
+            for h in range(2):
+                mm(half("P0", h), w("SS1" if h else "SS", 0, 128, 1, 16), half("R6", 0, 16))
+            cp(w("PW"), w("P4", 0, 16))
+            cp(w("PU"), A("P0"))
+            if t < 2:
                 for j in range(16):
-                    act(w("TH", 128 * j, 128 * j + 128), w("IO"), F.Sign, w("NB", j, j + 1))
-            for c in range(16):
-                a = 32 * (c // 2) if c < 8 else 128
-                x = w("PU", a, 256)
-                if t < 2 and c >= FK:
-                    x = (x[0], x[1], w("NB")[1])
-                ts(w("MK", 256 * c + a, 256 * c + 256), x, w("PW", c, c + 1), O.is_equal)
-                wc = w("WC", 8 * (c % 8), 8 * (c % 8) + 8)
-                for x, y in ([(a, 128)] if a in (0, 64, 96) else [(32, 64), (64, 128)] if a == 32 else []):
-                    mm(w("P3", 0, 8, 1, y, x), w("MK", 256 * c + x, 256 * c + y), wc, False, False)
-                mm(w("P3", 8, 16), w("MK", 256 * c + 128, 256 * c + 256), wc if c > 7 else w("WBIG"), False, c == 15)
-        act(w("AT"), w(IB), F.Identity, MAG)
-        if CQV:
-            act(A("P6"), w("AT"), F.Identity, MAG, -1.0)
-            tt(w("CQ"), w(IB), A("P6"), O.add)
-            group([(A("P6"), w("I2B"), w("CQ"))] + [(half("P6", h), w("IDB"), half("CO", h)) for h in (hn, hf)])
-        else:
-            act(w("NA"), w("AT"), F.Identity, MAG, -1.0)
-            group([(half("P6", h), w("I256"), half(x, h)) for h in range(2) for x in (IB, "NA")]
-                  + [(half("P6", h), w("IDB"), half("CO", h)) for h in (hn, hf)])
-        if t < 2:
-            act(w("ABN"), A("P6"), F.Abs)
-        ts(w("CNW"), A("P6"), 127.0, O.min, -127.0, O.max)
+                    act(w("TH", 128 * j, 128 * j + 128), w("IO", 0, 128), F.Sign, w("NB", j, j + 1))
+            WHO = ("P3", "P1")
+            for h in range(2):
+                mm(w(WHO[h], 0, 8), w("IDB"), w("Z16", 0, 8), True, False)
+                for c in range(8 * h + 7, -1, -1):
+                    a = (0, 0, 64, 96)[c % 8 // 2] if c // 8 == h else 0
+                    x = w("MK", 256 * c + 128 * h + a, 256 * c + 128 * h + 128)
+                    ts(x, w("PU", 128 * h + a, 128 * h + 128), w("PW", c, c + 1), O.is_equal)
+                    if h:
+                        behind("who%d" % t)
+                    elif c == 0:
+                        mark("who%d" % t)
+                    mm(w(WHO[h], 0, 8, 1, 128, a), x, w("WC", 8 * (c % 8), 8 * (c % 8) + 8) if c // 8 == h else w("WBIG"), False, c == 0)
+                    if h:
+                        behind("whp%d" % t)
+                    elif c == 0:
+                        mark("whp%d" % t)
+        act(w("CQ"), ind(w("SD%d" % t), w("OI")), F.Identity, -128.0)
+        act(w(IB), ind(w("SB%d" % t), w("OI")))
+        for h, p in enumerate((half("P6", 0), half("P0", 2))):
+            group([(p, w("IDB"), half("CQ", h)), (p, w("IDB"), half("CO", h))])
+            if t < 2:
+                act(half("ABN", h), p, F.Abs)
+            ts(half("CNW", h), p, 127.0, O.min, -127.0, O.max)
         if t < 2:
             for a in range(0, 1024, 256):
                 for x, y, p in rot(t + 1, a, a + 256):
@@ -853,34 +924,43 @@ def rank_program(g, core, T, topo):
             ky = w("KY", 19, 320, 20)
             ts(w("VAL"), ky, YCAP, O.is_lt)
             ts(w("OLD"), ky, Y0 + 2560, O.is_lt)
-            tt(w("AK", 0, 128), ind(w("KJ"), w("OD", 0, 8)), w("KI"), O.is_equal)
-            tt(w("AK", 128, 256), ind(w("KJ"), w("OD", 0, 8)), w("KI"), O.is_le)
+            cp(w("KF"), w("KJ"))
+            for k in range(8):
+                act(sk(k), w("KF"), F.Sign, float(k), -1.0)
+            act(w("SQ"), sk(), F.Abs)
             for h in range(2):
+                act(w("AK", 128 * h + 64, 128 * h + 128), sk(h=h), F.Identity, 1.0)
+                act(w("AK", 128 * h, 128 * h + 64), w("SQ", 64 * h, 64 * h + 64), F.Identity, 1.0, -1.0)
+                c = (8 * h, 8 * h + 8)
                 mm(w("P4", 16 + 8 * h, 24 + 8 * h), half("ABN", h), w("G8"))
-            tt(w("NL"), w("P4", 16, 32), w("VAL"), O.min)
-            tt(w("D0"), w("NL"), w("OLD"), O.subtract)
-            ts(w("WIN"), w("P3", 0, 16), w("THR"), O.is_lt)
-            tt(w("DW"), w("WIN"), w("D0"), O.mult)
-            tt(w("DK"), ind(w("DW"), w("OD")), w("AK"), O.mult)
-        ts(w("LO"), w("P3", 0, 16), w("THR"), O.is_ge)
-        tt(w("XF"), ind(w("LO"), w("OC")), w("MT"), O.mult)
-        wrap("P4")
+                tt(w("NL", *c), w("P4", 16 + 8 * h, 24 + 8 * h), w("VAL", *c), O.min)
+                tt(w("D0", *c), w("NL", *c), w("OLD", *c), O.subtract)
+        for h in range(2):
+            c, p = (8 * h, 8 * h + 8), w(WHO[h], 0, 8)
+            if t < 2:
+                ts(w("WIN", *c), p, w("THR"), O.is_lt)
+                tt(w("DW", *c), w("WIN", *c), w("D0", *c), O.mult)
+                tt(half("DK", h), ind(w("DW", *c), w("OD", 0, 8)), half("AK", h), O.mult)
+                mark("dk%d" % t)
+            ts(w("LO", *c), p, w("THR"), O.is_ge)
+            tt(half("XF", h), ind(w("LO", *c), w("OC", 0, 8)), half("MT", h), O.mult)
+            if XD and h:
+                behind("dk%d" % t)
+            mm(w("P7", *c), half("XF", h), w("G8"))
         mark("wrap%d" % t)
-        tt(w("FO"), w("P4", 0, 16), w("PW"), O.max)
+        tt(w("FO"), w("P7", 0, 16), w("PW"), O.max)
         if t < 2:
-            for h in range(2):
-                mm(w("P5", 0, 64), w("MONE"), w("DK", 64 * h, 64 * h + 64), False, False)
-                mm(w("P5", 0, 64), w("TWOS"), w("DK", 128 + 64 * h, 192 + 64 * h), False, False)
             for j in range(16):
                 h, gg = j // 8, j % 8
-                mm(w("P5", gg, 64, 8), w("TH", 128 * j, 128 * j + 128), w("DK", 64 * h + gg, 64 * h + 64, 8), False, j == 15)
+                if not gg:
+                    mm(w("P5", 0, 64), w("ONEB", 0, 128), w("DK", 128 * h + 64, 128 * h + 128), False, False)
+                mm(w("P5", gg, 64, 8), w("TH", 128 * j, 128 * j + 128), w("DK", 128 * h + gg, 128 * h + 64, 8), False, j == 15)
                 if j == WR:
                     behind("wrap%d" % t)
             group([(half("P2", h), w("I32"), half(IA, h)) for h in range(2)] + [(A("P2"), w("R8"), w("ABN"))])
             act(w("QN"), A("P2"))
         else:
-            act(w("NA"), w("AT"), F.Identity, MAG, -1.0)
-            act(A("P2"), w("NA"), F.Identity, 128.0, -256.0)
+            act(A("P2"), w(IB), F.Identity, 128.0, 256.0)
             tt(w("YN"), w("CNW"), A("P2"), O.add)
         if t < 2:
             scatter("TC", "FO", "CNW", PT)

from concourse.bass import DstId, RemoteDMATransfer
from concourse.mybir import AluOpType as O, ActivationFunctionType as F, AxisListType as AX

TURNS, JOLT, SPAN, HV0, DIG, FS, CQV, PQ = 4000, 0.5, 0.1, 60, 1, 60, 1, 4
NX, WR, PT, TB = 0, 99, 2, 1
YV, TS, XD, FV = 1024, 0, 1, 0
DUP, PF, PG, TE = ((0, 16),), 1, 2, 0
PIECES = [0, 304, 608, 896, 1024]
ORDER = {}
WAKE, NEAR, FAR = 0.18, 2.1, 2.1
F32, BF, I32, U16, F16 = "float32", "bfloat16", "int32", "uint16", "float16"
BUFS = {
    F32: dict(TD=1536, QT=1536, TM=1024, TN=1024, YT=1280, ONE=160, I32=128, I256=128, QW32=128, SW=16, MR=16,
              PA=24, RC=1, QB0=1, BN=1, BP=1, THR=1, WX=1, PW3=128, PWT=128, Z128=128, M64=256, MT=256, JC=2, RS8=136, RS16=256,
              RS4=64, RSK=320, QC=64, HK=32, LM=136, LD=16, LE=16, DP=256, DN=256, SCN=256, HI=256, CT=256, HV=16, MX=16, VX=16, VD=16, QQ=64,
              SC2=64, REC=256, ED=256, QS=256, QN=256, AT=256, NA=256, KY=320, PL=16, PW=16, LO=16, YN=256, PR5=2560,
              RC8=1, NB=16, VAL=16, OLD=16, NL=16, D0=16, WIN=16, DW=16, AK=256,
              SA0=1280, SA1=1280, SA2=1280, SB0=1024, SB1=1024, SB2=1024, IA0=256, IA1=256, IA2=256, IB0=256, IB1=256, IB2=256),
    BF: dict(TC=1536, ham=3584, ONEB=320, G8=8, G16=8, GM8=8, TRX=128, TRS=128, IDB=128, NEG=128, IBG=128, I2B=128, IQ=128, BLK=128,
             KC=128, KD=136, DMB=136, C128=128, BL=128, R8=128, QW=128, SHP=128, SHN=128, WT=16, WC=128, WBIG=8, ZG=24, ZA=144,
             ZB=144, ZX=128, KW=160, KX=160, AB=256, SS=128, SS1=128, SH0=128, SH1=128, RW=16, KA=160, KB=160, KS=64, KZ=80, Z16=16, QB=1024, LV=64, OL=1024,
             CN=256, hv=4096, MK=4096, XK=272, AE=256, SG=256, SGN=256, RN=256, FB=256, CA=256, OM=64, SGC=256, CFD=256, ABF=256,
             ABN=256, CMP=2560, RZ=160, CO=256, CQ=256, CNW=256, TR2=128, TWOS=128, SD0=1024, SD1=1024, SD2=1024, KF=16, SQ=128, IO=256, R11=128, ZC=144, KQ=16, TH=2048, LW2=128, R32=64, DK=256),
    I32: dict(DET=1024, CI=1024, PI=16, PJ=1, PK=24, PLI=24, EI=4, EJ=4, EK=4, XI=16, E3=16, VV=16, H1=32, H2=32,
              HP=16, I1=32, I2=32, PR=16, OW=16, HS=32, EL=16, EM=1, PN=16, PM=16, KJ=16),
    F16: dict(OA=1024, DF=256, VB=256, CH=256, XF=256, T16=32, R4=128, IH=256, KU=64, RK=16, PL16=16, R6=256, PU=256),
    U16: dict(GU=16, DU=256, OFF=16, ZU=160, PO=16, FO=16, OC=16, OL4=16, OQ=4, OW4=4, OD=16, OI=16, GS=16),
}
SCRATCH, WIDTH, WHERE = {}, {}, {}
for _d in BUFS:
    _p = 0
    for _n, _w in BUFS[_d].items():
        _n = "hamt" if _n == "ham" else _n
        WIDTH[_n] = _w
        if _w <= 160:
            WHERE[_n] = ("small_" + _d, _p)
            _p += (_w + 15) // 16 * 16
        else:
            SCRATCH[_n] = ("sbuf", [128, _w], _d)
    if _p:
        SCRATCH["small_" + _d] = ("sbuf", [128, _p], _d)
SCRATCH["BS"] = ("sbuf", [128, 8, 17, 8], BF)
SCRATCH["OL"] = ("sbuf", [128, 64, 16], BF)
SCRATCH["SK"] = ("sbuf", [128, 2, 8, 8], BF)
TWO = list(BUFS[F16]) + list(BUFS[BF]) + list(BUFS[U16])
PSUM = ["P%d" % _k for _k in range(8)]
for _n in PSUM:
    WIDTH[_n] = 512
    SCRATCH[_n] = ("psum", [128, 512], F32)
SEMAPHORES = ["qv", "qs", "qt", "qg", "ld0", "ld1", "ld2", "ld3", "ld4", "st0", "snd"]
SEMAPHORES += [_n + str(_t) for _n in ("ra", "rn", "rb", "rc") for _t in range(3)]
W1 = [13 * _i + 5 for _i in range(16)]
W2 = [255 - 14 * _i for _i in range(16)]
MID = 1792
VOID = min(_c for _c in range(3584)
           if all((((sum(W1) * _c) % 4096 * ((sum(W2) * _c) % 4096) >> 5) + _t) % 4096 >= 3584 for _t in range(3)))


def rank_program(g, core, T, topo):
    me = T.rank_of(core)
    if me is None:
        return
    V, S, PE = g.vector, g.scalar, g.tensor
    ENG = {"v": V, "s": S, "t": PE, "g": g, "d": g.sync}
    cnt, known, clk = {"v": 0, "s": 0, "t": 0, "g": 0}, {q: {} for q in ENG}, {}
    wr, rd, last = {}, {}, {}
    semof = {"v": ("qv", 1), "s": ("qs", 1), "t": ("qt", 1), "g": ("qg", 1)}

    def w(name, a=0, b=None, st=1, p=128, p0=0):
        b = WIDTH[name] if b is None else b
        n, o = WHERE.get(name, (name, 0))
        ap = T[n][p0:p, o + a:o + b] if st == 1 else T[n][p0:p, o + a:o + b:st]
        m = 0
        if st == 1:
            m = ((1 << (b - a)) - 1) << a
        else:
            for c in range(a, b, st):
                m |= 1 << c
        return (ap, [(name, m)], [])

    def bs(k=None, h=None):
        if h is None:
            return (T["BS"][:, k, :, :], [("BS", ((1 << 136) - 1) << (136 * k))], [])
        return (T["BS"][:, :, h, :], [("BS", sum(255 << (136 * j + 8 * h) for j in range(8)))], [])

    def sk(k=None, h=None):
        if h is not None:
            return (T["SK"][:, h, :, :], [("SK", (1 << 64) - 1 << 64 * h)], [])
        if k is None:
            return (T["SK"][:, :, :, :], [("SK", (1 << 128) - 1)], [])
        return (T["SK"][:, :, k, :], [("SK", (255 | 255 << 64) << 8 * k)], [])

    def ind(win, off):
        return (win[0].indirect(off[0]), win[1], off[1], 16 * off[1][0][1].bit_count())

    def wait(q, q2, k):
        if known[q].get(q2, 0) >= k:
            return
        sem, inc = semof[q2]
        ENG[q].wait_ge(T.sem[sem], k * inc)
        for a, n in list(clk.get((q2, k), {}).items()) + [(q2, k)]:
            if known[q].get(a, 0) < n:
                known[q][a] = n

    def deps(q, reads, writes):
        need = {}

        def add(q2, k):
            if need.get(q2, 0) < k:
                need[q2] = k
        for n, m in reads + writes:
            if n in PSUM:
                for q2, k in last.get(n, {}).items():
                    if q2 != q:
                        add(q2, k)
        for n, m in reads:
            for q2, k, m2 in wr.get(n, []):
                if m & m2:
                    add(q2, k)
        for n, m in writes:
            for q2, k, m2 in wr.get(n, []):
                if m & m2 and not (q == "t" and q2 == "t"):
                    add(q2, k)
            for q2, k, m2 in rd.get(n, []):
                if m & m2:
                    add(q2, k)
        for q2, k in sorted(need.items(), key=lambda x: x[0] == q):
            wait(q, q2, k)

    def note(q, k, reads, writes):
        clk[(q, k)] = dict(known[q] if q in known else {})
        for n, m in writes:
            wr[n] = [x for x in wr.get(n, []) if x[2] & ~m] + [(q, k, m)]
            rd[n] = [x for x in rd.get(n, []) if x[2] & ~m]
        for n, m in reads:
            rd[n] = [x for x in rd.get(n, []) if not (x[0] == q and not x[2] & ~m)] + [(q, k, m)]
        for n, m in reads + writes:
            if n in PSUM:
                last.setdefault(n, {})[q] = k

    calls = []

    def wide(x):
        return x[3] if len(x) > 3 else x[1][0][1].bit_count()

    def E(q, f, ins, outs, cost):
        def emit(reads, writes):
            deps(q, reads, writes)
            cnt[q] += 1
            f().then_inc(T.sem[semof[q][0]], 1)
            note(q, cnt[q], reads, writes)
        reads = [r for x in ins for r in x[1] + x[2]] + [r for x in outs for r in x[2]]
        calls.append((q, emit, reads, [r for x in outs for r in x[1]], cost, 0.0))

    def dma(q, out, in_, sem, reads, writes, lat):
        def emit(reads, writes):
            deps(q, reads, writes)
            ENG[q].dma_start(out=out, in_=in_).then_inc(T.sem[sem], 16)
            semof[sem] = (sem, 16)
            clk[(sem, 1)] = dict(known[q])
            note(sem, 1, reads, writes)
        calls.append((q, emit, reads, writes, 0.1, lat))

    def schedule():
        n = len(calls)
        succ, npred, prev, done = [[] for _ in range(n)], [0] * n, [], [False] * n
        W, R, B = {}, {}, {}
        for j, (q, emit, reads, writes, cost, lat) in enumerate(calls):
            pred = {}

            def edge(i, wk):
                pred[i] = max(pred.get(i, 0.0), wk)
            for nm, m in reads + writes:
                if nm in PSUM:
                    for q2, i in B.get(nm, {}).items():
                        edge(i, 0.0 if q2 == q else WAKE)
            for nm, m in reads:
                for i, m2 in W.get(nm, []):
                    if m & m2:
                        edge(i, 0.0 if nm[0] == "~" else WAKE)
            for nm, m in writes:
                for i, m2 in W.get(nm, []) + R.get(nm, []):
                    if m & m2:
                        edge(i, 0.0 if q == calls[i][0] == "t" else WAKE)
            for i, wk in pred.items():
                succ[i].append((j, wk))
            npred[j] = len(pred)
            prev.append(list(pred.items()))
            for nm, m in writes:
                W[nm] = [x for x in W.get(nm, []) if x[1] & ~m] + [(j, m)]
                R[nm] = [x for x in R.get(nm, []) if x[1] & ~m]
            for nm, m in reads:
                R.setdefault(nm, []).append((j, m))
            for nm, m in reads + writes:
                if nm in PSUM:
                    B.setdefault(nm, {})[q] = j
        way = [0.0] * n
        for j in range(n - 1, -1, -1):
            way[j] = calls[j][4] + calls[j][5] + max([wk + way[k] for k, wk in succ[j]] + [0.0])
        for j in range(5):
            way[j] = 1e6 - j

        def lay(order, before, back):
            start, busy = [0.0] * n, {q: ([], []) for q in set(queue)}
            for j in order:
                s, c = lat[j] if back else 0.0, cost[j]
                for i, d in before[j]:
                    if start[i] + d > s:
                        s = start[i] + d
                bs, be = busy[queue[j]]
                m = lo = len(bs)
                while lo and be[lo - 1] > s:
                    lo -= 1
                while lo < m and bs[lo] < s + c - 1e-9:
                    if be[lo] > s:
                        s = be[lo]
                    lo += 1
                if lo and s - be[lo - 1] < 1e-9:
                    be[lo - 1] = s + c
                else:
                    bs.insert(lo, s)
                    be.insert(lo, s + c)
                start[j] = s
            return start
        queue, cost, lat = [[c[i] for c in calls] for i in (0, 4, 5)]
        fore = [[(i, cost[i] + lat[i] + wk) for i, wk in prev[j]] for j in range(n)]
        aft = [[(k, cost[k] + lat[j] + wk) for k, wk in succ[j]] for j in range(n)]
        last_calls = [j for j in range(n) if not succ[j]]

        def forth(key):
            key[:5] = [-1e6] * 5
            start = lay([j for k, j in sorted(zip(key, range(n)))], fore, False)
            return max(start[j] + cost[j] + lat[j] for j in last_calls), start

        def back(start):
            late = lay(sorted(range(n), key=lambda j: (-start[j] - calls[j][4], -j)), aft, True)
            end = max(late[j] + calls[j][4] for j in range(n))
            return [end - late[j] - calls[j][4] for j in range(n)]
        kind = me // 2
        if 0 in ORDER and kind not in ORDER:
            at = {j: i for i, j in enumerate(ORDER[0])}
            if all(at[i] < at[j] for j in range(n) for i, wk in prev[j]):
                ORDER[kind] = ORDER[0]
        if kind not in ORDER:
            best = forth([-x for x in way])
            best = min(best, forth(back(best[1])))
            now, seed, held = best, 1, None
            for turn in range(TURNS):
                start = now[1]
                if held is None:
                    ends = {(calls[j][0], round(start[j] + calls[j][4], 6)): j for j in range(n)}
                    held, j = [], max(range(n), key=lambda j: start[j] + calls[j][4] + calls[j][5])
                    while start[j] > 0:
                        ready, i = max([(start[i] + calls[i][4] + calls[i][5] + wk, i) for i, wk in prev[j]] + [(0.0, -1)])
                        if ready < start[j] - 1e-6:
                            held.append((j, ready))
                            i = ends[(calls[j][0], round(start[j], 6))]
                        j = i
                seed = seed * 48271 % 2147483647
                key = list(start)
                if turn % 50 == 49 or not held:
                    key = back(start)
                else:
                    j0, ready = held[seed // 3 % len(held)]
                    if seed % 3:
                        key[j0] = ready - JOLT * (seed // 7 % 101) / 100
                        todo = [j0]
                        while todo:
                            j = todo.pop()
                            for i, wk in prev[j]:
                                if key[i] > key[j]:
                                    key[i] = key[j]
                                    todo.append(i)
                    else:
                        ahead = [i for i in range(n) if calls[i][0] == calls[j0][0] and ready < start[i] + calls[i][4] and start[i] < start[j0]]
                        todo = [ahead[seed // 7 % len(ahead)]]
                        key[todo[0]] = start[j0] + JOLT * (seed // 11 % 101) / 100
                        while todo:
                            j = todo.pop()
                            for k, wk in succ[j]:
                                if key[k] < key[j]:
                                    key[k] = key[j]
                                    todo.append(k)
                new = forth(key)
                if new[0] <= now[0] + SPAN * (1 - turn / TURNS) * (seed // 13 % 97) / 97:
                    now, held = new, None
                    best = min(best, now)
            ORDER[kind] = sorted(range(n), key=lambda j: (best[1][j], j))
        order = ORDER[kind]
        for j in order:
            calls[j][1](*[[x for x in calls[j][i] if x[0][0] != "~"] for i in (2, 3)])

    def mark(name):
        calls[-1][3].append(("~" + name, 1))

    def behind(name):
        calls[-1][2].append(("~" + name, 1))

    def col(x):
        return [x] if isinstance(x, tuple) else []

    def ap(x):
        return x[0] if isinstance(x, tuple) else x

    CY = 0.00083

    def vcost(o, a, k=1.0):
        if len(a) > 3:
            return 0.055 + a[3] * 1.56 * CY
        if len(o) > 3:
            return 0.055 + o[3] * 3.8 * CY
        return max(64, wide(a) * k) * CY

    def tt(o, a, b, op):
        k = 1.0 if any(x[1][0][0] in PSUM for x in (a, b)) else 2.0
        E("v", lambda: V.tensor_tensor(out=o[0], in0=a[0], in1=b[0], op=op), [a, b], [o], vcost(o, a, k))

    def ts(o, a, s1, op0, s2=None, op1=None):
        kw = dict(scalar2=None) if op1 is None else dict(scalar2=ap(s2), op1=op1)
        k = 0.5 if a[1][0][0] in TWO and o[1][0][0] in TWO else 1.0
        E("v", lambda: V.tensor_scalar(out=o[0], in0=a[0], scalar1=ap(s1), op0=op0, **kw), [a] + col(s1) + col(s2), [o], vcost(o, a, k))

    def cp(o, a):
        k = 0.5 if a[1][0][0] in TWO and o[1][0][0] in TWO else 1.0
        E("v", lambda: V.tensor_copy(out=o[0], in_=a[0]), [a], [o], vcost(o, a, k))

    def scan(o, d0, d1, init, op0, op1):
        E("v", lambda: V.tensor_tensor_scan(out=o[0], data0=d0[0], data1=d1[0], initial=init, op0=op0, op1=op1), [d0, d1], [o],
          vcost(o, d1))

    def total(o, a):
        E("v", lambda: V.tensor_reduce(out=o[0], in_=a[0], axis=AX.X, op=O.add), [a], [o], vcost(o, a))

    def fill(o, c):
        E("v", lambda: V.memset(o[0], c), [], [o], vcost(o, o))

    def act(o, a, f=F.Copy, bias=0.0, scale=1.0):
        E("s", lambda: S.activation(out=o[0], in_=a[0], func=f, bias=ap(bias), scale=ap(scale)), [a] + col(bias) + col(scale), [o],
          vcost(o, a))

    def times(o, a, c):
        act(o, a, F.Copy, 0.0, c)

    def sfill(o, c):
        times(o, w("ONEB", 0, wide(o)), c)

    def half(n, h, p=128):
        return w(n, 128 * h, 128 * h + 128, 1, p)

    def mm(o, l, r, start=True, stop=True):
        k = 4 if l[1][0][0] in BUFS[F32] else 1
        E("t", lambda: PE.matmul(out=o[0], lhsT=l[0], rhs=r[0], start=start, stop=stop), [l, r], [o],
          max(min(64, wide(l)), wide(r)) * k * CY)

    def group(parts):
        for i, (o, l, r) in enumerate(parts):
            mm(o, l, r, i == 0, i == len(parts) - 1)

    def iota(o, pat, base, cm):
        E("g", lambda: g.iota(o[0], pattern=pat, base=base, channel_multiplier=cm, allow_small_or_imprecise_dtypes=True), [], [o],
          0.13 + 2 * CY * wide(o))

    def aff(o, a, pat, op, base, cm, other=0.0):
        E("g", lambda: g.affine_select(out=o[0], in_=a[0], pattern=pat, compare_op=op, fill=other, base=base, channel_multiplier=cm),
          [a], [o], 0.17 + 2 * CY * wide(o))

    def scatter(win, off, data, parts=1, after=None):
        n = 16 // parts
        for i in range(parts):
            cp(ind(w(win), w(off, n * i, n * i + n)), w(data, 16 * n * i, 16 * n * (i + 1)))
            if after:
                behind(after)

    for c in range(4):
        a, b = PIECES[c:c + 2]
        x = w("DET", a, b)
        dma("d", x[0], T.det[:, a:b], "ld%d" % c, [], x[1], 2.0 + b / 400 - 0.1 * c)
    dma("d", T["hamt"][:, :], T.ham[:, :], "ld4", [], w("hamt")[1], 9.0)

    BIG, KB, Y0, MAG = 8192.0, 16384.0, 16640.0, 12582912.0
    YCAP = Y0 + 256 * 20
    fill(w("ONEB"), 1.0)
    fill(w("ONE"), 1.0)
    fill(w("C128"), 1 / 128)
    fill(w("DMB"), 0.0)
    iota(w("PJ"), [[0, 1]], 0, 1)
    aff(w("G8"), w("ONEB", 0, 8), [[-16, 8]], O.is_ge, 0, 1)
    aff(w("G8"), w("G8"), [[16, 8]], O.is_ge, 15, -1)
    aff(w("IDB"), w("ONEB", 0, 128), [[-1, 128]], O.is_equal, 0, 1)
    aff(w("TRS"), w("ONEB", 0, 128), [[1, 128]], O.is_ge, -1, -1)
    for t in range(3):
        iota(w("PK", 8 * t, 8 * t + 8), [[128, 8]], 310 * (t + 1), 1)
    iota(w("PI"), [[-1, 16]], 16, 1)
    iota(w("KD"), [[-1280, 17], [0, 8]], 0, 0)
    aff(w("DMB"), w("DMB"), [[0, 17], [-16, 8]], O.is_ge, 0, 1, 262144.0)
    aff(w("DMB"), w("DMB"), [[0, 17], [16, 8]], O.is_ge, 15, -1, 262144.0)
    iota(w("SW"), [[16, 16]], 1280, 0)
    iota(w("XI"), [[1, 16]], 0, 0)
    iota(w("JC"), [[128, 2]], 1024, 1)
    ts(w("NEG"), w("IDB"), -4096.0, O.mult)
    tt(w("TRX"), w("TRS"), w("NEG"), O.add)
    ts(w("TR2"), w("TRS"), 2.0, O.mult)
    tt(w("TR2"), w("TR2"), w("IDB"), O.add)
    fill(w("TWOS"), 2.0)
    fill(w("KU"), 6128.0)
    times(w("NEG"), w("IDB"), -1.0)
    ts(w("PLI"), w("PK"), 1023, O.bitwise_and)
    ts(w("PA"), w("PLI"), -1280.0, O.add, 0.5, O.mult)
    ts(w("PI"), w("PI"), 15, O.bitwise_and)
    ts(w("MR"), w("PI"), 0.0, O.is_equal)
    ts(w("PJ"), w("PJ"), 15, O.bitwise_and)
    cp(w("RC"), w("PJ"))
    ts(w("SW"), w("SW"), w("RC"), O.add)
    fill(w("RS8"), 0.0)
    fill(w("RS8", 0, 136, 8), 1048576.0)
    fill(w("TC", 1024, 1536), 0.0)
    fill(w("TD", 1024, 1536), float(VOID))
    aff(w("SHP"), w("ONEB", 0, 128), [[1, 128]], O.is_equal, -1, -1)
    aff(w("SHN"), w("ONEB", 0, 128), [[1, 128]], O.is_equal, 1, -1)
    iota(w("WT", 0, 8), [[-208, 8]], 5, 13)
    iota(w("WT", 8, 16), [[224, 8]], 255, -14)
    aff(w("WT"), w("WT"), [[0, 2], [-16, 8]], O.is_ge, 0, 1)
    aff(w("WT"), w("WT"), [[0, 2], [16, 8]], O.is_ge, 15, -1)
    iota(w("KC"), [[0, 8], [-1, 16]], 15, 0)
    fill(w("QW32"), 4096.0)
    aff(w("QW32"), w("QW32"), [[-16, 8], [-2, 16]], O.is_equal, 0, 1)
    aff(w("I32"), w("ONE", 0, 128), [[-16, 8], [-2, 16]], O.is_equal, -1, 1)
    tt(w("QW32"), w("QW32"), w("I32"), O.add)
    aff(w("QW32"), w("QW32"), [[0, 8], [-1, 16]], O.is_ge, 7, 0)
    act(w("QW"), w("QW32"))
    iota(w("QC"), [[0, 16], [1, 4]], 128, 0)
    iota(w("KS"), [[0, 16], [256, 4]], 4096, 0)
    iota(w("EI"), [[16, 4]], 0, 0)
    for h in range(2):
        aff(w("SH%d" % h), w("ONEB", 0, 128), [[-2, 8], [-16, 16]], O.is_equal, 144 - h, 1)
    fill(w("SHP", 0, 128, 16), 0.0)
    fill(w("SHN", 15, 128, 16), 0.0)
    fill(w("BL"), -BIG / 128)
    fill(w("BL", 0, 128, 16), -BIG / 64)
    sfill(w("RS16"), 1.0)
    fill(w("RS16", 0, 256, 16), 0.0)
    fill(w("RS4"), 0.0)
    fill(w("RS4", 0, 64, 4), 1048576.0)
    fill(w("XK", 0, 16), 1.0)
    fill(w("HK", 0, 16), float(MID * sum(W1)))
    fill(w("HK", 16, 32), float(MID * sum(W2)))
    fill(w("ZG"), 0.0)
    cp(w("ZG", 8, 16), w("G8"))
    SEL = [w("ZG", 8, 24), w("ZG", 0, 16)]
    for n, c in (("G16", 16.0 * 37), ("GM8", -8.0), ("WBIG", 1e29)):
        times(w(n), w("G8"), c)
    for n, c in (("IBG", BIG), ("I2B", 256.0), ("IQ", 1 / 256), ("I32", 1.0), ("I256", 256.0)):
        times(w(n), w("IDB"), c)
    ts(w("BN"), w("RC"), 15.0, O.is_equal, BIG, O.mult)
    ts(w("BP"), w("RC"), 0.0, O.is_equal, -BIG, O.mult)
    ts(w("QB0"), w("RC"), 8.0, O.is_lt, 4097.0 * MID, O.mult)
    fill(w("R8"), 0.0)
    cp(w("R8", 8, 128, 16), w("G8"))
    for r in range(16):
        times(w("BLK", r, 128, 16), w("G8"), -256.0)
    cp(w("OC"), w("XI"))
    ts(w("OL4"), w("XI"), 4.0, O.mult, 3.0, O.add)
    ts(w("EI"), w("EI"), w("RC"), O.add)
    ts(w("EI"), w("EI"), 2, O.arith_shift_right)
    cp(w("OQ"), w("EI"))
    ts(w("EJ"), w("EI"), 7, O.bitwise_and)
    ts(w("EK"), w("EI"), 3, O.arith_shift_right)
    ts(w("EJ"), w("EJ"), 2.0, O.mult)
    tt(w("OW4"), w("EJ"), w("EK"), O.add)
    ts(w("EM"), w("PJ"), 7, O.bitwise_and)
    cp(w("RC8"), w("EM"))
    ts(w("OD"), w("ONE", 0, 16), w("RC8"), O.mult)
    iota(w("IO"), [[1, 256]], 0, 0)
    fill(w("R11"), 0.0)
    fill(w("R11", 11, 128, 16), 1 / 128)
    fill(w("ZC", 0, 16), 0.0)
    aff(w("ZC", 16, 144), w("ONEB", 0, 128), [[-16, 8], [128, 16]], O.is_equal, -11, 1)
    iota(w("KQ"), [[256, 4], [0, 4]], 0, 0)
    ts(w("M64", 0, 16), w("MR"), 64.0, O.mult)
    for n in (16, 32, 64, 128):
        act(w("M64", n, 2 * n), w("M64", 0, n))
    for h in range(2):
        ts(w("MT", 128 * h, 128 * h + 128), w("M64", 0, 128), w("JC", h, h + 1), O.mult, 1 / 64, O.mult)
    for t in range(3):
        for q in range(4):
            sfill(w("SA%d" % t, 256 * q, 256 * q + 64), -1.0)
    for z, m0, n in (("ZA", 0, 8), ("ZB", 8, 2)):
        fill(w(z, 0, 16), 0.0)
        iota(w("ZX"), [[0, 8], [1, 16]], m0, 0)
        aff(w("ZX"), w("ZX"), [[-16, 8], [0, 16]], O.is_equal, -10, 1)
        aff(w(z, 16, 144), w("ONEB", 0, 128), [[-16, 8], [0, 16]], O.is_equal, -9, 1)
        tt(w(z, 16, 144), w(z, 16, 144), w("ZX"), O.add)
        aff(w(z, 16, 144), w(z, 16, 144), [[0, 8], [-1, 16]], O.is_ge, n - 1, 0)
    aff(w("SS"), w("ONEB", 0, 128), [[-1, 8], [0, 16]], O.is_equal, 0, 1)
    times(w("SS"), w("SS"), 64.0)
    aff(w("SS1"), w("ONEB", 0, 128), [[-1, 8], [0, 16]], O.is_equal, -8, 1)
    times(w("SS1"), w("SS1"), 64.0)
    fill(w("KZ"), 196608.0)
    fill(w("Z16"), 0.0)
    iota(w("KX"), [[0, 16], [1, 10]], 0, 0)
    aff(w("KX"), w("KX"), [[-16, 8], [0, 20]], O.is_equal, -10, 1)
    aff(w("KW"), w("ONEB", 0, 160), [[-16, 8], [0, 20]], O.is_equal, -9, 1)
    tt(w("KW"), w("KW"), w("KX"), O.add)
    times(w("KW"), w("KW"), 1 / 64)
    iota(w("KA"), [[0, 8], [256, 20]], int(Y0), 0)
    iota(w("KB"), [[0, 8], [-7, 2], [0, 10]], 8, 0)
    times(w("KB"), w("KB"), KB)
    ts(w("RW", 1, 16, 2), w("R8", 8, 128, 16), w("MR", 8, 9), O.mult, -KB, O.mult)
    ts(w("WX"), w("RC"), 8.0, O.is_lt, -KB, O.mult)
    ts(w("RW", 0, 16, 2), w("G8"), w("WX"), O.mult)
    tt(w("RW", 0, 16, 2), w("RW", 0, 16, 2), w("RW", 1, 16, 2), O.subtract)
    sfill(w("RSK"), 0.0)
    for h in range(2):
        ts(w("RSK", 160 * h, 160 * h + 160, 20), w("ONE", 0, 8), w("JC", h, h + 1), O.mult, 1 / 64, O.mult)
    ts(w("RSK", 0, 320, 20), w("RSK", 0, 320, 20), YCAP, O.add)
    fill(w("PWT"), 1 / 3)
    fill(w("Z128"), 0.0)
    scan(w("PW3"), w("PWT"), w("Z128"), 3.0 ** 56, O.mult, O.add)
    tt(w("PWT"), w("PW3"), w("I32"), O.mult)
    total(w("THR"), w("PWT"))
    ts(w("THR"), w("THR"), 2.2, O.mult)
    tt(w("PWT", 0, 16), w("PW3", 48, 64), w("MR"), O.mult)
    total(w("WX"), w("PWT", 0, 16))
    for c in range(8):
        ts(w("WC", 8 * c, 8 * c + 8), w("G8"), w("WX"), O.mult, 3.0 ** (48 - 16 * c), O.mult)

    START = [310 * (t + 1) & 1023 for t in range(3)]

    def rot(t, a, b):
        s, out = START[t], []
        if a < s:
            out.append((a, min(b, s), a - s + 1024))
        if b > s:
            out.append((max(a, s), b, max(a, s) - s))
        return out

    for c, d in zip(PIECES, PIECES[1:]):
        ts(w("CI", c, d), w("DET", c, d), 255, O.bitwise_and)
        for x, y, p in rot(0, c, d):
            ts(w("QB", p, p + y - x), w("CI", x, y), 128.0, O.not_equal)
    for c in range(0, 1024, 256):
        ts(w("TC", c, c + 256), w("CI", c, c + 256), -128.0, O.add)
        ts(w("TD", c, c + 256), w("DET", c, c + 256), -128.0, O.add, 1 / 256, O.mult)

    def whole(c, scale, after=None):
        act(w("TM", c, c + 256), w("TD", c, c + 256), F.Identity, MAG)
        if after:
            behind(after)
        act(w("TN", c, c + 256), w("TM", c, c + 256), F.Identity, -MAG * scale, scale)

    def first_qt(c):
        b = "P7" if c else "P6"
        whole(c, 1.0)
        whole(c + 256, 1.0)
        parts = [(half(b, h), w("QW32"), w("TN", c + 128 * h, c + 128 * h + 128)) for h in range(4)]
        parts += [(w(b, x - c, y - c), w("R8"), w("QB", p, p + y - x)) for x, y, p in rot(0, c, c + 512)]
        group(parts)
        mark("qt%d" % c)
        for x in (0, 256):
            act(w("QT", c + x, c + x + 256), w(b, x, x + 256))
            behind("hv0")

    peers = [q for q in range(4) if q != me]
    near = [q for q in peers if T.cores[q] in topo.cores_of(core)]
    far = [q for q in peers if q not in near]

    def send(sb, dst, rx, rn):
        plan, used, share = [], [], []
        for i, q in enumerate(far):
            e = topo.engines(core, T.cores[q])
            k = len(e) // len(far)
            share.append(k)
            plan.append((q, e[i * k:(i + 1) * k]))
            used += e[i * k:(i + 1) * k]
        for i, q in enumerate(near):
            e = [x for x in topo.engines(core, T.cores[q]) if x not in used]
            k = min([len(e) // len(near)] + share)
            plan.append((q, e[i * k:(i + 1) * k]))
        got = sum(len(e) for q, e in plan)

        def emit(reads, writes):
            deps("g", reads, [])
            tf = []
            for q, e in plan:
                rid, pid = topo.addr(T.cores[q], core)
                tf.append(RemoteDMATransfer(dst_ids=[DstId(rid=rid, pnc=pid)], dma_engine_mask=sum(1 << x for x in e),
                                            remote_sem=T.sem[rn if q in near else rx], src=src(q)[0],
                                            dst=T[dst][:, n * me:n * me + n], alu_op=0))
            g.remote_dma_fused(tf, local_sem=T.sem["snd"])
            for sem in sorted({rx, rn}):
                mine = [(q, e) for q, e in plan if sem == (rn if q in near else rx)]
                semof[sem] = (sem, sum(len(e) for q, e in mine))
                note(sem, 1, [], lands([q for q, e in mine]))
        n = 256 if sb == dst else 64
        src = lambda q: w(sb, 256 * me, 256 * me + 256) if sb == dst else w(sb, 256 * q, 256 * q + 64)
        lands = lambda qs: [r for q in qs for r in w(dst, n * q, n * q + n)[1]]
        calls.append(("g", emit, [r for q in peers for r in src(q)[1]], lands(near) + [(rx, 1)], 0.5, NEAR + (n > 64) * 2.0))
        if sb == dst:
            behind("sent")
        mark("sent")
        calls.append(("x", lambda reads, writes: None, [(rx, 1)], lands(far), 0.0, FAR - NEAR))
        if sb != dst:
            act(w(dst, 64 * me, 64 * me + 64), w(sb, 256 * me, 256 * me + 64))
        return got

    def wrap(p):
        group([(w(p, 0, 16), w("XF", 128 * h, 128 * h + 128), SEL[h]) for h in range(2)])

    def ranks(end):
        for k in range(8):
            mm(w("P2", 8 * k, 8 * k + 8), w("QB", 128 * k, 128 * k + 128), w("G8"))
        ts(w("LV"), w("P2", 0, 64), 0.0, O.is_gt)
        mm(w("P5", 0, 64), w("C128"), w("KU"), True, False)
        mm(w("P5", 0, 64), w("TR2"), w("LV"), False, False)
        for d in range(1, 8):
            mm(w("P5", 8 * d, 64), w("TWOS"), w("LV", 0, 64 - 8 * d), False, end and d == 7)

    A = lambda n: w(n, 0, 256)
    sent = 0
    for t in range(3):
        IA, IB = "IA%d" % t, "IB%d" % t
        if t == 0:
            ranks(True)
        ts(w("R32"), w("P5", 0, 64), 0.5, O.add)
        tt(w("LW2", 0, 128, 2), w("R32"), w("P5", 0, 64), O.subtract)
        tt(w("LW2", 1, 128, 2), w("P5", 0, 64), w("R32"), O.subtract)
        for h in range(17):
            act(bs(h=h), w("R32"), F.Sign, 0.5 - 6144 - 32 * h)
        for i in range(8):
            x = (T["OL"][:, :, 7 - i:9 + i:2 * i + 1], [("OL", sum((1 << 7 - i | 1 << 8 + i) << 16 * j for j in range(64)))], [])
            ts(x, w("LW2"), 2.0 * i + 1, O.is_equal)
        for k in range(8):
            c = (128 * k, 128 * k + 128)
            ts(w("OA", *c), (T["OL"][:, 8 * k:8 * k + 8, :], [("OL", ((1 << 128) - 1) << (128 * k))], []), w("PA", 8 * t + k, 8 * t + k + 1), O.mult)
        group([(w("P2", 0, 136), w("C128"), w("KD")), (w("P2", 0, 136), w("IDB"), w("DMB"))]
              + [(w("P2", 0, 136), w("OA", 128 * k, 128 * k + 128), bs(k=k)) for k in range(8)])
        if t:
            scatter("TD", "FO", "IB%d" % (t - 1), PT)
        scan(w("LM"), w("RS8"), w("P2", 0, 136), 0.0, O.add, O.min)
        if t and TB:
            behind("tc%d" % (t - 1))
        tt(w("GU"), w("LM", 7, 128, 8), w("LM", 15, 136, 8), O.subtract)
        for a, b in DUP:
            cp(w("DU", 16 * a, 16 * b), ind(w("TD"), w("GU", a, b)))
        mark("du%d" % t)
        act(w("AB"), ind(w("TC"), w("GU")), F.Abs)
        mark("ab%d" % t)
        mm(A("P3"), w("IDB"), w("AB"))
        CUT = [0, HV0, 128, 192, 256]

        def look(a, b):
            return w("hv", 16 * a, 16 * b), ind(w("hamt"), w("DU", a, b))
        for j in range(1, 4):
            act(*look(CUT[j], CUT[j + 1]))
            if TB or j > 1:
                behind("ab%d" % t)
        mark("hv%d" % t)
        cp(*look(CUT[0], CUT[1]))
        behind("du%d" % t)
        act(w("CN"), ind(w("TC"), w("GU")))
        ts(w("DF"), w("DU"), -float(MID), O.add)
        for h in range(2):
            mm(w("P0", h, 32, 2), half("DF", h), w("WT"))
        mm(w("P4", 0, 256), w("SHP"), w("DF"))
        mm(w("P4", 256, 512), w("SHN"), w("DF"))
        act(w("DP"), w("P4", 0, 256), F.Identity, w("BP"))
        act(w("DN"), w("P4", 256, 512), F.Identity, w("BN"))
        tt(w("H1"), w("P0", 0, 32), w("HK"), O.add)
        ts(w("H2"), w("H1"), 4095, O.bitwise_and)
        tt(w("HP"), w("H2", 0, 16), w("H2", 16, 32), O.mult)
        ts(w("HP"), w("HP"), 5, O.arith_shift_right, 4095, O.bitwise_and)
        for h in range(2):
            ts(w("HV", 8 * h, 8 * h + 8), w("HP", h, 16, 2), 16.0, O.mult, 16.0 * t, O.add)
        if t == 0:
            for c in (0, 512):
                first_qt(c)
        if t == 2:
            for c in range(0, 1024, 256):
                whole(c, 256.0, "hv2")
        mm(A("P7"), w("NEG"), w("DF"), True, False)

        def mins(a, b, h=None):
            for k in range(16):
                x = w("hv", 16 * a + k, 16 * b, 16)
                if a == CUT[3]:
                    x = (x[0], x[1], w("HV")[1])
                tt(w("MK", 256 * k + a, 256 * k + b), x, w("P3", a, b), O.min)
            if h is not None:
                p = "P%d" % (1 + h)
                group([(w(p, 0, 128), w("C128"), w("KC"))]
                      + [(w(p, k, 128, 16), w("MK", 256 * k + 128 * h, 256 * k + 128 * h + 128), w("G16")) for k in range(16)])
                calls[-16][2].append(("~qt%d" % (512 * h), 1))
                scan(half("SCN", h), w("RS16", 0, 128), w(p, 0, 128), 0.0, O.mult, O.max)
        mins(0, CUT[2], 0)
        mins(CUT[2], CUT[3])
        mins(CUT[3], CUT[4], 1)
        act(w("ABF"), w("AB"), F.Relu, -1.0)
        act(w("FB"), w("CN"), F.Identity, 191.625, 0.25)
        act(w("SGC"), w("CN"), F.Sign)
        group([(A("P1"), w("QW"), w("DF")), (A("P1"), w("R8"), w("ABF"))])
        act(w("QS"), A("P1"), F.Identity, w("QB0"))
        group([(A("P2"), w("IDB"), w("CN")), (A("P2"), w("NEG"), w("SGC"))])
        act(w("CFD"), A("P2"))
        for hs in ([(0,), (1,)] if TS else [(0, 1)]):
            c, z = (8 * hs[0], 8 * hs[-1] + 8), (128 * hs[0], 128 * hs[-1] + 128)
            top, oc = w("SCN", z[0] + 15, z[1], 16), w("OC", 0, c[1] - c[0])
            mm(w("P5", *z), w("IDB"), w("DF", *z), True, False)
            mm(w("P6", *z), w("IDB"), w("DF", *z), True, False)
            mm(w("P6", *z), w("BL"), w("ONEB", *z), False, False)
            tt(w("E3", *c), top, w("HV", *c), O.add)
            cp(w("MX", *c), top)
            tt(w("XK", 16 + z[0], 16 + z[1]), ind(w("MX", *c), oc), w("SCN", *z), O.is_equal)
            ts(w("VV", *c), w("E3", *c), 4, O.arith_shift_right, 4095, O.bitwise_and)
            ts(w("VB", *z), ind(w("VV", *c), oc), -float(MID), O.add)
            mark("vb%d" % t)
            for h in hs:
                mm(half("P5", h), w("XK", 16 + 128 * h, 144 + 128 * h), w("IBG"), False, h == hs[-1])
            for h in hs:
                mm(half("P6", h), w("XK", 15 + 128 * h, 143 + 128 * h), w("IBG"), False, h == hs[-1])
            for h in hs:
                mm(half("P4", h), half("VB", h), w("IDB"))
            for h in hs:
                mm(half("P7", h), half("VB", h), w("IDB"), False, h == 1)
            tt(w("HI", *z), w("P5", *z), w("DN", *z), O.min)
            tt(w("P6", *z), w("P6", *z), w("DP", *z), O.max)
            tt(w("CT", *z), w("P4", *z), w("HI", *z), O.min)
            tt(w("CH", *z), w("CT", *z), w("P6", *z), O.max)
            for h in hs:
                mm(w("P0", h, 32, 2), half("CH", h), w("WT"))
        act(w("AE"), A("P7"), F.Abs)
        act(w("SG"), w("AE"), F.Sign)
        for h in range(2):
            mm(w("P3", 8 * h, 8 * h + 8), half("SG", h), w("GM8"))
        ts(w("VX"), w("VV"), 3584.0, O.is_ge, 8.0, O.mult)
        tt(w("VD"), w("P3", 0, 16), w("VX"), O.add)
        tt(w("QQ"), ind(w("VD"), w("OQ")), w("QC"), O.add)
        tt(w("I1"), w("P0", 0, 32), w("HK"), O.add)
        ts(w("I2"), w("I1"), 4095, O.bitwise_and)
        tt(w("PR"), w("I2", 0, 16), w("I2", 16, 32), O.mult)
        ts(w("OW"), w("PR"), 5, O.arith_shift_right, 3, O.bitwise_and)
        tt(w("OM"), ind(w("OW"), w("OW4")), w("QQ"), O.is_equal)
        group([(w("P3", 64, 128), w("C128"), w("KS")), (w("P3", 64, 128), w("TRX"), w("OM")),
               (w("P3", 96, 128), w("ONEB", 0, 128), w("OM", 0, 32))])
        scan(w("SC2"), w("RS4"), w("P3", 64, 128), 0.0, O.add, O.min)
        tt(w("XF"), ind(w("SC2"), w("OL4")), w("MT"), O.min)
        wrap("P4")
        cp(w("OFF"), w("P4", 0, 16))
        ts(w("LE"), w("GU"), -1279.0, O.add, 4096.0, O.mult)
        behind("vb%d" % t)
        cp(w("LD"), w("GU"))
        behind("vb%d" % t)
        tt(w("LE"), w("LE"), w("SW"), O.min)
        tt(w("GS"), w("LD"), w("LE"), O.max)
        if TE:
            scatter("TC", "GS", "CFD", 4)
            mark("tf%d" % t)
        mm(A("P5"), w("R11"), w("IO"), True, False)
        mm(A("P5"), w("QW"), w("CH"), False, False)
        ts(w("HS", 0, 16), w("PR"), 7, O.arith_shift_right, 1023, O.bitwise_and)
        ts(w("HS", 16, 32), w("I2", 0, 16), 511, O.bitwise_and)
        cp(w("T16", 0, 16), w("HS", 0, 16))
        ts(w("T16", 16, 32), w("HS", 16, 32), 2.0, O.mult, 1.0, O.add)
        mm(w("P7", 0, 128, 1, 32), w("T16"), w("IDB"))
        cp(w("R4", 0, 128, 1, 32), w("P7", 0, 128, 1, 32))
        for h in range(2):
            mm(half("P5", h), w("SH%d" % h, 0, 128, 1, 32), w("R4", 0, 128, 1, 32), False, h == 1)
        act(w("REC"), A("P5"), F.Identity, w("QB0"))
        scatter("SA%d" % t, "OFF", "REC", 1, "tf%d" % t if TE > 1 and t != 1 else None)
        sent += send("SA%d" % t, IA, "ra%d" % t, "rn%d" % t)
        group([(A("P1"), w("IDB"), w("CH")), (A("P1"), w("NEG"), w("DF"))])
        act(w("SGN"), A("P1"), F.Sign)
        mm(A("P2"), w("BLK"), w("SGN"))
        act(w("RN"), A("P2"), F.Identity, 384.5, -1 / 256)
        group([(A("P1"), w("BLK"), w("SGN")), (A("P1"), w("IDB"), w("FB")), (A("P1"), w("I2B"), w("RN"))])
        act(w("SD%d" % t, 256 * me, 256 * me + 256), A("P1"), F.Abs, -98304.0 - 128 - 192)
        sent += send("SD%d" % t, "SD%d" % t, "rc%d" % t, "rc%d" % t)
        mm(A("P6"), w("IDB"), w("CH"))
        act(w("SB%d" % t, 256 * me, 256 * me + 256), A("P6"), F.Identity, float(MID))
        sent += send("SB%d" % t, "SB%d" % t, "rb%d" % t, "rb%d" % t)
        if t:
            scatter("QT", "FO", "QN", PQ, "vb%d" % t)
        scatter("QT", "GS", "QS", PF)
        if not TE:
            scatter("TC", "GS", "CFD", PG)
        if t == 2:
            for c in range(0, 1024, 256):
                if c < YV:
                    p = w("P2", 256, 512)
                    act(p, w("TN", c, c + 256), F.Identity, 128.0)
                    tt(w("YT", c, c + 256), w("TC", c, c + 256), p, O.add)
                    continue
                group([(A("P2"), w("IDB"), w("TC", c, c + 256))]
                      + [(half("P2", h), w("I32"), w("TN", c + 128 * h, c + 128 * h + 128)) for h in range(2)])
                act(w("YT", c, c + 256), A("P2"), F.Identity, 128.0)
        def probe(x, y):
            return w("PR5", 16 * x, 16 * y), ind(w("QT", 0, 1024), w("ZU", x, y))
        hn, hf = me // 2, min(far) // 2
        KEY, BRO = {hn: "P5", hf: "P7"}, {hn: "P0", hf: "P1"}
        sets = [(64 * me, 64), (64 * near[0], 64), (128 * hf, 128)]

        def lists(p, z, o, a, n, u):
            x, k = w(p, 0, n // u), (o + a // u, o + (a + n) // u)
            group([(x, w("C128"), w("KZ", 0, n // u))]
                  + [(x, w(z, 16 - 16 // u * i, 144 - 16 // u * i), w("IH", a + i, a + n, u)) for i in range(u)])
            if n == 128:
                mark("far%d" % t)
            if n == 256:
                for c in calls[-u:]:
                    c[2].append(("~far%d" % t, 1))
            ts(w("RZ", *k), x, -511.5, O.add)
            tt(w("ZU", *k), x, w("RZ", *k), O.subtract)
        for (a, n), p in zip(sets, ("P4", "P3", "P4")):
            ts(w("IH", a, a + n), w(IA, a, a + n), 2000.0, O.min)
            lists(p, "ZA", 0, a, n, 2)
            if a == 64 * me:
                lists("P3", "ZB", 128, a, n, 8)
                act(*probe(a // 2, (a + n) // 2))
                act(*probe(128 + a // 8, 128 + (a + n) // 8))
        lists("P6", "ZB", 128, 0, 256, 8)
        for h in (hn, hf):
            p = w(KEY[h], 0, 160)
            mm(p, w("C128"), w("KA"), True, False)
            mm(p, w("C128"), w("KB"), False, False)
            mm(p, half("IH", h), w("KW"), False, False)

        group([(w("P2", 0, 16), w("C128"), w("KQ"))]
              + [(w("P2", 0, 16), w("ZC", 16 - u, 144 - u), w("IH", u, 256, 16)) for u in range(16)])
        for c in calls[-16:]:
            c[2].append(("~far%d" % t, 1))
        cp(w("OI"), w("P2", 0, 16))
        mark("oi%d" % t)

        def same(m, a, n):
            b, st = (m, 8) if m < 8 else (2048 + m - 8, 2)
            tt(w("CMP", 256 * m + a, 256 * m + a + n), w("PR5", b + st * a, b + st * (a + n - 1) + 1, st),
               w(BRO[a // 128], a % 128, a % 128 + n), O.is_equal)

        def key(h, m, end):
            mm(w(KEY[h], m, 160, 10), w("CMP", 256 * m + 128 * h, 256 * m + 128 * h + 128), w("RW"), False, end)

        for a, n in sets:
            act(w(BRO[a // 128], a % 128, a % 128 + n), w(IA, a, a + n))
            if a == 64 * me:
                for m in range(10):
                    same(m, a, n)
        (b, _), (a, n) = sets[1:]
        for x, y in ((b, 32), (a, 32), (a + 64, 32 - FV)):
            act(*probe(x // 2, x // 2 + y))
        if FV:
            cp(*probe(a // 2 + 64 - FV, a // 2 + 64))
        for x, y in sets[1:]:
            cp(*probe(128 + x // 8, 128 + (x + y) // 8))
        for m in range(10):
            same(m, b, 64)
            key(hn, m, m == 9)
        for m in (8, 9):
            same(m, a, 128)
            key(hf, m, False)
        for m in range(8):
            same(m, a, 64)
        for m in range(8):
            same(m, a + 64, 64)
            behind("oi%d" % t)
            key(hf, m, m == 7)
        if True:
            ky = w("KY", 19, 320, 20)
            for h in (hn, hf):
                scan(w("KY", 160 * h, 160 * h + 160), w("RSK", 160 * h, 160 * h + 160), w(KEY[h], 0, 160), 0.0, O.max, O.min)
            ts(w("RK"), ky, -7.9921875, O.add, YCAP, O.min)
            tt(w("PL16"), ky, w("RK"), O.subtract)
            tt(w("PL"), ky, w("RK"), O.subtract)
            mm(w("P7", 0, 128, 1, 16), w("PL16"), w("IDB"))
            if t < 2:
                ts(w("PN"), w("PL"), 64.0, O.mult, 1024.0 - START[t + 1], O.add)
                ts(w("PM"), w("PN"), 127, O.bitwise_and)
                ts(w("KJ"), w("PN"), 7, O.arith_shift_right, 7, O.bitwise_and)
                ts(w("NB"), w("PM"), -1.0, O.mult)
                mark("nb%d" % t)
            for h in range(2):
                tt(half("XF", h), ind(w("PL", 8 * h, 8 * h + 8), w("OC", 0, 8)), half("M64", 0), O.mult)
                if h and NX:
                    behind("nb%d" % t)
            cp(half("R6", 0, 16), w("P7", 0, 128, 1, 16))
            for h in range(2):
                c = (8 * h, 8 * h + 8)
                mm(w("P4", *c), half("XF", h), w("G8"))
                cp(w("PO", *c), w("P4", *c))
                act(half("CO", h), ind(w("TC"), w("PO", *c)))
            for h in range(2):
                mm(half("P0", h), w("SS1" if h else "SS", 0, 128, 1, 16), half("R6", 0, 16))
            cp(w("PW"), w("P4", 0, 16))
            cp(w("PU"), A("P0"))
            if t < 2:
                for j in range(16):
                    act(w("TH", 128 * j, 128 * j + 128), w("IO", 0, 128), F.Sign, w("NB", j, j + 1))
            WHO = ("P3", "P1")
            for h in range(2):
                mm(w(WHO[h], 0, 8), w("IDB"), w("Z16", 0, 8), True, False)
                for c in range(8 * h + 7, -1, -1):
                    a = (0, 0, 64, 96)[c % 8 // 2] if c // 8 == h else 0
                    x = w("MK", 256 * c + 128 * h + a, 256 * c + 128 * h + 128)
                    ts(x, w("PU", 128 * h + a, 128 * h + 128), w("PW", c, c + 1), O.is_equal)
                    if h:
                        behind("who%d" % t)
                    elif c == 0:
                        mark("who%d" % t)
                    mm(w(WHO[h], 0, 8, 1, 128, a), x, w("WC", 8 * (c % 8), 8 * (c % 8) + 8) if c // 8 == h else w("WBIG"), False, c == 0)
                    if h:
                        behind("whp%d" % t)
                    elif c == 0:
                        mark("whp%d" % t)
        act(w("CQ"), ind(w("SD%d" % t), w("OI")), F.Identity, -128.0)
        act(w(IB), ind(w("SB%d" % t), w("OI")))
        for h, p in enumerate((half("P6", 0), half("P0", 2))):
            group([(p, w("IDB"), half("CQ", h)), (p, w("IDB"), half("CO", h))])
            if t < 2:
                act(half("ABN", h), p, F.Abs)
            ts(half("CNW", h), p, 127.0, O.min, -127.0, O.max)
        if t < 2:
            for a in range(0, 1024, 256):
                for x, y, p in rot(t + 1, a, a + 256):
                    act(w("QB", p, p + y - x), w("TC", x, y), F.Abs)
            ranks(False)
            ky = w("KY", 19, 320, 20)
            ts(w("VAL"), ky, YCAP, O.is_lt)
            ts(w("OLD"), ky, Y0 + 2560, O.is_lt)
            cp(w("KF"), w("KJ"))
            for k in range(8):
                act(sk(k), w("KF"), F.Sign, float(k), -1.0)
            act(w("SQ"), sk(), F.Abs)
            for h in range(2):
                act(w("AK", 128 * h + 64, 128 * h + 128), sk(h=h), F.Identity, 1.0)
                act(w("AK", 128 * h, 128 * h + 64), w("SQ", 64 * h, 64 * h + 64), F.Identity, 1.0, -1.0)
                c = (8 * h, 8 * h + 8)
                mm(w("P4", 16 + 8 * h, 24 + 8 * h), half("ABN", h), w("G8"))
                tt(w("NL", *c), w("P4", 16 + 8 * h, 24 + 8 * h), w("VAL", *c), O.min)
                tt(w("D0", *c), w("NL", *c), w("OLD", *c), O.subtract)
        for h in range(2):
            c, p = (8 * h, 8 * h + 8), w(WHO[h], 0, 8)
            if t < 2:
                ts(w("WIN", *c), p, w("THR"), O.is_lt)
                tt(w("DW", *c), w("WIN", *c), w("D0", *c), O.mult)
                tt(half("DK", h), ind(w("DW", *c), w("OD", 0, 8)), half("AK", h), O.mult)
                mark("dk%d" % t)
            ts(w("LO", *c), p, w("THR"), O.is_ge)
            tt(half("XF", h), ind(w("LO", *c), w("OC", 0, 8)), half("MT", h), O.mult)
            if XD and h:
                behind("dk%d" % t)
            mm(w("P7", *c), half("XF", h), w("G8"))
        mark("wrap%d" % t)
        tt(w("FO"), w("P7", 0, 16), w("PW"), O.max)
        if t < 2:
            for j in range(16):
                h, gg = j // 8, j % 8
                if not gg:
                    mm(w("P5", 0, 64), w("ONEB", 0, 128), w("DK", 128 * h + 64, 128 * h + 128), False, False)
                mm(w("P5", gg, 64, 8), w("TH", 128 * j, 128 * j + 128), w("DK", 128 * h + gg, 128 * h + 64, 8), False, j == 15)
                if j == WR:
                    behind("wrap%d" % t)
            group([(half("P2", h), w("I32"), half(IA, h)) for h in range(2)] + [(A("P2"), w("R8"), w("ABN"))])
            act(w("QN"), A("P2"))
        else:
            act(A("P2"), w(IB), F.Identity, 128.0, 256.0)
            tt(w("YN"), w("CNW"), A("P2"), O.add)
        if t < 2:
            scatter("TC", "FO", "CNW", PT)
            mark("tc%d" % t)
        else:
            scatter("YT", "FO", "YN")
            dma("d", T.y[:, :], T["YT"][:, 0:1024], "st0", w("YT", 0, 1024)[1], [], 4.0)
    schedule()
    wait("d", "st0", 1)
    g.wait_ge(T.sem.snd, sent)
    for q in ("v", "s", "t", "g"):
        wait("g", q, cnt[q])
